import numpy as np
import ml_dtypes


def mxq(x, axis, fmt="e4m3"):
    dtype, down = {"e4m3": (ml_dtypes.float8_e4m3fn, 7), "e5m2": (ml_dtypes.float8_e5m2, 14)}[fmt]
    v = np.moveaxis(np.asarray(x, np.float32).astype(ml_dtypes.bfloat16).astype(np.float64), axis, -1)
    blocks = v.reshape(v.shape[:-1] + (-1, 32))
    amax = np.abs(blocks).max(-1, keepdims=True)
    byte = np.maximum(np.where(amax > 0, np.frexp(amax)[1] - 1 + 127, 0) - down, 1)
    scale = np.exp2(byte - 127.0)
    codes = (blocks / scale).astype(np.float32).astype(dtype).astype(np.float64)
    return np.moveaxis((codes * scale).reshape(v.shape), -1, axis)


WIDE = False


def mx_kscale(k):
    if not WIDE:
        return np.ones(k)
    levels = np.array([10, -10, 5, -5, 0])
    if k % 512:
        return np.exp2(np.random.permutation(np.resize(levels, k // 32))).repeat(32)
    a = np.empty((k // 512, 16))
    for p in range(k // 512):
        a[p, :8] = np.random.permutation(np.resize(levels, 8))
        for g in range(8):
            far = levels[np.abs(levels - a[p, g]) >= 10]
            a[p, g + 8] = far[np.random.randint(len(far))]
    return np.exp2(a.ravel()).repeat(32)


BF16 = ml_dtypes.bfloat16


def bf(x):
    return np.asarray(x, np.float32).astype(BF16)


def f64(x):
    return np.asarray(x).astype(np.float64)


T, D, F, E = 1536, 1024, 512, 1024


def draw0():
    sq, sk, sv = mx_kscale(D), mx_kscale(D), mx_kscale(D)
    u = mx_kscale(F)
    r = mx_kscale(T)
    return {
        "xq": bf(np.random.standard_normal((T, D)) * sq),
        "xk": bf(np.random.standard_normal((T, D)) * sk * r[:, None]),
        "xv": bf(np.random.standard_normal((T, D)) * sv / r[:, None]),
        "wq": bf(np.random.standard_normal((D, F)) / np.sqrt(D) / F ** 0.25 / sq[:, None] * u),
        "wk": bf(np.random.standard_normal((D, F)) / np.sqrt(D) / T ** 0.25 / sk[:, None]),
        "wv": bf(np.random.standard_normal((D, E)) / np.sqrt(D) / T ** 0.25 / sv[:, None]),
        "state": bf(np.random.standard_normal((F, E)) / u[:, None]),
        "decay": bf(np.random.uniform(0.4, 0.9, F) * u),
    }


def core(xq, xk, xv, wq, wk, wv, state, decay):
    st = f64(state)
    q = mxq(f64(xq), 1, "e4m3") @ mxq(f64(wq), 0, "e4m3")
    k = mxq(f64(xk), 1, "e4m3") @ mxq(f64(wk), 0, "e4m3")
    v = mxq(f64(xv), 1, "e4m3") @ mxq(f64(wv), 0, "e4m3")
    k = np.maximum(k, 0.0)
    o = mxq(q, 1, "e4m3") @ mxq(st, 0, "e4m3")
    upd = mxq(k, 0, "e4m3").T @ mxq(v, 0, "e4m3")
    new_state = f64(decay)[:, None] * st + upd
    return o, new_state


def e4m3fn_bytes(y):
    return np.clip(np.asarray(y, np.float64), -448.0, 448.0).astype(np.float32).astype(ml_dtypes.float8_e4m3fn).view(np.uint8)


def e4m3fn_values(b):
    return np.asarray(b, np.uint8).view(ml_dtypes.float8_e4m3fn).astype(np.float64)


def setup_inputs():
    d = draw0()
    x0 = np.asarray(d['xq']).astype(np.float64)
    s = (np.max(np.abs(x0), axis=(0,), keepdims=True) / 448.0).astype(np.float32)
    out = {}
    for k, v in d.items():
        if k == 'xq':
            out['xq_bytes'] = e4m3fn_bytes(x0 / s.astype(np.float64))
            out['xq_scale'] = s
        else:
            out[k] = v
    return out


def reference(xq_bytes, xq_scale, xk, xv, wq, wk, wv, state, decay):
    return core(e4m3fn_values(xq_bytes) * xq_scale.astype(np.float64), xk, xv, wq, wk, wv, state, decay)

@@ -1,0 +1,430 @@
+from contextlib import ExitStack
+
+import concourse.mybir as mybir
+from concourse.masks import make_identity
+
+T, D, F, E = 1536, 1024, 512, 1024
+FLOPS = 2 * T * (2 * D * F + D * E + 2 * F * E)
+
+F32 = mybir.dt.float32
+BF16 = mybir.dt.bfloat16
+U32 = mybir.dt.uint32
+U8 = mybir.dt.uint8
+FP8 = mybir.dt.float8_e4m3fn
+FP8X4 = mybir.dt.float8_e4m3fn_x4
+ACT = mybir.ActivationFunctionType
+ALU = mybir.AluOpType
+
+P = 128
+PACK = 4
+CHUNK = 512
+CHUNKS = T // CHUNK
+PASSES = D // 512
+HALF = 512
+
+
+def tile_linear_state_step_s7_kernel(
+    tc, xq_bytes, xq_scale, xk, xv, wq, wk, wv, state, decay, out_0, out_1
+):
+    nc = tc.nc
+
+    with ExitStack() as ctx:
+        sb = ctx.enter_context(tc.tile_pool(name="sb", bufs=1))
+        ps = ctx.enter_context(tc.psum_pool(name="ps", bufs=8))
+
+        ident = sb.tile([P, P], F32, name="ident", align_bytes=64)
+        make_identity(nc, ident[:])
+
+        decay_sb = sb.tile([P, PACK], BF16, name="decay_sb")
+        warm = sb.tile([P, 1], F32, name="warm")
+        nc.vector.memset(warm[:], 0.0)
+        nc.scalar.activation(out=warm[:], in_=warm[:], func=ACT.Relu)
+
+        xdram = {"k": xk, "v": xv, "q": xq_bytes}
+        rows = {}
+        rows_q = {}
+        xcodes = {}
+
+        def load_x(kind, c, cuts=(0, 4)):
+            view = xdram[kind][c * CHUNK : (c + 1) * CHUNK, :].rearrange("(m s) d -> m s d", s=PACK)
+            if kind == "q":
+                t = sb.tile([P, PACK, D], U8, name=f"xqb{c}", tag="xq_bytes", bufs=2, align_bytes=64)
+                rows_q[c] = t
+            else:
+                if cuts[0] == 0:
+                    rows[kind, c] = sb.tile([P, PACK, D], BF16, name=f"x{kind}{c}", tag="x_rows", bufs=4, align_bytes=64)
+                t = rows[kind, c]
+            for a, b in zip(cuts[:-1], cuts[1:]):
+                nc.sync.dma_start(out=t[:, a:b, :], in_=view[:, a:b, :])
+
+        scale_pt = sb.tile([P, PASSES, PACK], F32, name="scale_pt", align_bytes=64)
+        ones = sb.tile([P, 1], F32, name="ones")
+        nc.vector.memset(ones[:], 1.0)
+
+        def load_scales():
+            nc.sync.dma_start(out=scale_pt[:], in_=xq_scale.rearrange("o (g p t) -> p (o g) t", p=P, t=PACK))
+
+        wraw = {}
+
+        def load_w(name, w, passes=None):
+            width = w.shape[1]
+            for g in passes or range(w.shape[0] // 512):
+                if name in ("wk", "wq"):
+                    t = sb.tile([P, PACK, width], BF16, name=f"{name}raw{g}", tag="w_small", bufs=2, align_bytes=64)
+                else:
+                    t = sb.tile([P, PACK, width], BF16, name=f"{name}raw{g}", align_bytes=64)
+                nc.sync.dma_start(out=t[:], in_=w[512 * g : 512 * (g + 1), :].rearrange("(p j) n -> p j n", j=PACK))
+                wraw[name, g] = t
+
+        load_x("k", 0, (0, 2))
+        load_w("wk", wk, (0,))
+        load_x("k", 0, (2, 4))
+        load_w("wk", wk, (1,))
+        load_x("k", 1, (0, 2))
+        load_x("k", 1, (2, 4))
+
+        wcodes = {}
+
+        def weight_piece(name, g, on_scalar=False):
+            raw = wraw[name, g]
+            width = raw.shape[2]
+            grouped = sb.tile([P, width * PACK], BF16, name=f"{name}g{g}", tag="w_grouped", bufs=2, align_bytes=64)
+            codes = sb.tile([P, width], U32, name=f"{name}c{g}", align_bytes=64)
+            scales = sb.tile([P, width], U8, name=f"{name}s{g}", align_bytes=64)
+            wcodes[name, g] = (codes, scales)
+
+            def interleave():
+                if name == "wq":
+                    nc.vector.tensor_copy(
+                        out=grouped[:].rearrange("p (t m j) -> p t m j", t=PACK, j=PACK),
+                        in_=raw[:].rearrange("p j (m t) -> p t m j", t=PACK),
+                    )
+                else:
+                    copy_out(
+                        grouped[:].rearrange("p (c i j) -> p c j i", i=4, j=PACK),
+                        raw[:].rearrange("p j (c i) -> p c j i", i=4),
+                        on_vector=not on_scalar,
+                    )
+
+            def quant():
+                nc.vector.quantize_mx(out=codes[:].bitcast(FP8X4), scales=scales[:], in_=grouped[:])
+
+            return interleave, quant
+
+        def weights(name, scalar_passes=()):
+            passes = range(F // 512 if name == "st" else PASSES)
+            made = [weight_piece(name, g, g in scalar_passes) for g in passes]
+            return [x for x, _ in made] + [x for _, x in made]
+
+        def copy_out(out, in_, on_vector):
+            if on_vector:
+                nc.vector.tensor_copy(out=out, in_=in_)
+            else:
+                nc.scalar.copy(out=out, in_=in_)
+
+        def widen_q(c):
+            def pair(h):
+                if h == 0:
+                    rows["q", c] = sb.tile([P, 2, PACK * D // 2], BF16, name=f"xq{c}", tag="xq_rows", bufs=2, align_bytes=64)
+                half = PACK * D // 4
+                nc.vector.tensor_scalar(
+                    out=rows["q", c][:, :, h * half : (h + 1) * half].rearrange("p u (m e) -> p m u e", e=2),
+                    in0=rows_q[c][:, 2 * h : 2 * h + 2, :].bitcast(FP8).rearrange("p s (m u e) -> p (s m) u e", u=2, e=2),
+                    scalar1=ones[:, 0:1], scalar2=None, op0=ALU.mult,
+                )
+
+            return [lambda: pair(0), lambda: pair(1)]
+
+        def transpose_pair(kind, c, h):
+            t = rows[kind, c]
+            width = PASSES * P * PACK
+            grouped = sb.tile([P, 2 * width], BF16, name=f"g{kind}{c}{h}", tag="x_grouped", bufs=3, align_bytes=64)
+            for i in range(2):
+                s = 2 * h + i
+                bank = ps.tile([P, 512], F32, name=f"t{kind}{c}{s}", tag="bank")
+                if kind == "q":
+                    bank4 = bank[:].rearrange("p (u g m) -> p g u m", g=PASSES, u=2)
+                else:
+                    bank4 = bank[:].rearrange("p (g u m) -> p g u m", g=PASSES, u=2)
+                for g in range(PASSES):
+                    for u in range(2):
+                        if kind == "q":
+                            first = s * PASSES * P + g * P
+                            chosen = t[:, u, :].bitcast(F32)[:, first : first + P]
+                        else:
+                            chosen = t[:, s, :].bitcast(F32)[:, 256 * g + u : 256 * (g + 1) : 2]
+                        nc.tensor.transpose(bank4[:, g, u, :], chosen, ident[:])
+                if kind == "q":
+                    nc.vector.tensor_tensor(
+                        out=grouped[:, i * width : (i + 1) * width].rearrange("p (g m u e) -> p g m u e", g=PASSES, u=2, e=2),
+                        in0=bank[:].bitcast(BF16).rearrange("p (u g m e) -> p g m u e", g=PASSES, u=2, e=2),
+                        in1=scale_pt[:].rearrange("p g (u e) -> p g u e", u=2).unsqueeze(2).to_broadcast([P, PASSES, P, 2, 2]),
+                        op=ALU.mult,
+                    )
+                else:
+                    nc.scalar.copy(
+                        out=grouped[:, i * width : (i + 1) * width].bitcast(F32).rearrange("p (g m u) -> p g m u", g=PASSES, u=2),
+                        in_=bank4.rearrange("p g u m -> p g m u"),
+                    )
+            codes, scales = new_operand(f"x{kind}{c}{h}", 2 * PASSES * P, "x", 6)
+            xcodes[kind, c, h] = (codes, scales)
+            nc.vector.quantize_mx(out=codes[:].bitcast(FP8X4), scales=scales[:], in_=grouped[:])
+
+        def x_operand(kind, c, s, g):
+            codes, scales = xcodes[kind, c, s // 2]
+            first = (s % 2) * PASSES * P + g * P
+            return codes[:, first : first + P].bitcast(FP8X4), scales[:, first : first + P]
+
+        def w_operand(name, g, h, a, b):
+            codes, scales = wcodes[name, g]
+            a, b = a + h * HALF, b + h * HALF
+            return codes[:, a:b].bitcast(FP8X4), scales[:, a:b]
+
+        kcodes, vcodes, qcodes = {}, {}, {}
+
+        def new_operand(name, words, tag, bufs):
+            codes = sb.tile([P, words], U32, name=f"{name}_codes", tag=f"{tag}_codes", bufs=bufs, align_bytes=64)
+            scales = sb.tile([P, words], U8, name=f"{name}_scales", tag=f"{tag}_scales", bufs=bufs, align_bytes=64)
+            return codes, scales
+
+        def grouped_tile(name):
+            return sb.tile([P, 2048], BF16, name=name, tag="y_grouped", bufs=4, align_bytes=64)
+
+        def project_k(c):
+            grouped = grouped_tile(f"kg{c}")
+            kcodes[c] = new_operand(f"k{c}", F, "k", 3)
+
+            def fill(q):
+                bank = ps.tile([P, 512], F32, name=f"kb{c}{q}", tag="bank")
+                for s in range(PACK):
+                    for g in range(PASSES):
+                        lhs, lhs_s = x_operand("k", c, s, g)
+                        rhs, rhs_s = w_operand("wk", g, 0, q * P, (q + 1) * P)
+                        nc.tensor.matmul_mx(
+                            out=bank[:, s * P : (s + 1) * P], lhsT=lhs, lhsT_scale=lhs_s, rhs=rhs, rhs_scale=rhs_s,
+                            start=(g == 0), stop=(g == PASSES - 1),
+                        )
+                nc.scalar.activation(
+                    out=grouped[:].rearrange("p (i m s) -> p i m s", i=PACK, s=PACK)[:, :, 32 * q : 32 * q + 32, :],
+                    in_=bank[:].rearrange("p (s m i) -> p i m s", s=PACK, i=PACK),
+                    func=ACT.Relu,
+                )
+                if q == 3:
+                    codes, scales = kcodes[c]
+                    nc.vector.quantize_mx(out=codes[:].bitcast(FP8X4), scales=scales[:], in_=grouped[:])
+
+            return [(fill, q) for q in range(4)]
+
+        def project_v(c):
+            halves = {}
+
+            def fill(n):
+                h, q = n // 4, n % 4
+                if q == 0:
+                    grouped = grouped_tile(f"vg{c}{h}")
+                    halves[h] = grouped
+                    vcodes[c, h] = new_operand(f"v{c}{h}", HALF, "v", 6)
+                grouped = halves[h]
+                if True:
+                    bank = ps.tile([P, 512], F32, name=f"vb{c}{h}{q}", tag="bank")
+                    for s in range(PACK):
+                        for g in range(PASSES):
+                            lhs, lhs_s = x_operand("v", c, s, g)
+                            rhs, rhs_s = w_operand("wv", g, h, q * P, (q + 1) * P)
+                            nc.tensor.matmul_mx(
+                                out=bank[:, s * P : (s + 1) * P], lhsT=lhs, lhsT_scale=lhs_s, rhs=rhs, rhs_scale=rhs_s,
+                                start=(g == 0), stop=(g == PASSES - 1),
+                            )
+                    copy_out(
+                        grouped[:].rearrange("p (n s) -> p n s", s=PACK)[:, q * P : (q + 1) * P, :],
+                        bank[:].rearrange("p (s n) -> p n s", s=PACK),
+                        on_vector=False,
+                    )
+                if q == 3:
+                    codes, scales = vcodes[c, h]
+                    nc.vector.quantize_mx(out=codes[:].bitcast(FP8X4), scales=scales[:], in_=grouped[:])
+
+            return [(fill, n) for n in range(8)]
+
+        def project_q(c):
+            grouped = grouped_tile(f"qg{c}")
+
+            def fill(s):
+                bank = ps.tile([P, 512], F32, name=f"qb{c}{s}", tag="bank")
+                for j in range(PACK):
+                    for g in range(PASSES):
+                        lhs, lhs_s = w_operand("wq", g, 0, j * P, (j + 1) * P)
+                        rhs, rhs_s = x_operand("q", c, s, g)
+                        nc.tensor.matmul_mx(
+                            out=bank[:, j * P : (j + 1) * P], lhsT=lhs, lhsT_scale=lhs_s, rhs=rhs, rhs_scale=rhs_s,
+                            start=(g == 0), stop=(g == PASSES - 1),
+                        )
+                copy_out(
+                    grouped[:, s * 512 : (s + 1) * 512].rearrange("p (m j) -> p m j", j=PACK),
+                    bank[:].rearrange("p (j m) -> p m j", j=PACK),
+                    on_vector=False,
+                )
+                if s % 2 == 1:
+                    pair = s // 2
+                    qcodes[c, pair] = new_operand(f"q{c}{pair}", 2 * P, "q", 4)
+                    codes, scales = qcodes[c, pair]
+                    nc.vector.quantize_mx(
+                        out=codes[:].bitcast(FP8X4), scales=scales[:], in_=grouped[:, pair * 1024 : (pair + 1) * 1024]
+                    )
+
+            return [(fill, s) for s in range(PACK)]
+
+        out_view = out_0.rearrange("(c m s) e -> c m s e", m=P, s=PACK)
+
+        def read_state(c):
+            row_tiles = {}
+
+            def fill(n):
+                s, h = n // 2, n % 2
+                codes, scales = qcodes[c, s // 2]
+                cols = slice((s % 2) * P, (s % 2 + 1) * P)
+                if h == 0:
+                    o_sb = sb.tile([P, E], F32, name=f"o{c}{s}", tag="out_rows", bufs=4)
+                    row_tiles[s] = o_sb
+                o_sb = row_tiles[s]
+                if True:
+                    bank = ps.tile([P, 512], F32, name=f"ob{c}{s}{h}", tag="bank")
+                    rhs, rhs_s = w_operand("st", 0, h, 0, HALF)
+                    nc.tensor.matmul_mx(
+                        out=bank[:], lhsT=codes[:, cols].bitcast(FP8X4), lhsT_scale=scales[:, cols],
+                        rhs=rhs, rhs_scale=rhs_s, start=True, stop=True,
+                    )
+                    copy_out(o_sb[:, h * HALF : (h + 1) * HALF], bank[:], on_vector=False)
+                if c == CHUNKS - 1:
+                    cut = slice(h * HALF, (h + 1) * HALF)
+                    nc.sync.dma_start(out=out_view[c, :, s, cut], in_=o_sb[:, cut])
+                elif h == 1:
+                    nc.sync.dma_start(out=out_view[c, :, s, :], in_=o_sb[:])
+
+            return [(fill, n) for n in range(8)]
+
+        new_view = out_1.rearrange("(p i) e -> p i e", i=PACK)
+
+        def update_state(h):
+            banks = {}
+
+            def passes(i, chunks):
+                for c in chunks:
+                    codes, scales = kcodes[c]
+                    vc, vs = vcodes[c, h]
+                    cols = slice(i * P, (i + 1) * P)
+                    nc.tensor.matmul_mx(
+                        out=banks[i][:], lhsT=codes[:, cols].bitcast(FP8X4), lhsT_scale=scales[:, cols],
+                        rhs=vc[:].bitcast(FP8X4), rhs_scale=vs[:], start=(c == 0), stop=(c == 2),
+                    )
+
+            def fill(i):
+                bank = ps.tile([P, 512], F32, name=f"ub{h}{i}", tag="bank")
+                banks[i] = bank
+                passes(i, (0, 1, 2))
+                new_sb = sb.tile([P, HALF], F32, name=f"n{h}{i}", tag="new_rows", bufs=4)
+                cut = slice(h * HALF, (h + 1) * HALF)
+                nc.vector.scalar_tensor_tensor(
+                    out=new_sb[:], in0=wraw["st", 0][:, i, cut], scalar=decay_sb[:, i : i + 1], in1=bank[:],
+                    op0=ALU.mult, op1=ALU.add,
+                )
+                nc.sync.dma_start(out=new_view[:, i, cut], in_=new_sb[:])
+
+            return [(fill, i) for i in range(PACK)]
+
+        background = []
+
+        def work(n):
+            for _ in range(min(n, len(background))):
+                job = background[0]
+                background.remove(job)
+                job()
+
+        def spread(fills, n):
+            for i, (fill, arg) in enumerate(fills):
+                work((i + 1) * n // len(fills) - i * n // len(fills))
+                fill(arg)
+
+        def mix(a, b):
+            return [x for pair in zip(a, b) for x in pair]
+
+        def run(*lists):
+            for n in range(max(len(x) for x in lists)):
+                for x in lists:
+                    if n < len(x):
+                        fill, arg = x[n]
+                        fill(arg)
+
+        with tc.manual_schedule(engines={mybir.EngineType.PE}):
+            transpose_pair("k", 0, 0)
+            transpose_pair("k", 0, 1)
+            for job in weights("wk"):
+                job()
+            load_w("wv", wv, (0,))
+            load_x("k", 2)
+            load_w("wv", wv, (1,))
+            load_x("v", 0)
+            load_x("v", 1)
+            load_scales()
+            load_x("q", 0)
+            background.extend(weights("wv"))
+            background.extend(widen_q(0))
+            transpose_pair("k", 1, 0)
+            fills = project_k(0)
+            spread(fills[:2], 1)
+            transpose_pair("k", 1, 1)
+            spread(fills[2:], 1)
+            load_w("wq", wq)
+            load_x("q", 1)
+            load_w("st", state)
+            nc.sync.dma_start(out=decay_sb[:], in_=decay.rearrange("(p i) -> p i", i=PACK))
+            load_x("v", 2)
+            background.extend(weights("wq"))
+            background.extend(widen_q(1))
+            background.extend(weights("st"))
+            background.extend(widen_q(2))
+            transpose_pair("k", 2, 0)
+            fills = project_k(1)
+            spread(fills[:2], 2)
+            transpose_pair("k", 2, 1)
+            spread(fills[2:], 1)
+            transpose_pair("v", 0, 0)
+            fills = project_k(2)
+            spread(fills[:2], 2)
+            transpose_pair("v", 0, 1)
+            spread(fills[2:], 3)
+            transpose_pair("v", 1, 0)
+            fills = project_v(0)
+            spread(fills[:4], 2)
+            transpose_pair("v", 1, 1)
+            spread(fills[4:], 0)
+            load_x("q", 2)
+            transpose_pair("q", 0, 0)
+            fills = project_v(1)
+            spread(fills[:4], 0)
+            transpose_pair("q", 0, 1)
+            spread(fills[4:], 1)
+            transpose_pair("v", 2, 0)
+            fills = project_q(0)
+            spread(fills[:2], 0)
+            transpose_pair("v", 2, 1)
+            spread(fills[2:], 1)
+            transpose_pair("q", 1, 0)
+            fills = project_v(2)
+            read = read_state(0)
+            spread(mix(fills[:4], read[:4]), 1)
+            transpose_pair("q", 1, 1)
+            spread(mix(fills[4:], read[4:]), 1)
+            transpose_pair("q", 2, 0)
+            fills = project_q(1)
+            spread(fills[:2], 0)
+            transpose_pair("q", 2, 1)
+            spread(fills[2:], 0)
+            update = update_state(0) + update_state(1)
+            read = read_state(1)
+            run(read[:4], update[:2])
+            run(project_q(2), read[4:])
+            run(update[2:3])
+            read = read_state(2)
+            run(read, update[3:5])
+            run(update[5:])

@@ -39,392 +39,396 @@ def tile_linear_state_step_s7_kernel(
         warm = sb.tile([P, 1], F32, name="warm")
         nc.vector.memset(warm[:], 0.0)
         nc.scalar.activation(out=warm[:], in_=warm[:], func=ACT.Relu)
-
-        xdram = {"k": xk, "v": xv, "q": xq_bytes}
-        rows = {}
-        rows_q = {}
-        xcodes = {}
-
-        def load_x(kind, c, cuts=(0, 4)):
-            view = xdram[kind][c * CHUNK : (c + 1) * CHUNK, :].rearrange("(m s) d -> m s d", s=PACK)
-            if kind == "q":
-                t = sb.tile([P, PACK, D], U8, name=f"xqb{c}", tag="xq_bytes", bufs=2, align_bytes=64)
-                rows_q[c] = t
-            else:
-                if cuts[0] == 0:
-                    rows[kind, c] = sb.tile([P, PACK, D], BF16, name=f"x{kind}{c}", tag="x_rows", bufs=4, align_bytes=64)
-                t = rows[kind, c]
-            for a, b in zip(cuts[:-1], cuts[1:]):
-                nc.sync.dma_start(out=t[:, a:b, :], in_=view[:, a:b, :])
-
         scale_pt = sb.tile([P, PASSES, PACK], F32, name="scale_pt", align_bytes=64)
         ones = sb.tile([P, 1], F32, name="ones")
         nc.vector.memset(ones[:], 1.0)
 
-        def load_scales():
-            nc.sync.dma_start(out=scale_pt[:], in_=xq_scale.rearrange("o (g p t) -> p (o g) t", p=P, t=PACK))
+        xdram = {"k": xk, "v": xv, "q": xq_bytes}
+        wdram = {"wk": wk, "wq": wq, "wv": wv, "st": state}
+        rows, wide_q, wraw = {}, {}, {}
+        x_grouped, x_banks, xcodes = {}, {}, {}
+        w_grouped, wcodes = {}, {}
+        y_grouped, ycodes = {}, {}
+        out_rows = {}
 
-        wraw = {}
-
-        def load_w(name, w, passes=None):
-            width = w.shape[1]
-            for g in passes or range(w.shape[0] // 512):
-                if name in ("wk", "wq"):
-                    t = sb.tile([P, PACK, width], BF16, name=f"{name}raw{g}", tag="w_small", bufs=2, align_bytes=64)
-                else:
-                    t = sb.tile([P, PACK, width], BF16, name=f"{name}raw{g}", align_bytes=64)
-                nc.sync.dma_start(out=t[:], in_=w[512 * g : 512 * (g + 1), :].rearrange("(p j) n -> p j n", j=PACK))
-                wraw[name, g] = t
-
-        load_x("k", 0, (0, 2))
-        load_w("wk", wk, (0,))
-        load_x("k", 0, (2, 4))
-        load_w("wk", wk, (1,))
-        load_x("k", 1, (0, 2))
-        load_x("k", 1, (2, 4))
-
-        wcodes = {}
-
-        def weight_piece(name, g, on_scalar=False):
-            raw = wraw[name, g]
-            width = raw.shape[2]
-            grouped = sb.tile([P, width * PACK], BF16, name=f"{name}g{g}", tag="w_grouped", bufs=2, align_bytes=64)
-            codes = sb.tile([P, width], U32, name=f"{name}c{g}", align_bytes=64)
-            scales = sb.tile([P, width], U8, name=f"{name}s{g}", align_bytes=64)
-            wcodes[name, g] = (codes, scales)
-
-            def interleave():
-                if name == "wq":
-                    nc.vector.tensor_copy(
-                        out=grouped[:].rearrange("p (t m j) -> p t m j", t=PACK, j=PACK),
-                        in_=raw[:].rearrange("p j (m t) -> p t m j", t=PACK),
-                    )
-                else:
-                    copy_out(
-                        grouped[:].rearrange("p (c i j) -> p c j i", i=4, j=PACK),
-                        raw[:].rearrange("p j (c i) -> p c j i", i=4),
-                        on_vector=not on_scalar,
-                    )
-
-            def quant():
-                nc.vector.quantize_mx(out=codes[:].bitcast(FP8X4), scales=scales[:], in_=grouped[:])
-
-            return interleave, quant
-
-        def weights(name, scalar_passes=()):
-            passes = range(F // 512 if name == "st" else PASSES)
-            made = [weight_piece(name, g, g in scalar_passes) for g in passes]
-            return [x for x, _ in made] + [x for _, x in made]
-
-        def copy_out(out, in_, on_vector):
-            if on_vector:
-                nc.vector.tensor_copy(out=out, in_=in_)
-            else:
-                nc.scalar.copy(out=out, in_=in_)
-
-        def widen_q(c):
-            def pair(h):
-                if h == 0:
-                    rows["q", c] = sb.tile([P, 2, PACK * D // 2], BF16, name=f"xq{c}", tag="xq_rows", bufs=2, align_bytes=64)
-                half = PACK * D // 4
-                nc.vector.tensor_scalar(
-                    out=rows["q", c][:, :, h * half : (h + 1) * half].rearrange("p u (m e) -> p m u e", e=2),
-                    in0=rows_q[c][:, 2 * h : 2 * h + 2, :].bitcast(FP8).rearrange("p s (m u e) -> p (s m) u e", u=2, e=2),
-                    scalar1=ones[:, 0:1], scalar2=None, op0=ALU.mult,
-                )
-
-            return [lambda: pair(0), lambda: pair(1)]
-
-        def transpose_pair(kind, c, h):
-            t = rows[kind, c]
-            width = PASSES * P * PACK
-            grouped = sb.tile([P, 2 * width], BF16, name=f"g{kind}{c}{h}", tag="x_grouped", bufs=3, align_bytes=64)
-            for i in range(2):
-                s = 2 * h + i
-                bank = ps.tile([P, 512], F32, name=f"t{kind}{c}{s}", tag="bank")
-                if kind == "q":
-                    bank4 = bank[:].rearrange("p (u g m) -> p g u m", g=PASSES, u=2)
-                else:
-                    bank4 = bank[:].rearrange("p (g u m) -> p g u m", g=PASSES, u=2)
-                for g in range(PASSES):
-                    for u in range(2):
-                        if kind == "q":
-                            first = s * PASSES * P + g * P
-                            chosen = t[:, u, :].bitcast(F32)[:, first : first + P]
-                        else:
-                            chosen = t[:, s, :].bitcast(F32)[:, 256 * g + u : 256 * (g + 1) : 2]
-                        nc.tensor.transpose(bank4[:, g, u, :], chosen, ident[:])
-                if kind == "q":
-                    nc.vector.tensor_tensor(
-                        out=grouped[:, i * width : (i + 1) * width].rearrange("p (g m u e) -> p g m u e", g=PASSES, u=2, e=2),
-                        in0=bank[:].bitcast(BF16).rearrange("p (u g m e) -> p g m u e", g=PASSES, u=2, e=2),
-                        in1=scale_pt[:].rearrange("p g (u e) -> p g u e", u=2).unsqueeze(2).to_broadcast([P, PASSES, P, 2, 2]),
-                        op=ALU.mult,
-                    )
-                else:
-                    nc.scalar.copy(
-                        out=grouped[:, i * width : (i + 1) * width].bitcast(F32).rearrange("p (g m u) -> p g m u", g=PASSES, u=2),
-                        in_=bank4.rearrange("p g u m -> p g m u"),
-                    )
-            codes, scales = new_operand(f"x{kind}{c}{h}", 2 * PASSES * P, "x", 6)
-            xcodes[kind, c, h] = (codes, scales)
-            nc.vector.quantize_mx(out=codes[:].bitcast(FP8X4), scales=scales[:], in_=grouped[:])
-
-        def x_operand(kind, c, s, g):
-            codes, scales = xcodes[kind, c, s // 2]
-            first = (s % 2) * PASSES * P + g * P
-            return codes[:, first : first + P].bitcast(FP8X4), scales[:, first : first + P]
-
-        def w_operand(name, g, h, a, b):
-            codes, scales = wcodes[name, g]
-            a, b = a + h * HALF, b + h * HALF
-            return codes[:, a:b].bitcast(FP8X4), scales[:, a:b]
-
-        kcodes, vcodes, qcodes = {}, {}, {}
+        def new_bank(name):
+            return ps.tile([P, 512], F32, name=name, tag="bank")
 
         def new_operand(name, words, tag, bufs):
             codes = sb.tile([P, words], U32, name=f"{name}_codes", tag=f"{tag}_codes", bufs=bufs, align_bytes=64)
             scales = sb.tile([P, words], U8, name=f"{name}_scales", tag=f"{tag}_scales", bufs=bufs, align_bytes=64)
             return codes, scales
 
-        def grouped_tile(name):
-            return sb.tile([P, 2048], BF16, name=name, tag="y_grouped", bufs=4, align_bytes=64)
+        def quantize(operand, grouped):
+            codes, scales = operand
+            nc.vector.quantize_mx(out=codes[:].bitcast(FP8X4), scales=scales[:], in_=grouped)
 
-        def project_k(c):
-            grouped = grouped_tile(f"kg{c}")
-            kcodes[c] = new_operand(f"k{c}", F, "k", 3)
+        def columns(operand, first, width):
+            codes, scales = operand
+            return codes[:, first : first + width].bitcast(FP8X4), scales[:, first : first + width]
 
-            def fill(q):
-                bank = ps.tile([P, 512], F32, name=f"kb{c}{q}", tag="bank")
-                for s in range(PACK):
-                    for g in range(PASSES):
-                        lhs, lhs_s = x_operand("k", c, s, g)
-                        rhs, rhs_s = w_operand("wk", g, 0, q * P, (q + 1) * P)
-                        nc.tensor.matmul_mx(
-                            out=bank[:, s * P : (s + 1) * P], lhsT=lhs, lhsT_scale=lhs_s, rhs=rhs, rhs_scale=rhs_s,
-                            start=(g == 0), stop=(g == PASSES - 1),
-                        )
-                nc.scalar.activation(
-                    out=grouped[:].rearrange("p (i m s) -> p i m s", i=PACK, s=PACK)[:, :, 32 * q : 32 * q + 32, :],
-                    in_=bank[:].rearrange("p (s m i) -> p i m s", s=PACK, i=PACK),
-                    func=ACT.Relu,
+        def multiply(out, stationary, moving, start, stop):
+            nc.tensor.matmul_mx(
+                out=out, lhsT=stationary[0], lhsT_scale=stationary[1], rhs=moving[0], rhs_scale=moving[1],
+                start=start, stop=stop,
+            )
+
+        def copy_on(engine, out, in_):
+            if engine == "vector":
+                nc.vector.tensor_copy(out=out, in_=in_)
+            else:
+                nc.scalar.copy(out=out, in_=in_)
+
+        def load_x(kind, c, h):
+            view = xdram[kind][c * CHUNK : (c + 1) * CHUNK, :].rearrange("(m s) d -> m s d", s=PACK)
+            if kind == "q":
+                t = sb.tile([P, 2, D], U8, name=f"xqb{c}{h}", tag="xq_bytes", bufs=6, align_bytes=64)
+            else:
+                t = sb.tile([P, 2, D], BF16, name=f"x{kind}{c}{h}", tag="rows", bufs=10, align_bytes=64)
+            rows[kind, c, h] = t
+            nc.sync.dma_start(out=t[:], in_=view[:, 2 * h : 2 * h + 2, :])
+
+        def load_w(name, g):
+            w = wdram[name]
+            width = w.shape[1]
+            if width == HALF:
+                t = sb.tile([P, PACK, width], BF16, name=f"{name}raw{g}", tag="w_small", bufs=2, align_bytes=64)
+            else:
+                t = sb.tile([P, PACK, width], BF16, name=f"{name}raw{g}", align_bytes=64)
+            nc.sync.dma_start(out=t[:], in_=w[512 * g : 512 * (g + 1), :].rearrange("(p j) n -> p j n", j=PACK))
+            wraw[name, g] = t
+
+        def load_scales():
+            nc.sync.dma_start(out=scale_pt[:], in_=xq_scale.rearrange("o (g p t) -> p (o g) t", p=P, t=PACK))
+
+        def load_decay():
+            nc.sync.dma_start(out=decay_sb[:], in_=decay.rearrange("(p i) -> p i", i=PACK))
+
+        def w_interleave(name, g, h, engine="vector", first=0, width=HALF):
+            raw = wraw[name, g][:, :, h * HALF + first : h * HALF + first + width]
+            if first == 0:
+                w_grouped[name, g, h] = sb.tile(
+                    [P, HALF * PACK], BF16, name=f"{name}g{g}{h}", tag="w_grouped", bufs=4, align_bytes=64
                 )
-                if q == 3:
-                    codes, scales = kcodes[c]
-                    nc.vector.quantize_mx(out=codes[:].bitcast(FP8X4), scales=scales[:], in_=grouped[:])
-
-            return [(fill, q) for q in range(4)]
-
-        def project_v(c):
-            halves = {}
-
-            def fill(n):
-                h, q = n // 4, n % 4
-                if q == 0:
-                    grouped = grouped_tile(f"vg{c}{h}")
-                    halves[h] = grouped
-                    vcodes[c, h] = new_operand(f"v{c}{h}", HALF, "v", 6)
-                grouped = halves[h]
-                if True:
-                    bank = ps.tile([P, 512], F32, name=f"vb{c}{h}{q}", tag="bank")
-                    for s in range(PACK):
-                        for g in range(PASSES):
-                            lhs, lhs_s = x_operand("v", c, s, g)
-                            rhs, rhs_s = w_operand("wv", g, h, q * P, (q + 1) * P)
-                            nc.tensor.matmul_mx(
-                                out=bank[:, s * P : (s + 1) * P], lhsT=lhs, lhsT_scale=lhs_s, rhs=rhs, rhs_scale=rhs_s,
-                                start=(g == 0), stop=(g == PASSES - 1),
-                            )
-                    copy_out(
-                        grouped[:].rearrange("p (n s) -> p n s", s=PACK)[:, q * P : (q + 1) * P, :],
-                        bank[:].rearrange("p (s n) -> p n s", s=PACK),
-                        on_vector=False,
-                    )
-                if q == 3:
-                    codes, scales = vcodes[c, h]
-                    nc.vector.quantize_mx(out=codes[:].bitcast(FP8X4), scales=scales[:], in_=grouped[:])
-
-            return [(fill, n) for n in range(8)]
-
-        def project_q(c):
-            grouped = grouped_tile(f"qg{c}")
-
-            def fill(s):
-                bank = ps.tile([P, 512], F32, name=f"qb{c}{s}", tag="bank")
-                for j in range(PACK):
-                    for g in range(PASSES):
-                        lhs, lhs_s = w_operand("wq", g, 0, j * P, (j + 1) * P)
-                        rhs, rhs_s = x_operand("q", c, s, g)
-                        nc.tensor.matmul_mx(
-                            out=bank[:, j * P : (j + 1) * P], lhsT=lhs, lhsT_scale=lhs_s, rhs=rhs, rhs_scale=rhs_s,
-                            start=(g == 0), stop=(g == PASSES - 1),
-                        )
-                copy_out(
-                    grouped[:, s * 512 : (s + 1) * 512].rearrange("p (m j) -> p m j", j=PACK),
-                    bank[:].rearrange("p (j m) -> p m j", j=PACK),
-                    on_vector=False,
+            grouped = w_grouped[name, g, h][:, first * PACK : (first + width) * PACK]
+            if name == "wq":
+                copy_on(
+                    engine,
+                    grouped.rearrange("p (t c i j) -> p c t (i j)", t=PACK, i=2, j=PACK).rearrange("p c t (i j) -> p c t i j", i=2),
+                    raw.rearrange("p j (c i t) -> p c t i j", i=2, t=PACK),
                 )
-                if s % 2 == 1:
-                    pair = s // 2
-                    qcodes[c, pair] = new_operand(f"q{c}{pair}", 2 * P, "q", 4)
-                    codes, scales = qcodes[c, pair]
-                    nc.vector.quantize_mx(
-                        out=codes[:].bitcast(FP8X4), scales=scales[:], in_=grouped[:, pair * 1024 : (pair + 1) * 1024]
-                    )
+            else:
+                copy_on(
+                    engine,
+                    grouped.rearrange("p (c i j) -> p c j i", i=4, j=PACK),
+                    raw.rearrange("p j (c i) -> p c j i", i=4),
+                )
 
-            return [(fill, s) for s in range(PACK)]
+        def w_quantize(name, g, h):
+            wcodes[name, g, h] = new_operand(f"{name}c{g}{h}", HALF, f"{name}{g}{h}", 1)
+            quantize(wcodes[name, g, h], w_grouped[name, g, h][:])
+
+        def widen(c, h):
+            t = sb.tile([P, 2, D], BF16, name=f"xq{c}{h}", tag="xq_rows", bufs=4, align_bytes=64)
+            wide_q[c, h] = t
+            nc.vector.tensor_scalar(
+                out=t[:].rearrange("p u (m e) -> p m u e", e=2),
+                in0=rows["q", c, h][:].bitcast(FP8).rearrange("p s (m u e) -> p (s m) u e", u=2, e=2),
+                scalar1=ones[:, 0:1], scalar2=None, op0=ALU.mult,
+            )
+
+        def turn(kind, c, s):
+            h, i = s // 2, s % 2
+            bank = new_bank(f"t{kind}{c}{s}")
+            x_banks[kind, c, s] = bank
+            for g in range(PASSES):
+                for u in range(2):
+                    if kind == "q":
+                        first = (i * PASSES + g) * P
+                        chosen = wide_q[c, h][:, u, :].bitcast(F32)[:, first : first + P]
+                        place = (u * PASSES + g) * P
+                    else:
+                        chosen = rows[kind, c, h][:, i, :].bitcast(F32)[:, 256 * g + u : 256 * (g + 1) : 2]
+                        place = (g * 2 + u) * P
+                    nc.tensor.transpose(bank[:, place : place + P], chosen, ident[:])
+            if kind != "q":
+                empty_turned(kind, c, s)
+
+        def empty_turned(kind, c, s):
+            h, i = s // 2, s % 2
+            width = PASSES * P * PACK
+            if i == 0:
+                x_grouped[kind, c, h] = sb.tile(
+                    [P, 2 * width], BF16, name=f"g{kind}{c}{h}", tag="x_grouped", bufs=4, align_bytes=64
+                )
+            part = x_grouped[kind, c, h][:, i * width : (i + 1) * width]
+            bank = x_banks[kind, c, s]
+            if kind == "q":
+                nc.vector.tensor_tensor(
+                    out=part.rearrange("p (g m u e) -> p g m u e", g=PASSES, u=2, e=2),
+                    in0=bank[:].bitcast(BF16).rearrange("p (u g m e) -> p g m u e", g=PASSES, u=2, e=2),
+                    in1=scale_pt[:].rearrange("p g (u e) -> p g u e", u=2).unsqueeze(2).to_broadcast([P, PASSES, P, 2, 2]),
+                    op=ALU.mult,
+                )
+            else:
+                nc.scalar.copy(
+                    out=part.bitcast(F32).rearrange("p (g m u) -> p g m u", g=PASSES, u=2),
+                    in_=bank[:].rearrange("p (g u m) -> p g m u", g=PASSES, u=2),
+                )
+
+        def x_quantize(kind, c, h):
+            xcodes[kind, c, h] = new_operand(f"x{kind}{c}{h}", 2 * PASSES * P, "x", 6)
+            quantize(xcodes[kind, c, h], x_grouped[kind, c, h][:])
+
+        def x_operand(kind, c, s, g):
+            return columns(xcodes[kind, c, s // 2], ((s % 2) * PASSES + g) * P, P)
+
+        def grouped_y(key, first):
+            if first:
+                y_grouped[key] = sb.tile(
+                    [P, 2048], BF16, name="y" + "".join(str(x) for x in key), tag="y_grouped", bufs=8, align_bytes=64
+                )
+            return y_grouped[key]
+
+        def project_k(c, q):
+            grouped = grouped_y(("k", c, 0), q == 0)
+            bank = new_bank(f"kb{c}{q}")
+            for s in range(PACK):
+                for g in range(PASSES):
+                    multiply(bank[:, s * P : (s + 1) * P], x_operand("k", c, s, g),
+                             columns(wcodes["wk", g, 0], q * P, P), g == 0, g == PASSES - 1)
+            nc.scalar.activation(
+                out=grouped[:].rearrange("p (i m s) -> p i m s", i=PACK, s=PACK)[:, :, 32 * q : 32 * q + 32, :],
+                in_=bank[:].rearrange("p (s m i) -> p i m s", s=PACK, i=PACK),
+                func=ACT.Relu,
+            )
+
+        def project_v(c, h, q, engine="scalar"):
+            grouped = grouped_y(("v", c, h), q == 0)
+            bank = new_bank(f"vb{c}{h}{q}")
+            for s in range(PACK):
+                for g in range(PASSES):
+                    multiply(bank[:, s * P : (s + 1) * P], x_operand("v", c, s, g),
+                             columns(wcodes["wv", g, h], q * P, P), g == 0, g == PASSES - 1)
+            copy_on(
+                engine,
+                grouped[:].rearrange("p (n s) -> p n s", s=PACK)[:, q * P : (q + 1) * P, :],
+                bank[:].rearrange("p (s n) -> p n s", s=PACK),
+            )
+
+        def y_quantize(kind, c, h):
+            ycodes[kind, c, h] = new_operand(f"{kind}{c}{h}", HALF, kind, 3 if kind == "k" else 6)
+            quantize(ycodes[kind, c, h], y_grouped[kind, c, h][:])
+
+        def project_q(c, s, engine="scalar"):
+            grouped = grouped_y(("q", c, 0), s == 0)
+            bank = new_bank(f"qb{c}{s}")
+            for j in range(PACK):
+                for g in range(PASSES):
+                    multiply(bank[:, j * P : (j + 1) * P], columns(wcodes["wq", g, 0], j * P, P),
+                             x_operand("q", c, s, g), g == 0, g == PASSES - 1)
+            copy_on(
+                engine,
+                grouped[:, s * 512 : (s + 1) * 512].rearrange("p (m j) -> p m j", j=PACK),
+                bank[:].rearrange("p (j m) -> p m j", j=PACK),
+            )
+
+        def q_quantize(c, h):
+            ycodes["q", c, h] = new_operand(f"q{c}{h}", 2 * P, "q", 4)
+            quantize(ycodes["q", c, h], y_grouped["q", c, 0][:, h * 1024 : (h + 1) * 1024])
 
         out_view = out_0.rearrange("(c m s) e -> c m s e", m=P, s=PACK)
 
-        def read_state(c):
-            row_tiles = {}
-
-            def fill(n):
-                s, h = n // 2, n % 2
-                codes, scales = qcodes[c, s // 2]
-                cols = slice((s % 2) * P, (s % 2 + 1) * P)
-                if h == 0:
-                    o_sb = sb.tile([P, E], F32, name=f"o{c}{s}", tag="out_rows", bufs=4)
-                    row_tiles[s] = o_sb
-                o_sb = row_tiles[s]
-                if True:
-                    bank = ps.tile([P, 512], F32, name=f"ob{c}{s}{h}", tag="bank")
-                    rhs, rhs_s = w_operand("st", 0, h, 0, HALF)
-                    nc.tensor.matmul_mx(
-                        out=bank[:], lhsT=codes[:, cols].bitcast(FP8X4), lhsT_scale=scales[:, cols],
-                        rhs=rhs, rhs_scale=rhs_s, start=True, stop=True,
-                    )
-                    copy_out(o_sb[:, h * HALF : (h + 1) * HALF], bank[:], on_vector=False)
-                if c == CHUNKS - 1:
-                    cut = slice(h * HALF, (h + 1) * HALF)
-                    nc.sync.dma_start(out=out_view[c, :, s, cut], in_=o_sb[:, cut])
-                elif h == 1:
-                    nc.sync.dma_start(out=out_view[c, :, s, :], in_=o_sb[:])
-
-            return [(fill, n) for n in range(8)]
+        def read_state(c, s, h, engine="scalar"):
+            if h == 0:
+                out_rows[c, s] = sb.tile([P, E], F32, name=f"o{c}{s}", tag="rows", bufs=10, align_bytes=64)
+            o_sb = out_rows[c, s]
+            bank = new_bank(f"ob{c}{s}{h}")
+            multiply(bank[:], columns(ycodes["q", c, s // 2], (s % 2) * P, P), columns(wcodes["st", 0, h], 0, HALF),
+                     True, True)
+            copy_on(engine, o_sb[:, h * HALF : (h + 1) * HALF], bank[:])
+            if h == 1:
+                nc.sync.dma_start(out=out_view[c, :, s, :], in_=o_sb[:])
 
         new_view = out_1.rearrange("(p i) e -> p i e", i=PACK)
 
-        def update_state(h):
-            banks = {}
+        def update_state(h, i):
+            bank = new_bank(f"ub{h}{i}")
+            for c in range(CHUNKS):
+                multiply(bank[:], columns(ycodes["k", c, 0], i * P, P), columns(ycodes["v", c, h], 0, HALF),
+                         c == 0, c == CHUNKS - 1)
+            new_sb = sb.tile([P, HALF], F32, name=f"n{h}{i}", tag="rows", bufs=10, align_bytes=64)
+            cut = slice(h * HALF, (h + 1) * HALF)
+            nc.vector.scalar_tensor_tensor(
+                out=new_sb[:], in0=wraw["st", 0][:, i, cut], scalar=decay_sb[:, i : i + 1], in1=bank[:],
+                op0=ALU.mult, op1=ALU.add,
+            )
+            nc.sync.dma_start(out=new_view[:, i, cut], in_=new_sb[:])
 
-            def passes(i, chunks):
-                for c in chunks:
-                    codes, scales = kcodes[c]
-                    vc, vs = vcodes[c, h]
-                    cols = slice(i * P, (i + 1) * P)
-                    nc.tensor.matmul_mx(
-                        out=banks[i][:], lhsT=codes[:, cols].bitcast(FP8X4), lhsT_scale=scales[:, cols],
-                        rhs=vc[:].bitcast(FP8X4), rhs_scale=vs[:], start=(c == 0), stop=(c == 2),
-                    )
+        def turn_pair(kind, c, h):
+            turn(kind, c, 2 * h)
+            turn(kind, c, 2 * h + 1)
 
-            def fill(i):
-                bank = ps.tile([P, 512], F32, name=f"ub{h}{i}", tag="bank")
-                banks[i] = bank
-                passes(i, (0, 1, 2))
-                new_sb = sb.tile([P, HALF], F32, name=f"n{h}{i}", tag="new_rows", bufs=4)
-                cut = slice(h * HALF, (h + 1) * HALF)
-                nc.vector.scalar_tensor_tensor(
-                    out=new_sb[:], in0=wraw["st", 0][:, i, cut], scalar=decay_sb[:, i : i + 1], in1=bank[:],
-                    op0=ALU.mult, op1=ALU.add,
-                )
-                nc.sync.dma_start(out=new_view[:, i, cut], in_=new_sb[:])
+        def keys(c, h):
+            project_k(c, 2 * h)
+            project_k(c, 2 * h + 1)
 
-            return [(fill, i) for i in range(PACK)]
+        def queries(c, h):
+            project_q(c, 2 * h)
+            project_q(c, 2 * h + 1)
 
-        background = []
+        def scale_pair(c, h):
+            empty_turned("q", c, 2 * h)
+            empty_turned("q", c, 2 * h + 1)
 
-        def work(n):
-            for _ in range(min(n, len(background))):
-                job = background[0]
-                background.remove(job)
-                job()
+        def values(c, h):
+            for q in range(4):
+                project_v(c, h, q)
 
-        def spread(fills, n):
-            for i, (fill, arg) in enumerate(fills):
-                work((i + 1) * n // len(fills) - i * n // len(fills))
-                fill(arg)
+        def weight(name, g, h):
+            w_interleave(name, g, h)
+            w_quantize(name, g, h)
 
-        def mix(a, b):
-            return [x for pair in zip(a, b) for x in pair]
-
-        def run(*lists):
-            for n in range(max(len(x) for x in lists)):
-                for x in lists:
-                    if n < len(x):
-                        fill, arg = x[n]
-                        fill(arg)
-
-        with tc.manual_schedule(engines={mybir.EngineType.PE}):
-            transpose_pair("k", 0, 0)
-            transpose_pair("k", 0, 1)
-            for job in weights("wk"):
-                job()
-            load_w("wv", wv, (0,))
-            load_x("k", 2)
-            load_w("wv", wv, (1,))
-            load_x("v", 0)
-            load_x("v", 1)
+        with tc.manual_schedule():
+            load_x("k", 0, 0)
+            load_w("wk", 0)
+            load_x("k", 0, 1)
+            load_w("wk", 1)
+            load_x("k", 1, 0)
+            load_x("k", 1, 1)
+            load_w("wv", 0)
+            load_x("k", 2, 0)
+            load_x("k", 2, 1)
+            load_w("wv", 1)
+            load_x("v", 0, 0)
+            load_x("v", 0, 1)
             load_scales()
-            load_x("q", 0)
-            background.extend(weights("wv"))
-            background.extend(widen_q(0))
-            transpose_pair("k", 1, 0)
-            fills = project_k(0)
-            spread(fills[:2], 1)
-            transpose_pair("k", 1, 1)
-            spread(fills[2:], 1)
-            load_w("wq", wq)
-            load_x("q", 1)
-            load_w("st", state)
-            nc.sync.dma_start(out=decay_sb[:], in_=decay.rearrange("(p i) -> p i", i=PACK))
-            load_x("v", 2)
-            background.extend(weights("wq"))
-            background.extend(widen_q(1))
-            background.extend(weights("st"))
-            background.extend(widen_q(2))
-            transpose_pair("k", 2, 0)
-            fills = project_k(1)
-            spread(fills[:2], 2)
-            transpose_pair("k", 2, 1)
-            spread(fills[2:], 1)
-            transpose_pair("v", 0, 0)
-            fills = project_k(2)
-            spread(fills[:2], 2)
-            transpose_pair("v", 0, 1)
-            spread(fills[2:], 3)
-            transpose_pair("v", 1, 0)
-            fills = project_v(0)
-            spread(fills[:4], 2)
-            transpose_pair("v", 1, 1)
-            spread(fills[4:], 0)
-            load_x("q", 2)
-            transpose_pair("q", 0, 0)
-            fills = project_v(1)
-            spread(fills[:4], 0)
-            transpose_pair("q", 0, 1)
-            spread(fills[4:], 1)
-            transpose_pair("v", 2, 0)
-            fills = project_q(0)
-            spread(fills[:2], 0)
-            transpose_pair("v", 2, 1)
-            spread(fills[2:], 1)
-            transpose_pair("q", 1, 0)
-            fills = project_v(2)
-            read = read_state(0)
-            spread(mix(fills[:4], read[:4]), 1)
-            transpose_pair("q", 1, 1)
-            spread(mix(fills[4:], read[4:]), 1)
-            transpose_pair("q", 2, 0)
-            fills = project_q(1)
-            spread(fills[:2], 0)
-            transpose_pair("q", 2, 1)
-            spread(fills[2:], 0)
-            update = update_state(0) + update_state(1)
-            read = read_state(1)
-            run(read[:4], update[:2])
-            run(project_q(2), read[4:])
-            run(update[2:3])
-            read = read_state(2)
-            run(read, update[3:5])
-            run(update[5:])
+            load_x("q", 0, 0)
+            load_x("q", 0, 1)
+            load_x("v", 1, 0)
+            load_x("v", 1, 1)
+
+            turn_pair("k", 0, 0)
+            w_interleave("wk", 0, 0)
+            x_quantize("k", 0, 0)
+            w_quantize("wk", 0, 0)
+            turn_pair("k", 0, 1)
+            w_interleave("wk", 1, 0)
+            x_quantize("k", 0, 1)
+            w_quantize("wk", 1, 0)
+            load_w("wq", 0)
+            load_w("wq", 1)
+            load_x("q", 1, 0)
+            load_x("q", 1, 1)
+            load_w("st", 0)
+            load_decay()
+
+            turn_pair("k", 1, 0)
+            x_quantize("k", 1, 0)
+            keys(0, 0)
+            turn_pair("k", 1, 1)
+            w_interleave("wv", 0, 0)
+            w_interleave("wv", 0, 1)
+            x_quantize("k", 1, 1)
+            load_x("v", 2, 0)
+            load_x("v", 2, 1)
+            load_x("q", 2, 0)
+            load_x("q", 2, 1)
+            keys(0, 1)
+            turn_pair("k", 2, 0)
+            w_quantize("wv", 0, 0)
+            w_quantize("wv", 0, 1)
+            y_quantize("k", 0, 0)
+            x_quantize("k", 2, 0)
+            keys(1, 0)
+            turn_pair("k", 2, 1)
+            w_interleave("wv", 1, 0)
+            w_interleave("wv", 1, 1)
+            x_quantize("k", 2, 1)
+            keys(1, 1)
+            turn_pair("v", 0, 0)
+            w_quantize("wv", 1, 0)
+            w_quantize("wv", 1, 1)
+            y_quantize("k", 1, 0)
+            x_quantize("v", 0, 0)
+            keys(2, 0)
+            turn_pair("v", 0, 1)
+            widen(0, 0)
+            widen(0, 1)
+            x_quantize("v", 0, 1)
+            keys(2, 1)
+
+            turn_pair("v", 1, 0)
+            w_interleave("wq", 0, 0)
+            w_interleave("wq", 1, 0)
+            x_quantize("v", 1, 0)
+            y_quantize("k", 2, 0)
+            w_quantize("wq", 0, 0)
+            w_quantize("wq", 1, 0)
+            values(0, 0)
+            turn_pair("v", 1, 1)
+            widen(1, 0)
+            x_quantize("v", 1, 1)
+            widen(1, 1)
+            values(0, 1)
+            for h in range(2):
+                turn_pair("q", 0, h)
+                w_interleave("st", 0, 0, "scalar", 256 * h, 256)
+                scale_pair(0, h)
+                y_quantize("v", 0, h)
+                x_quantize("q", 0, h)
+                values(1, h)
+            turn_pair("q", 1, 0)
+            w_interleave("st", 0, 1, "scalar", 0, 256)
+            scale_pair(1, 0)
+            queries(0, 0)
+            w_quantize("st", 0, 0)
+            x_quantize("q", 1, 0)
+            q_quantize(0, 0)
+            turn_pair("q", 1, 1)
+            w_interleave("st", 0, 1, "scalar", 256, 256)
+            w_quantize("st", 0, 1)
+            scale_pair(1, 1)
+            queries(0, 1)
+            q_quantize(0, 1)
+            x_quantize("q", 1, 1)
+            for h in range(2):
+                turn_pair("v", 2, h)
+                project_q(1, 2 * h)
+                read_state(0, 2 * h, 0)
+                read_state(0, 2 * h, 1, "vector")
+                x_quantize("v", 2, h)
+                project_q(1, 2 * h + 1)
+                read_state(0, 2 * h + 1, 0)
+                read_state(0, 2 * h + 1, 1, "vector")
+                q_quantize(1, h)
+                if h == 0:
+                    widen(2, 0)
+            for h in range(2):
+                turn_pair("q", 2, h)
+                scale_pair(2, h)
+                if h == 0:
+                    widen(2, 1)
+                else:
+                    y_quantize("v", 1, 0)
+                x_quantize("q", 2, h)
+                for q in range(4):
+                    read_state(1, 2 * h + q // 2, q % 2)
+                    project_v(2, h, q)
+            y_quantize("v", 2, 0)
+            y_quantize("v", 1, 1)
+            last = 2
+            queries(last, 0)
+            y_quantize("v", 2, 1)
+            update_state(0, 0)
+            q_quantize(last, 0)
+            queries(last, 1)
+            for h in range(2):
+                if h == 1:
+                    q_quantize(last, 1)
+                    update_state(0, 1)
+                for s in range(2 * h, 2 * h + 2):
+                    read_state(last, s, 0)
+                    read_state(last, s, 1, "vector" if s % 2 == 0 else "scalar")
+            for n in range(2, 8):
+                update_state(n // 4, n % 4)

@@ -252,15 +252,15 @@ def tile_linear_state_step_s7_kernel(
 
         new_view = out_1.rearrange("(p i) e -> p i e", i=PACK)
 
-        def update_state(h, i):
-            bank = new_bank(f"ub{h}{i}")
+        def update_state(h, i, first=0, width=HALF):
+            bank = new_bank(f"ub{h}{i}{first}")
             for c in range(CHUNKS):
-                multiply(bank[:], columns(ycodes["k", c, 0], i * P, P), columns(ycodes["v", c, h], 0, HALF),
+                multiply(bank[:, :width], columns(ycodes["k", c, 0], i * P, P), columns(ycodes["v", c, h], first, width),
                          c == 0, c == CHUNKS - 1)
-            new_sb = sb.tile([P, HALF], F32, name=f"n{h}{i}", tag="rows", bufs=10, align_bytes=64)
-            cut = slice(h * HALF, (h + 1) * HALF)
+            new_sb = sb.tile([P, width], F32, name=f"n{h}{i}{first}", tag="rows", bufs=10, align_bytes=64)
+            cut = slice(h * HALF + first, h * HALF + first + width)
             nc.vector.scalar_tensor_tensor(
-                out=new_sb[:], in0=wraw["st", 0][:, i, cut], scalar=decay_sb[:, i : i + 1], in1=bank[:],
+                out=new_sb[:], in0=wraw["st", 0][:, i, cut], scalar=decay_sb[:, i : i + 1], in1=bank[:, :width],
                 op0=ALU.mult, op1=ALU.add,
             )
             nc.sync.dma_start(out=new_view[:, i, cut], in_=new_sb[:])
@@ -289,24 +289,32 @@ def tile_linear_state_step_s7_kernel(
             w_interleave(name, g, h)
             w_quantize(name, g, h)
 
+        def read_pair(c, h, second="vector"):
+            for s in (2 * h, 2 * h + 1):
+                read_state(c, s, 0)
+                read_state(c, s, 1, second)
+
+        def turn_chunk(kind, c):
+            turn_pair(kind, c, 0)
+            turn_pair(kind, c, 1)
+
+        def load_chunk(kind, c):
+            load_x(kind, c, 0)
+            load_x(kind, c, 1)
+
         with tc.manual_schedule():
             load_x("k", 0, 0)
             load_w("wk", 0)
             load_x("k", 0, 1)
             load_w("wk", 1)
             load_x("k", 1, 0)
+            load_chunk("q", 0)
             load_x("k", 1, 1)
             load_w("wv", 0)
-            load_x("k", 2, 0)
-            load_x("k", 2, 1)
+            load_chunk("k", 2)
             load_w("wv", 1)
-            load_x("v", 0, 0)
-            load_x("v", 0, 1)
-            load_scales()
-            load_x("q", 0, 0)
-            load_x("q", 0, 1)
-            load_x("v", 1, 0)
-            load_x("v", 1, 1)
+            load_chunk("v", 0)
+            load_chunk("v", 1)
 
             turn_pair("k", 0, 0)
             w_interleave("wk", 0, 0)
@@ -318,117 +326,129 @@ def tile_linear_state_step_s7_kernel(
             w_quantize("wk", 1, 0)
             load_w("wq", 0)
             load_w("wq", 1)
-            load_x("q", 1, 0)
-            load_x("q", 1, 1)
+            load_scales()
+            load_chunk("q", 1)
             load_w("st", 0)
             load_decay()
 
             turn_pair("k", 1, 0)
+            widen(0, 0)
             x_quantize("k", 1, 0)
+            widen(0, 1)
             keys(0, 0)
             turn_pair("k", 1, 1)
             w_interleave("wv", 0, 0)
-            w_interleave("wv", 0, 1)
             x_quantize("k", 1, 1)
-            load_x("v", 2, 0)
-            load_x("v", 2, 1)
-            load_x("q", 2, 0)
-            load_x("q", 2, 1)
+            w_interleave("wv", 0, 1)
+            load_chunk("v", 2)
+            load_chunk("q", 2)
             keys(0, 1)
-            turn_pair("k", 2, 0)
+
+            turn_chunk("k", 2)
             w_quantize("wv", 0, 0)
             w_quantize("wv", 0, 1)
-            y_quantize("k", 0, 0)
             x_quantize("k", 2, 0)
-            keys(1, 0)
-            turn_pair("k", 2, 1)
+            y_quantize("k", 0, 0)
+            x_quantize("k", 2, 1)
             w_interleave("wv", 1, 0)
             w_interleave("wv", 1, 1)
-            x_quantize("k", 2, 1)
+            keys(1, 0)
             keys(1, 1)
-            turn_pair("v", 0, 0)
+
+            turn_chunk("v", 0)
+            y_quantize("k", 1, 0)
             w_quantize("wv", 1, 0)
             w_quantize("wv", 1, 1)
-            y_quantize("k", 1, 0)
             x_quantize("v", 0, 0)
-            keys(2, 0)
-            turn_pair("v", 0, 1)
-            widen(0, 0)
-            widen(0, 1)
             x_quantize("v", 0, 1)
+            keys(2, 0)
             keys(2, 1)
 
-            turn_pair("v", 1, 0)
+            turn_chunk("v", 1)
             w_interleave("wq", 0, 0)
             w_interleave("wq", 1, 0)
-            x_quantize("v", 1, 0)
             y_quantize("k", 2, 0)
+            x_quantize("v", 1, 0)
+            x_quantize("v", 1, 1)
             w_quantize("wq", 0, 0)
             w_quantize("wq", 1, 0)
-            values(0, 0)
-            turn_pair("v", 1, 1)
             widen(1, 0)
-            x_quantize("v", 1, 1)
             widen(1, 1)
+            values(0, 0)
             values(0, 1)
-            for h in range(2):
-                turn_pair("q", 0, h)
-                w_interleave("st", 0, 0, "scalar", 256 * h, 256)
-                scale_pair(0, h)
-                y_quantize("v", 0, h)
-                x_quantize("q", 0, h)
-                values(1, h)
-            turn_pair("q", 1, 0)
+            w_interleave("st", 0, 0)
+
+            turn_chunk("q", 0)
             w_interleave("st", 0, 1, "scalar", 0, 256)
-            scale_pair(1, 0)
-            queries(0, 0)
+            scale_pair(0, 0)
             w_quantize("st", 0, 0)
-            x_quantize("q", 1, 0)
-            q_quantize(0, 0)
-            turn_pair("q", 1, 1)
+            x_quantize("q", 0, 0)
+            scale_pair(0, 1)
+            y_quantize("v", 0, 0)
+            x_quantize("q", 0, 1)
+            values(1, 0)
+            values(1, 1)
+
+            turn_chunk("q", 1)
             w_interleave("st", 0, 1, "scalar", 256, 256)
+            scale_pair(1, 0)
             w_quantize("st", 0, 1)
-            scale_pair(1, 1)
+            x_quantize("q", 1, 0)
+            queries(0, 0)
             queries(0, 1)
+            q_quantize(0, 0)
+            scale_pair(1, 1)
             q_quantize(0, 1)
             x_quantize("q", 1, 1)
+
+            widen(2, 0)
+            widen(2, 1)
+
+            turn_chunk("v", 2)
+            x_quantize("v", 2, 0)
+            x_quantize("v", 2, 1)
             for h in range(2):
-                turn_pair("v", 2, h)
-                project_q(1, 2 * h)
                 read_state(0, 2 * h, 0)
-                read_state(0, 2 * h, 1, "vector")
-                x_quantize("v", 2, h)
-                project_q(1, 2 * h + 1)
+                project_q(1, 2 * h)
+                read_state(0, 2 * h, 1)
                 read_state(0, 2 * h + 1, 0)
-                read_state(0, 2 * h + 1, 1, "vector")
-                q_quantize(1, h)
-                if h == 0:
-                    widen(2, 0)
-            for h in range(2):
-                turn_pair("q", 2, h)
-                scale_pair(2, h)
-                if h == 0:
-                    widen(2, 1)
-                else:
-                    y_quantize("v", 1, 0)
-                x_quantize("q", 2, h)
-                for q in range(4):
-                    read_state(1, 2 * h + q // 2, q % 2)
-                    project_v(2, h, q)
-            y_quantize("v", 2, 0)
-            y_quantize("v", 1, 1)
-            last = 2
-            queries(last, 0)
-            y_quantize("v", 2, 1)
-            update_state(0, 0)
-            q_quantize(last, 0)
-            queries(last, 1)
-            for h in range(2):
+                project_q(1, 2 * h + 1)
                 if h == 1:
-                    q_quantize(last, 1)
-                    update_state(0, 1)
-                for s in range(2 * h, 2 * h + 2):
-                    read_state(last, s, 0)
-                    read_state(last, s, 1, "vector" if s % 2 == 0 else "scalar")
-            for n in range(2, 8):
+                    q_quantize(1, 0)
+                read_state(0, 2 * h + 1, 1, "vector" if h == 1 else "scalar")
+
+            last = 2
+            turn_chunk("q", last)
+            scale_pair(last, 0)
+            q_quantize(1, 1)
+            x_quantize("q", last, 0)
+            scale_pair(last, 1)
+            for q in range(4):
+                project_v(last, 0, q)
+                read_state(1, q // 2, q % 2)
+            queries(last, 0)
+            y_quantize("v", 1, 0)
+            x_quantize("q", last, 1)
+            read_state(1, 2, 0)
+            read_state(1, 2, 1, "vector")
+            q_quantize(last, 0)
+            read_state(1, 3, 0)
+            read_state(1, 3, 1, "vector")
+            project_v(last, 1, 0)
+            project_v(last, 1, 1)
+            y_quantize("v", 2, 0)
+            read_pair(last, 0)
+            queries(last, 1)
+            y_quantize("v", 0, 1)
+            y_quantize("v", 1, 1)
+            project_v(last, 1, 2)
+            project_v(last, 1, 3)
+            q_quantize(last, 1)
+            update_state(0, 0)
+            read_pair(last, 1)
+            update_state(0, 1)
+            y_quantize("v", 2, 1)
+            for n in range(2, 7):
                 update_state(n // 4, n % 4)
+            update_state(1, 3, 0, 256)
+            update_state(1, 3, 256, 256)

@@ -36,9 +36,6 @@ def tile_linear_state_step_s7_kernel(
         make_identity(nc, ident[:])
 
         decay_sb = sb.tile([P, PACK], BF16, name="decay_sb")
-        warm = sb.tile([P, 1], F32, name="warm")
-        nc.vector.memset(warm[:], 0.0)
-        nc.scalar.activation(out=warm[:], in_=warm[:], func=ACT.Relu)
         scale_pt = sb.tile([P, PASSES, PACK], F32, name="scale_pt", align_bytes=64)
         ones = sb.tile([P, 1], F32, name="ones")
         nc.vector.memset(ones[:], 1.0)
@@ -82,7 +79,7 @@ def tile_linear_state_step_s7_kernel(
         def load_x(kind, c, h):
             view = xdram[kind][c * CHUNK : (c + 1) * CHUNK, :].rearrange("(m s) d -> m s d", s=PACK)
             if kind == "q":
-                t = sb.tile([P, 2, D], U8, name=f"xqb{c}{h}", tag="xq_bytes", bufs=6, align_bytes=64)
+                t = sb.tile([P, 2, D], U8, name=f"xqb{c}{h}", tag="xq_bytes", bufs=4, align_bytes=64)
             else:
                 t = sb.tile([P, 2, D], BF16, name=f"x{kind}{c}{h}", tag="rows", bufs=10, align_bytes=64)
             rows[kind, c, h] = t
@@ -176,11 +173,43 @@ def tile_linear_state_step_s7_kernel(
                     in_=bank[:].rearrange("p (g u m) -> p g m u", g=PASSES, u=2),
                 )
 
+        plane_banks, planes = {}, {}
+
+        def turn_first_q(h):
+            for g in range(PASSES):
+                for u in range(2):
+                    if h == 0:
+                        plane_banks[g, u] = new_bank(f"tp{g}{u}")
+                    for i in range(2):
+                        first = (i * PASSES + g) * P
+                        place = (2 * h + i) * P
+                        nc.tensor.transpose(
+                            plane_banks[g, u][:, place : place + P],
+                            wide_q[0, h][:, u, :].bitcast(F32)[:, first : first + P], ident[:],
+                        )
+
+        def scale_planes(g, u):
+            if u == 0:
+                planes[g] = sb.tile([P, PACK, CHUNK], BF16, name=f"planes{g}", tag="y_grouped", bufs=8, align_bytes=64)
+            halves = plane_banks[g, u][:].bitcast(BF16).rearrange("p (m e) -> p e m", e=2)
+            for e in range(2):
+                t = 2 * u + e
+                nc.scalar.activation(out=planes[g][:, t, :], in_=halves[:, e, :], func=ACT.Copy, scale=scale_pt[:, g, t : t + 1])
+
+        def interleave_planes(g):
+            x_grouped["q", 0, g] = sb.tile([P, 2048], BF16, name=f"gq0{g}", tag="w_grouped", bufs=4, align_bytes=64)
+            nc.vector.tensor_copy(
+                out=x_grouped["q", 0, g][:].rearrange("p (c i j) -> p c j i", i=4, j=PACK),
+                in_=planes[g][:].rearrange("p j (c i) -> p c j i", i=4),
+            )
+
         def x_quantize(kind, c, h):
-            xcodes[kind, c, h] = new_operand(f"x{kind}{c}{h}", 2 * PASSES * P, "x", 6)
+            xcodes[kind, c, h] = new_operand(f"x{kind}{c}{h}", 2 * PASSES * P, "x", 8)
             quantize(xcodes[kind, c, h], x_grouped[kind, c, h][:])
 
         def x_operand(kind, c, s, g):
+            if (kind, c) == ("q", 0):
+                return columns(xcodes[kind, c, g], s * P, P)
             return columns(xcodes[kind, c, s // 2], ((s % 2) * PASSES + g) * P, P)
 
         def grouped_y(key, first):
@@ -303,12 +332,13 @@ def tile_linear_state_step_s7_kernel(
             load_x(kind, c, 1)
 
         with tc.manual_schedule():
+            load_chunk("q", 0)
+            load_scales()
             load_x("k", 0, 0)
             load_w("wk", 0)
             load_x("k", 0, 1)
             load_w("wk", 1)
             load_x("k", 1, 0)
-            load_chunk("q", 0)
             load_x("k", 1, 1)
             load_w("wv", 0)
             load_chunk("k", 2)
@@ -316,39 +346,48 @@ def tile_linear_state_step_s7_kernel(
             load_chunk("v", 0)
             load_chunk("v", 1)
 
+            widen(0, 0)
+            widen(0, 1)
+            turn_first_q(0)
             turn_pair("k", 0, 0)
+            turn_first_q(1)
+            scale_planes(0, 0)
             w_interleave("wk", 0, 0)
             x_quantize("k", 0, 0)
             w_quantize("wk", 0, 0)
             turn_pair("k", 0, 1)
+            scale_planes(0, 1)
             w_interleave("wk", 1, 0)
             x_quantize("k", 0, 1)
             w_quantize("wk", 1, 0)
+            load_chunk("q", 1)
             load_w("wq", 0)
             load_w("wq", 1)
-            load_scales()
-            load_chunk("q", 1)
             load_w("st", 0)
             load_decay()
 
             turn_pair("k", 1, 0)
-            widen(0, 0)
+            interleave_planes(0)
             x_quantize("k", 1, 0)
-            widen(0, 1)
+            x_quantize("q", 0, 0)
+            scale_planes(1, 0)
             keys(0, 0)
             turn_pair("k", 1, 1)
             w_interleave("wv", 0, 0)
-            x_quantize("k", 1, 1)
             w_interleave("wv", 0, 1)
+            x_quantize("k", 1, 1)
             load_chunk("v", 2)
             load_chunk("q", 2)
             keys(0, 1)
-
-            turn_chunk("k", 2)
+            scale_planes(1, 1)
             w_quantize("wv", 0, 0)
             w_quantize("wv", 0, 1)
-            x_quantize("k", 2, 0)
+            interleave_planes(1)
+
+            turn_chunk("k", 2)
             y_quantize("k", 0, 0)
+            x_quantize("q", 0, 1)
+            x_quantize("k", 2, 0)
             x_quantize("k", 2, 1)
             w_interleave("wv", 1, 0)
             w_interleave("wv", 1, 1)
@@ -356,7 +395,6 @@ def tile_linear_state_step_s7_kernel(
             keys(1, 1)
 
             turn_chunk("v", 0)
-            y_quantize("k", 1, 0)
             w_quantize("wv", 1, 0)
             w_quantize("wv", 1, 1)
             x_quantize("v", 0, 0)
@@ -365,57 +403,48 @@ def tile_linear_state_step_s7_kernel(
             keys(2, 1)
 
             turn_chunk("v", 1)
-            w_interleave("wq", 0, 0)
-            w_interleave("wq", 1, 0)
-            y_quantize("k", 2, 0)
-            x_quantize("v", 1, 0)
-            x_quantize("v", 1, 1)
-            w_quantize("wq", 0, 0)
-            w_quantize("wq", 1, 0)
             widen(1, 0)
             widen(1, 1)
+            x_quantize("v", 1, 0)
+            x_quantize("v", 1, 1)
+            w_interleave("wq", 0, 0)
+            w_interleave("wq", 1, 0)
+            y_quantize("k", 1, 0)
+            w_quantize("wq", 0, 0)
+            w_quantize("wq", 1, 0)
             values(0, 0)
             values(0, 1)
-            w_interleave("st", 0, 0)
-
-            turn_chunk("q", 0)
-            w_interleave("st", 0, 1, "scalar", 0, 256)
-            scale_pair(0, 0)
-            w_quantize("st", 0, 0)
-            x_quantize("q", 0, 0)
-            scale_pair(0, 1)
-            y_quantize("v", 0, 0)
-            x_quantize("q", 0, 1)
-            values(1, 0)
-            values(1, 1)
 
             turn_chunk("q", 1)
-            w_interleave("st", 0, 1, "scalar", 256, 256)
+            w_interleave("st", 0, 1, "scalar", 0, 256)
+            w_interleave("st", 0, 0)
             scale_pair(1, 0)
-            w_quantize("st", 0, 1)
+            w_quantize("st", 0, 0)
             x_quantize("q", 1, 0)
+            values(1, 0)
             queries(0, 0)
-            queries(0, 1)
-            q_quantize(0, 0)
+            w_interleave("st", 0, 1, "scalar", 256, 256)
             scale_pair(1, 1)
-            q_quantize(0, 1)
+            q_quantize(0, 0)
             x_quantize("q", 1, 1)
-
+            values(1, 1)
+            queries(0, 1)
+            w_quantize("st", 0, 1)
             widen(2, 0)
+            q_quantize(0, 1)
             widen(2, 1)
 
             turn_chunk("v", 2)
             x_quantize("v", 2, 0)
             x_quantize("v", 2, 1)
-            for h in range(2):
-                read_state(0, 2 * h, 0)
-                project_q(1, 2 * h)
-                read_state(0, 2 * h, 1)
-                read_state(0, 2 * h + 1, 0)
-                project_q(1, 2 * h + 1)
-                if h == 1:
+            y_quantize("k", 2, 0)
+            y_quantize("v", 0, 0)
+            for s in range(PACK):
+                read_state(0, s, 0)
+                project_q(1, s)
+                if s == 2:
                     q_quantize(1, 0)
-                read_state(0, 2 * h + 1, 1, "vector" if h == 1 else "scalar")
+                read_state(0, s, 1, "vector" if s > 0 else "scalar")
 
             last = 2
             turn_chunk("q", last)
@@ -440,11 +469,11 @@ def tile_linear_state_step_s7_kernel(
             read_pair(last, 0)
             queries(last, 1)
             y_quantize("v", 0, 1)
-            y_quantize("v", 1, 1)
-            project_v(last, 1, 2)
-            project_v(last, 1, 3)
             q_quantize(last, 1)
             update_state(0, 0)
+            project_v(last, 1, 2)
+            project_v(last, 1, 3)
+            y_quantize("v", 1, 1)
             read_pair(last, 1)
             update_state(0, 1)
             y_quantize("v", 2, 1)

@@ -90,6 +90,8 @@ def tile_linear_state_step_s7_kernel(
             width = w.shape[1]
             if width == HALF:
                 t = sb.tile([P, PACK, width], BF16, name=f"{name}raw{g}", tag="w_small", bufs=2, align_bytes=64)
+            elif name == "wv":
+                t = sb.tile([P, PACK, width], BF16, name=f"{name}raw{g}", tag="wide", bufs=2, align_bytes=64)
             else:
                 t = sb.tile([P, PACK, width], BF16, name=f"{name}raw{g}", align_bytes=64)
             nc.sync.dma_start(out=t[:], in_=w[512 * g : 512 * (g + 1), :].rearrange("(p j) n -> p j n", j=PACK))
@@ -121,9 +123,12 @@ def tile_linear_state_step_s7_kernel(
                     raw.rearrange("p j (c i) -> p c j i", i=4),
                 )
 
-        def w_quantize(name, g, h):
-            wcodes[name, g, h] = new_operand(f"{name}c{g}{h}", HALF, f"{name}{g}{h}", 1)
-            quantize(wcodes[name, g, h], w_grouped[name, g, h][:])
+        def w_quantize(name, g, h, first=0, width=HALF):
+            if first == 0:
+                wcodes[name, g, h] = new_operand(f"{name}c{g}{h}", HALF, f"{name}{g}{h}", 1)
+            codes, scales = wcodes[name, g, h]
+            quantize((codes[:, first : first + width], scales[:, first : first + width]),
+                     w_grouped[name, g, h][:, first * PACK : (first + width) * PACK])
 
         def widen(c, h):
             t = sb.tile([P, 2, D], BF16, name=f"xq{c}{h}", tag="xq_rows", bufs=4, align_bytes=64)
@@ -213,7 +218,12 @@ def tile_linear_state_step_s7_kernel(
             return columns(xcodes[kind, c, s // 2], ((s % 2) * PASSES + g) * P, P)
 
         def grouped_y(key, first):
-            if first:
+            kind, c, h = key
+            if kind == "v" and c < 2:
+                if first and h == 0:
+                    both = sb.tile([P, 4096], BF16, name=f"yv{c}", tag="wide", bufs=2, align_bytes=64)
+                    y_grouped["v", c, 0], y_grouped["v", c, 1] = both[:, :2048], both[:, 2048:]
+            elif first:
                 y_grouped[key] = sb.tile(
                     [P, 2048], BF16, name="y" + "".join(str(x) for x in key), tag="y_grouped", bufs=8, align_bytes=64
                 )
@@ -357,9 +367,11 @@ def tile_linear_state_step_s7_kernel(
             w_quantize("wk", 0, 0)
             turn_pair("k", 0, 1)
             scale_planes(0, 1)
-            w_interleave("wk", 1, 0)
+            w_interleave("wk", 1, 0, "vector", 0, 256)
+            w_interleave("wk", 1, 0, "vector", 256, 256)
+            w_quantize("wk", 1, 0, 0, 256)
             x_quantize("k", 0, 1)
-            w_quantize("wk", 1, 0)
+            w_quantize("wk", 1, 0, 256, 256)
             load_chunk("q", 1)
             load_w("wq", 0)
             load_w("wq", 1)
@@ -385,7 +397,6 @@ def tile_linear_state_step_s7_kernel(
             interleave_planes(1)
 
             turn_chunk("k", 2)
-            y_quantize("k", 0, 0)
             x_quantize("q", 0, 1)
             x_quantize("k", 2, 0)
             x_quantize("k", 2, 1)
@@ -409,7 +420,6 @@ def tile_linear_state_step_s7_kernel(
             x_quantize("v", 1, 1)
             w_interleave("wq", 0, 0)
             w_interleave("wq", 1, 0)
-            y_quantize("k", 1, 0)
             w_quantize("wq", 0, 0)
             w_quantize("wq", 1, 0)
             values(0, 0)
@@ -431,6 +441,7 @@ def tile_linear_state_step_s7_kernel(
             queries(0, 1)
             w_quantize("st", 0, 1)
             widen(2, 0)
+            y_quantize("k", 0, 0)
             q_quantize(0, 1)
             widen(2, 1)
 
@@ -443,8 +454,9 @@ def tile_linear_state_step_s7_kernel(
                 read_state(0, s, 0)
                 project_q(1, s)
                 if s == 2:
+                    y_quantize("k", 1, 0)
                     q_quantize(1, 0)
-                read_state(0, s, 1, "vector" if s > 0 else "scalar")
+                read_state(0, s, 1, "vector" if s > 1 else "scalar")
 
             last = 2
             turn_chunk("q", last)

@@ -42,11 +42,11 @@ def tile_linear_state_step_s7_kernel(
 
         xdram = {"k": xk, "v": xv, "q": xq_bytes}
         wdram = {"wk": wk, "wq": wq, "wv": wv, "st": state}
-        rows, wide_q, wraw = {}, {}, {}
+        rows, sorted_x, wraw = {}, {}, {}
         x_grouped, x_banks, xcodes = {}, {}, {}
         w_grouped, wcodes = {}, {}
         y_grouped, ycodes = {}, {}
-        out_rows = {}
+        out_rows, update_banks = {}, {}
 
         def new_bank(name):
             return ps.tile([P, 512], F32, name=name, tag="bank")
@@ -103,11 +103,11 @@ def tile_linear_state_step_s7_kernel(
         def load_decay():
             nc.sync.dma_start(out=decay_sb[:], in_=decay.rearrange("(p i) -> p i", i=PACK))
 
-        def w_interleave(name, g, h, engine="vector", first=0, width=HALF):
+        def w_interleave(name, g, h, engine="vector", first=0, width=HALF, tag="w_grouped", bufs=3):
             raw = wraw[name, g][:, :, h * HALF + first : h * HALF + first + width]
             if first == 0:
                 w_grouped[name, g, h] = sb.tile(
-                    [P, HALF * PACK], BF16, name=f"{name}g{g}{h}", tag="w_grouped", bufs=4, align_bytes=64
+                    [P, HALF * PACK], BF16, name=f"{name}g{g}{h}", tag=tag, bufs=bufs, align_bytes=64
                 )
             grouped = w_grouped[name, g, h][:, first * PACK : (first + width) * PACK]
             if name == "wq":
@@ -123,6 +123,15 @@ def tile_linear_state_step_s7_kernel(
                     raw.rearrange("p j (c i) -> p c j i", i=4),
                 )
 
+        def w_interleave_gpsimd(name, g, width):
+            both = sb.tile([P, 2 * HALF * PACK], BF16, name=f"{name}g{g}", tag="handover", align_bytes=64)
+            w_grouped[name, g, 0], w_grouped[name, g, 1] = both[:, : HALF * PACK], both[:, HALF * PACK :]
+            nc.gpsimd.tensor_scalar(
+                out=both[:, : width * PACK].rearrange("p (c j) -> p c j", j=PACK),
+                in0=wraw[name, g][:, :, :width].rearrange("p j c -> p c j"),
+                scalar1=1.0, scalar2=0.0, op0=ALU.mult, op1=ALU.add,
+            )
+
         def w_quantize(name, g, h, first=0, width=HALF):
             if first == 0:
                 wcodes[name, g, h] = new_operand(f"{name}c{g}{h}", HALF, f"{name}{g}{h}", 1)
@@ -131,8 +140,8 @@ def tile_linear_state_step_s7_kernel(
                      w_grouped[name, g, h][:, first * PACK : (first + width) * PACK])
 
         def widen(c, h):
-            t = sb.tile([P, 2, D], BF16, name=f"xq{c}{h}", tag="xq_rows", bufs=4, align_bytes=64)
-            wide_q[c, h] = t
+            t = sb.tile([P, 2, D], BF16, name=f"xq{c}{h}", tag="sorted", bufs=4, align_bytes=64)
+            sorted_x["q", c, h] = t
             nc.vector.tensor_scalar(
                 out=t[:].rearrange("p u (m e) -> p m u e", e=2),
                 in0=rows["q", c, h][:].bitcast(FP8).rearrange("p s (m u e) -> p (s m) u e", u=2, e=2),
@@ -145,13 +154,12 @@ def tile_linear_state_step_s7_kernel(
             x_banks[kind, c, s] = bank
             for g in range(PASSES):
                 for u in range(2):
-                    if kind == "q":
+                    if (kind, c, h) in sorted_x:
                         first = (i * PASSES + g) * P
-                        chosen = wide_q[c, h][:, u, :].bitcast(F32)[:, first : first + P]
-                        place = (u * PASSES + g) * P
+                        chosen = sorted_x[kind, c, h][:, u, :].bitcast(F32)[:, first : first + P]
                     else:
                         chosen = rows[kind, c, h][:, i, :].bitcast(F32)[:, 256 * g + u : 256 * (g + 1) : 2]
-                        place = (g * 2 + u) * P
+                    place = (u * PASSES + g) * P
                     nc.tensor.transpose(bank[:, place : place + P], chosen, ident[:])
             if kind != "q":
                 empty_turned(kind, c, s)
@@ -175,46 +183,14 @@ def tile_linear_state_step_s7_kernel(
             else:
                 nc.scalar.copy(
                     out=part.bitcast(F32).rearrange("p (g m u) -> p g m u", g=PASSES, u=2),
-                    in_=bank[:].rearrange("p (g u m) -> p g m u", g=PASSES, u=2),
+                    in_=bank[:].rearrange("p (u g m) -> p g m u", g=PASSES, u=2),
                 )
-
-        plane_banks, planes = {}, {}
-
-        def turn_first_q(h):
-            for g in range(PASSES):
-                for u in range(2):
-                    if h == 0:
-                        plane_banks[g, u] = new_bank(f"tp{g}{u}")
-                    for i in range(2):
-                        first = (i * PASSES + g) * P
-                        place = (2 * h + i) * P
-                        nc.tensor.transpose(
-                            plane_banks[g, u][:, place : place + P],
-                            wide_q[0, h][:, u, :].bitcast(F32)[:, first : first + P], ident[:],
-                        )
-
-        def scale_planes(g, u):
-            if u == 0:
-                planes[g] = sb.tile([P, PACK, CHUNK], BF16, name=f"planes{g}", tag="y_grouped", bufs=8, align_bytes=64)
-            halves = plane_banks[g, u][:].bitcast(BF16).rearrange("p (m e) -> p e m", e=2)
-            for e in range(2):
-                t = 2 * u + e
-                nc.scalar.activation(out=planes[g][:, t, :], in_=halves[:, e, :], func=ACT.Copy, scale=scale_pt[:, g, t : t + 1])
-
-        def interleave_planes(g):
-            x_grouped["q", 0, g] = sb.tile([P, 2048], BF16, name=f"gq0{g}", tag="w_grouped", bufs=4, align_bytes=64)
-            nc.vector.tensor_copy(
-                out=x_grouped["q", 0, g][:].rearrange("p (c i j) -> p c j i", i=4, j=PACK),
-                in_=planes[g][:].rearrange("p j (c i) -> p c j i", i=4),
-            )
 
         def x_quantize(kind, c, h):
             xcodes[kind, c, h] = new_operand(f"x{kind}{c}{h}", 2 * PASSES * P, "x", 8)
             quantize(xcodes[kind, c, h], x_grouped[kind, c, h][:])
 
         def x_operand(kind, c, s, g):
-            if (kind, c) == ("q", 0):
-                return columns(xcodes[kind, c, g], s * P, P)
             return columns(xcodes[kind, c, s // 2], ((s % 2) * PASSES + g) * P, P)
 
         def grouped_y(key, first):
@@ -296,6 +272,10 @@ def tile_linear_state_step_s7_kernel(
             for c in range(CHUNKS):
                 multiply(bank[:, :width], columns(ycodes["k", c, 0], i * P, P), columns(ycodes["v", c, h], first, width),
                          c == 0, c == CHUNKS - 1)
+            update_banks[h, i, first] = bank
+
+        def finish_update(h, i, first=0, width=HALF):
+            bank = update_banks[h, i, first]
             new_sb = sb.tile([P, width], F32, name=f"n{h}{i}{first}", tag="rows", bufs=10, align_bytes=64)
             cut = slice(h * HALF + first, h * HALF + first + width)
             nc.vector.scalar_tensor_tensor(
@@ -324,9 +304,9 @@ def tile_linear_state_step_s7_kernel(
             for q in range(4):
                 project_v(c, h, q)
 
-        def weight(name, g, h):
-            w_interleave(name, g, h)
-            w_quantize(name, g, h)
+        def update(h, i, first=0, width=HALF):
+            update_state(h, i, first, width)
+            finish_update(h, i, first, width)
 
         def read_pair(c, h, second="vector"):
             for s in (2 * h, 2 * h + 1):
@@ -349,25 +329,22 @@ def tile_linear_state_step_s7_kernel(
             load_x("k", 0, 1)
             load_w("wk", 1)
             load_x("k", 1, 0)
-            load_x("k", 1, 1)
             load_w("wv", 0)
+            load_x("k", 1, 1)
             load_chunk("k", 2)
             load_w("wv", 1)
             load_chunk("v", 0)
             load_chunk("v", 1)
-
             widen(0, 0)
             widen(0, 1)
-            turn_first_q(0)
+            turn_pair("q", 0, 0)
             turn_pair("k", 0, 0)
-            turn_first_q(1)
-            scale_planes(0, 0)
+            turn_pair("q", 0, 1)
             w_interleave("wk", 0, 0)
             x_quantize("k", 0, 0)
             w_quantize("wk", 0, 0)
             turn_pair("k", 0, 1)
-            scale_planes(0, 1)
-            w_interleave("wk", 1, 0, "vector", 0, 256)
+            w_interleave("wk", 1, 0, "vector", 0, 256, tag="handover", bufs=1)
             w_interleave("wk", 1, 0, "vector", 256, 256)
             w_quantize("wk", 1, 0, 0, 256)
             x_quantize("k", 0, 1)
@@ -377,99 +354,91 @@ def tile_linear_state_step_s7_kernel(
             load_w("wq", 1)
             load_w("st", 0)
             load_decay()
-
+            w_interleave_gpsimd("wv", 0, 768)
             turn_pair("k", 1, 0)
-            interleave_planes(0)
-            x_quantize("k", 1, 0)
-            x_quantize("q", 0, 0)
-            scale_planes(1, 0)
             keys(0, 0)
+            scale_pair(0, 0)
+            w_interleave("wv", 0, 1, "scalar", 256, 256)
             turn_pair("k", 1, 1)
-            w_interleave("wv", 0, 0)
-            w_interleave("wv", 0, 1)
+            scale_pair(0, 1)
+            x_quantize("k", 1, 0)
             x_quantize("k", 1, 1)
             load_chunk("v", 2)
             load_chunk("q", 2)
             keys(0, 1)
-            scale_planes(1, 1)
+            x_quantize("q", 0, 0)
+            x_quantize("q", 0, 1)
             w_quantize("wv", 0, 0)
             w_quantize("wv", 0, 1)
-            interleave_planes(1)
-
             turn_chunk("k", 2)
-            x_quantize("q", 0, 1)
+            w_interleave("wv", 1, 0)
             x_quantize("k", 2, 0)
             x_quantize("k", 2, 1)
-            w_interleave("wv", 1, 0)
-            w_interleave("wv", 1, 1)
+            w_quantize("wv", 1, 0)
+            w_interleave("wv", 1, 1, "scalar", 0, 256)
             keys(1, 0)
             keys(1, 1)
-
+            w_interleave("wv", 1, 1, "vector", 256, 256)
             turn_chunk("v", 0)
-            w_quantize("wv", 1, 0)
-            w_quantize("wv", 1, 1)
+            widen(1, 0)
             x_quantize("v", 0, 0)
             x_quantize("v", 0, 1)
+            w_quantize("wv", 1, 1)
             keys(2, 0)
             keys(2, 1)
-
             turn_chunk("v", 1)
-            widen(1, 0)
             widen(1, 1)
+            w_interleave("wq", 0, 0)
             x_quantize("v", 1, 0)
             x_quantize("v", 1, 1)
-            w_interleave("wq", 0, 0)
-            w_interleave("wq", 1, 0)
+            w_interleave("wq", 1, 0, tag="handover", bufs=1)
             w_quantize("wq", 0, 0)
+            y_quantize("k", 0, 0)
+            y_quantize("k", 1, 0)
             w_quantize("wq", 1, 0)
             values(0, 0)
             values(0, 1)
-
             turn_chunk("q", 1)
-            w_interleave("st", 0, 1, "scalar", 0, 256)
-            w_interleave("st", 0, 0)
+            w_interleave_gpsimd("st", 0, 768)
             scale_pair(1, 0)
-            w_quantize("st", 0, 0)
+            scale_pair(1, 1)
+            w_interleave("st", 0, 1, "scalar", 256, 256)
             x_quantize("q", 1, 0)
+            w_quantize("st", 0, 0)
             values(1, 0)
             queries(0, 0)
-            w_interleave("st", 0, 1, "scalar", 256, 256)
-            scale_pair(1, 1)
-            q_quantize(0, 0)
             x_quantize("q", 1, 1)
+            w_quantize("st", 0, 1)
+            q_quantize(0, 0)
+            widen(2, 0)
             values(1, 1)
             queries(0, 1)
-            w_quantize("st", 0, 1)
-            widen(2, 0)
-            y_quantize("k", 0, 0)
-            q_quantize(0, 1)
             widen(2, 1)
-
+            q_quantize(0, 1)
             turn_chunk("v", 2)
+            y_quantize("k", 2, 0)
             x_quantize("v", 2, 0)
             x_quantize("v", 2, 1)
-            y_quantize("k", 2, 0)
-            y_quantize("v", 0, 0)
             for s in range(PACK):
                 read_state(0, s, 0)
                 project_q(1, s)
                 if s == 2:
-                    y_quantize("k", 1, 0)
                     q_quantize(1, 0)
-                read_state(0, s, 1, "vector" if s > 1 else "scalar")
+                read_state(0, s, 1, "vector")
 
             last = 2
             turn_chunk("q", last)
             scale_pair(last, 0)
             q_quantize(1, 1)
             x_quantize("q", last, 0)
-            scale_pair(last, 1)
             for q in range(4):
                 project_v(last, 0, q)
                 read_state(1, q // 2, q % 2)
+            scale_pair(last, 1)
             queries(last, 0)
-            y_quantize("v", 1, 0)
+            y_quantize("v", 0, 0)
             x_quantize("q", last, 1)
+            y_quantize("v", 1, 0)
             read_state(1, 2, 0)
             read_state(1, 2, 1, "vector")
             q_quantize(last, 0)
@@ -482,14 +451,14 @@ def tile_linear_state_step_s7_kernel(
             queries(last, 1)
             y_quantize("v", 0, 1)
             q_quantize(last, 1)
-            update_state(0, 0)
+            update(0, 0)
             project_v(last, 1, 2)
             project_v(last, 1, 3)
             y_quantize("v", 1, 1)
             read_pair(last, 1)
-            update_state(0, 1)
+            update(0, 1)
             y_quantize("v", 2, 1)
             for n in range(2, 7):
-                update_state(n // 4, n % 4)
-            update_state(1, 3, 0, 256)
-            update_state(1, 3, 256, 256)
+                update(n // 4, n % 4)
+            update(1, 3, 0, 256)
+            update(1, 3, 256, 256)

@@ -148,6 +148,14 @@ def tile_linear_state_step_s7_kernel(
                 scalar1=ones[:, 0:1], scalar2=None, op0=ALU.mult,
             )
 
+        def sort_words(kind, c, h):
+            t = sb.tile([P, 2, D], BF16, name=f"x{kind}s{c}{h}", tag="sorted", bufs=4, align_bytes=64)
+            sorted_x[kind, c, h] = t
+            words = rows[kind, c, h][:].rearrange("p s d -> p (s d)").bitcast(F32)
+            nc.vector.tensor_copy(
+                out=t[:].bitcast(F32).rearrange("p u m -> p m u"), in_=words.rearrange("p (m u) -> p m u", u=2)
+            )
+
         def turn(kind, c, s):
             h, i = s // 2, s % 2
             bank = new_bank(f"t{kind}{c}{s}")
@@ -304,6 +312,10 @@ def tile_linear_state_step_s7_kernel(
             for q in range(4):
                 project_v(c, h, q)
 
+        def sort_chunk(kind, c):
+            sort_words(kind, c, 0)
+            sort_words(kind, c, 1)
+
         def update(h, i, first=0, width=HALF):
             update_state(h, i, first, width)
             finish_update(h, i, first, width)
@@ -375,48 +387,46 @@ def tile_linear_state_step_s7_kernel(
             x_quantize("k", 2, 0)
             x_quantize("k", 2, 1)
             w_quantize("wv", 1, 0)
-            w_interleave("wv", 1, 1, "scalar", 0, 256)
             keys(1, 0)
             keys(1, 1)
-            w_interleave("wv", 1, 1, "vector", 256, 256)
             turn_chunk("v", 0)
-            widen(1, 0)
+            sort_chunk("v", 1)
             x_quantize("v", 0, 0)
+            w_interleave("wv", 1, 1)
             x_quantize("v", 0, 1)
             w_quantize("wv", 1, 1)
             keys(2, 0)
             keys(2, 1)
             turn_chunk("v", 1)
+            widen(1, 0)
             widen(1, 1)
-            w_interleave("wq", 0, 0)
             x_quantize("v", 1, 0)
             x_quantize("v", 1, 1)
+            w_interleave("wq", 0, 0)
             w_interleave("wq", 1, 0, tag="handover", bufs=1)
             w_quantize("wq", 0, 0)
-            y_quantize("k", 0, 0)
-            y_quantize("k", 1, 0)
             w_quantize("wq", 1, 0)
             values(0, 0)
             values(0, 1)
+            values(1, 0)
             turn_chunk("q", 1)
             w_interleave_gpsimd("st", 0, 768)
+            w_interleave("st", 0, 1, "scalar", 256, 256)
+            values(1, 1)
             scale_pair(1, 0)
             scale_pair(1, 1)
-            w_interleave("st", 0, 1, "scalar", 256, 256)
-            x_quantize("q", 1, 0)
-            w_quantize("st", 0, 0)
-            values(1, 0)
+            sort_chunk("v", 2)
             queries(0, 0)
-            x_quantize("q", 1, 1)
-            w_quantize("st", 0, 1)
-            q_quantize(0, 0)
-            widen(2, 0)
-            values(1, 1)
             queries(0, 1)
-            widen(2, 1)
+            w_quantize("st", 0, 0)
+            q_quantize(0, 0)
+            x_quantize("q", 1, 0)
+            w_quantize("st", 0, 1)
+            x_quantize("q", 1, 1)
             q_quantize(0, 1)
             turn_chunk("v", 2)
-            y_quantize("k", 2, 0)
+            widen(2, 0)
+            widen(2, 1)
             x_quantize("v", 2, 0)
             x_quantize("v", 2, 1)
             for s in range(PACK):
@@ -424,7 +434,7 @@ def tile_linear_state_step_s7_kernel(
                 project_q(1, s)
                 if s == 2:
                     q_quantize(1, 0)
-                read_state(0, s, 1, "vector")
+                read_state(0, s, 1, "vector" if s == 2 else "scalar")
 
             last = 2
             turn_chunk("q", last)
@@ -436,26 +446,32 @@ def tile_linear_state_step_s7_kernel(
                 read_state(1, q // 2, q % 2)
             scale_pair(last, 1)
             queries(last, 0)
-            y_quantize("v", 0, 0)
+            y_quantize("k", 0, 0)
             x_quantize("q", last, 1)
-            y_quantize("v", 1, 0)
             read_state(1, 2, 0)
-            read_state(1, 2, 1, "vector")
+            read_state(1, 2, 1)
+            y_quantize("k", 1, 0)
             q_quantize(last, 0)
             read_state(1, 3, 0)
             read_state(1, 3, 1, "vector")
+            queries(last, 1)
+            y_quantize("k", 2, 0)
+            read_pair(last, 0)
+            q_quantize(last, 1)
             project_v(last, 1, 0)
             project_v(last, 1, 1)
+            y_quantize("v", 0, 0)
+            y_quantize("v", 1, 0)
             y_quantize("v", 2, 0)
-            read_pair(last, 0)
-            queries(last, 1)
-            y_quantize("v", 0, 1)
-            q_quantize(last, 1)
-            update(0, 0)
+            read_state(last, 2, 0)
+            read_state(last, 2, 1, "vector")
+            read_state(last, 3, 0)
+            read_state(last, 3, 1)
             project_v(last, 1, 2)
             project_v(last, 1, 3)
+            y_quantize("v", 0, 1)
             y_quantize("v", 1, 1)
-            read_pair(last, 1)
+            update(0, 0)
             update(0, 1)
             y_quantize("v", 2, 1)
             for n in range(2, 7):

@@ -30,7 +30,7 @@ def tile_linear_state_step_s7_kernel(
 
     with ExitStack() as ctx:
         sb = ctx.enter_context(tc.tile_pool(name="sb", bufs=1))
-        ps = ctx.enter_context(tc.psum_pool(name="ps", bufs=8))
+        ps = ctx.enter_context(tc.psum_pool(name="ps", bufs=1))
 
         ident = sb.tile([P, P], F32, name="ident", align_bytes=64)
         make_identity(nc, ident[:])
@@ -46,10 +46,17 @@ def tile_linear_state_step_s7_kernel(
         x_grouped, x_banks, xcodes = {}, {}, {}
         w_grouped, wcodes = {}, {}
         y_grouped, ycodes = {}, {}
-        out_rows, update_banks = {}, {}
+        out_rows, update_banks, v_banks = {}, {}, {}
+
+        free_banks = list(range(8))
+        bank_of = {}
 
         def new_bank(name):
-            return ps.tile([P, 512], F32, name=name, tag="bank")
+            bank_of[name] = free_banks.pop(0)
+            return ps.tile([P, 512], F32, name=name, tag=f"bank{bank_of[name]}")
+
+        def release_bank(name):
+            free_banks.append(bank_of[name])
 
         def new_operand(name, words, tag, bufs):
             codes = sb.tile([P, words], U32, name=f"{name}_codes", tag=f"{tag}_codes", bufs=bufs, align_bytes=64)
@@ -103,9 +110,9 @@ def tile_linear_state_step_s7_kernel(
         def load_decay():
             nc.sync.dma_start(out=decay_sb[:], in_=decay.rearrange("(p i) -> p i", i=PACK))
 
-        def w_interleave(name, g, h, engine="vector", first=0, width=HALF, tag="w_grouped", bufs=3):
+        def w_interleave(name, g, h, engine="vector", first=0, width=HALF, tag="w_grouped", bufs=3, staged=False):
             raw = wraw[name, g][:, :, h * HALF + first : h * HALF + first + width]
-            if first == 0:
+            if first == 0 and not staged:
                 w_grouped[name, g, h] = sb.tile(
                     [P, HALF * PACK], BF16, name=f"{name}g{g}{h}", tag=tag, bufs=bufs, align_bytes=64
                 )
@@ -147,6 +154,11 @@ def tile_linear_state_step_s7_kernel(
                 in0=rows["q", c, h][:].bitcast(FP8).rearrange("p s (m u e) -> p (s m) u e", u=2, e=2),
                 scalar1=ones[:, 0:1], scalar2=None, op0=ALU.mult,
             )
+
+        def widen_plain(h, engine):
+            t = sb.tile([P, 2, D], BF16, name=f"xq0{h}", tag="sorted", bufs=4, align_bytes=64)
+            copy_on(engine, t[:].rearrange("p s d -> p (s d)"), rows["q", 0, h][:].rearrange("p s d -> p (s d)").bitcast(FP8))
+            rows["q", 0, h] = t
 
         def sort_words(kind, c, h):
             t = sb.tile([P, 2, D], BF16, name=f"x{kind}s{c}{h}", tag="sorted", bufs=4, align_bytes=64)
@@ -193,6 +205,7 @@ def tile_linear_state_step_s7_kernel(
                     out=part.bitcast(F32).rearrange("p (g m u) -> p g m u", g=PASSES, u=2),
                     in_=bank[:].rearrange("p (u g m) -> p g m u", g=PASSES, u=2),
                 )
+            release_bank(f"t{kind}{c}{s}")
 
         def x_quantize(kind, c, h):
             xcodes[kind, c, h] = new_operand(f"x{kind}{c}{h}", 2 * PASSES * P, "x", 8)
@@ -225,19 +238,28 @@ def tile_linear_state_step_s7_kernel(
                 in_=bank[:].rearrange("p (s m i) -> p i m s", s=PACK, i=PACK),
                 func=ACT.Relu,
             )
+            release_bank(f"kb{c}{q}")
 
-        def project_v(c, h, q, engine="scalar"):
-            grouped = grouped_y(("v", c, h), q == 0)
-            bank = new_bank(f"vb{c}{h}{q}")
+        def multiply_v(c, h, q):
+            bank = v_banks[c, h, q] = new_bank(f"vb{c}{h}{q}")
             for s in range(PACK):
                 for g in range(PASSES):
                     multiply(bank[:, s * P : (s + 1) * P], x_operand("v", c, s, g),
                              columns(wcodes["wv", g, h], q * P, P), g == 0, g == PASSES - 1)
+
+        def project_v(c, h, q):
+            multiply_v(c, h, q)
+            empty_v(c, h, q)
+
+        def empty_v(c, h, q):
+            grouped = grouped_y(("v", c, h), q == 0)
+            bank = v_banks[c, h, q]
             copy_on(
-                engine,
+                "scalar",
                 grouped[:].rearrange("p (n s) -> p n s", s=PACK)[:, q * P : (q + 1) * P, :],
                 bank[:].rearrange("p (s n) -> p n s", s=PACK),
             )
+            release_bank(f"vb{c}{h}{q}")
 
         def y_quantize(kind, c, h):
             ycodes[kind, c, h] = new_operand(f"{kind}{c}{h}", HALF, kind, 3 if kind == "k" else 6)
@@ -255,6 +277,7 @@ def tile_linear_state_step_s7_kernel(
                 grouped[:, s * 512 : (s + 1) * 512].rearrange("p (m j) -> p m j", j=PACK),
                 bank[:].rearrange("p (j m) -> p m j", j=PACK),
             )
+            release_bank(f"qb{c}{s}")
 
         def q_quantize(c, h):
             ycodes["q", c, h] = new_operand(f"q{c}{h}", 2 * P, "q", 4)
@@ -270,6 +293,7 @@ def tile_linear_state_step_s7_kernel(
             multiply(bank[:], columns(ycodes["q", c, s // 2], (s % 2) * P, P), columns(wcodes["st", 0, h], 0, HALF),
                      True, True)
             copy_on(engine, o_sb[:, h * HALF : (h + 1) * HALF], bank[:])
+            release_bank(f"ob{c}{s}{h}")
             if h == 1:
                 nc.sync.dma_start(out=out_view[c, :, s, :], in_=o_sb[:])
 
@@ -290,6 +314,7 @@ def tile_linear_state_step_s7_kernel(
                 out=new_sb[:], in0=wraw["st", 0][:, i, cut], scalar=decay_sb[:, i : i + 1], in1=bank[:, :width],
                 op0=ALU.mult, op1=ALU.add,
             )
+            release_bank(f"ub{h}{i}{first}")
             nc.sync.dma_start(out=new_view[:, i, cut], in_=new_sb[:])
 
         def turn_pair(kind, c, h):
@@ -347,38 +372,41 @@ def tile_linear_state_step_s7_kernel(
             load_w("wv", 1)
             load_chunk("v", 0)
             load_chunk("v", 1)
-            widen(0, 0)
-            widen(0, 1)
+            widen_plain(0, "vector")
+            widen_plain(1, "vector")
             turn_pair("q", 0, 0)
+            scale_pair(0, 0)
             turn_pair("k", 0, 0)
             turn_pair("q", 0, 1)
-            w_interleave("wk", 0, 0)
-            x_quantize("k", 0, 0)
-            w_quantize("wk", 0, 0)
+            w_interleave("wk", 0, 0, "vector", 0, 256)
+            w_interleave("wk", 0, 0, "scalar", 256, 256)
             turn_pair("k", 0, 1)
+            x_quantize("k", 0, 0)
             w_interleave("wk", 1, 0, "vector", 0, 256, tag="handover", bufs=1)
-            w_interleave("wk", 1, 0, "vector", 256, 256)
+            w_quantize("wk", 0, 0)
             w_quantize("wk", 1, 0, 0, 256)
             x_quantize("k", 0, 1)
+            w_interleave("wk", 1, 0, "vector", 256, 256)
             w_quantize("wk", 1, 0, 256, 256)
             load_chunk("q", 1)
             load_w("wq", 0)
             load_w("wq", 1)
             load_w("st", 0)
             load_decay()
-            w_interleave_gpsimd("wv", 0, 768)
+            w_interleave_gpsimd("wv", 0, 384)
             turn_pair("k", 1, 0)
             keys(0, 0)
-            scale_pair(0, 0)
             w_interleave("wv", 0, 1, "scalar", 256, 256)
             turn_pair("k", 1, 1)
             scale_pair(0, 1)
             x_quantize("k", 1, 0)
+            x_quantize("q", 0, 0)
+            w_interleave("wv", 0, 0, "vector", 384, 128)
+            w_interleave("wv", 0, 1, "vector", 0, 256, staged=True)
             x_quantize("k", 1, 1)
             load_chunk("v", 2)
             load_chunk("q", 2)
             keys(0, 1)
-            x_quantize("q", 0, 0)
             x_quantize("q", 0, 1)
             w_quantize("wv", 0, 0)
             w_quantize("wv", 0, 1)
@@ -392,35 +420,35 @@ def tile_linear_state_step_s7_kernel(
             turn_chunk("v", 0)
             sort_chunk("v", 1)
             x_quantize("v", 0, 0)
-            w_interleave("wv", 1, 1)
             x_quantize("v", 0, 1)
-            w_quantize("wv", 1, 1)
+            w_interleave("wv", 1, 1)
             keys(2, 0)
             keys(2, 1)
             turn_chunk("v", 1)
             widen(1, 0)
+            w_quantize("wv", 1, 1)
             widen(1, 1)
             x_quantize("v", 1, 0)
             x_quantize("v", 1, 1)
             w_interleave("wq", 0, 0)
             w_interleave("wq", 1, 0, tag="handover", bufs=1)
+            sort_chunk("v", 2)
             w_quantize("wq", 0, 0)
             w_quantize("wq", 1, 0)
             values(0, 0)
             values(0, 1)
             values(1, 0)
             turn_chunk("q", 1)
-            w_interleave_gpsimd("st", 0, 768)
-            w_interleave("st", 0, 1, "scalar", 256, 256)
+            w_interleave_gpsimd("st", 0, 704)
             values(1, 1)
             scale_pair(1, 0)
             scale_pair(1, 1)
-            sort_chunk("v", 2)
             queries(0, 0)
             queries(0, 1)
-            w_quantize("st", 0, 0)
-            q_quantize(0, 0)
             x_quantize("q", 1, 0)
+            w_interleave("st", 0, 1, "vector", 192, 320)
+            q_quantize(0, 0)
+            w_quantize("st", 0, 0)
             w_quantize("st", 0, 1)
             x_quantize("q", 1, 1)
             q_quantize(0, 1)
@@ -430,11 +458,11 @@ def tile_linear_state_step_s7_kernel(
             x_quantize("v", 2, 0)
             x_quantize("v", 2, 1)
             for s in range(PACK):
-                read_state(0, s, 0)
                 project_q(1, s)
+                read_state(0, s, 0)
                 if s == 2:
                     q_quantize(1, 0)
-                read_state(0, s, 1, "vector" if s == 2 else "scalar")
+                read_state(0, s, 1, "scalar")
 
             last = 2
             turn_chunk("q", last)
@@ -446,25 +474,28 @@ def tile_linear_state_step_s7_kernel(
                 read_state(1, q // 2, q % 2)
             scale_pair(last, 1)
             queries(last, 0)
-            y_quantize("k", 0, 0)
             x_quantize("q", last, 1)
+            y_quantize("k", 0, 0)
             read_state(1, 2, 0)
-            read_state(1, 2, 1)
             y_quantize("k", 1, 0)
+            read_state(1, 2, 1, "vector")
             q_quantize(last, 0)
             read_state(1, 3, 0)
             read_state(1, 3, 1, "vector")
             queries(last, 1)
             y_quantize("k", 2, 0)
-            read_pair(last, 0)
+            read_state(last, 0, 0)
+            read_state(last, 0, 1, "vector")
             q_quantize(last, 1)
+            read_state(last, 1, 0)
+            read_state(last, 1, 1, "vector")
             project_v(last, 1, 0)
             project_v(last, 1, 1)
             y_quantize("v", 0, 0)
             y_quantize("v", 1, 0)
             y_quantize("v", 2, 0)
             read_state(last, 2, 0)
-            read_state(last, 2, 1, "vector")
+            read_state(last, 2, 1)
             read_state(last, 3, 0)
             read_state(last, 3, 1)
             project_v(last, 1, 2)

@@ -17,10 +17,13 @@ ALU = mybir.AluOpType
 
 P = 128
 PACK = 4
-CHUNK = 512
+CHUNK = P * PACK
 CHUNKS = T // CHUNK
 PASSES = D // 512
 HALF = 512
+STAGE = 2048
+STAGES = 37
+XBUFS = 11
 
 
 def tile_linear_state_step_s7_kernel(
@@ -34,42 +37,43 @@ def tile_linear_state_step_s7_kernel(
 
         ident = sb.tile([P, P], F32, name="ident", align_bytes=64)
         make_identity(nc, ident[:])
-
         decay_sb = sb.tile([P, PACK], BF16, name="decay_sb")
         scale_pt = sb.tile([P, PASSES, PACK], F32, name="scale_pt", align_bytes=64)
         ones = sb.tile([P, 1], F32, name="ones")
         nc.vector.memset(ones[:], 1.0)
 
-        xdram = {"k": xk, "v": xv, "q": xq_bytes}
-        wdram = {"wk": wk, "wq": wq, "wv": wv, "st": state}
-        rows, sorted_x, wraw = {}, {}, {}
-        x_grouped, x_banks, xcodes = {}, {}, {}
-        w_grouped, wcodes = {}, {}
-        y_grouped, ycodes = {}, {}
-        out_rows, update_banks, v_banks = {}, {}, {}
+        free_banks, free_stages = list(range(8)), list(range(STAGES))
+        held, place, operands = {}, {}, {}
 
-        free_banks = list(range(8))
-        bank_of = {}
+        def take_bank(key):
+            place[key] = free_banks.pop(0)
+            held[key] = ps.tile([P, 512], F32, name="".join(map(str, key)), tag=f"bank{place[key]}")
+            return held[key]
 
-        def new_bank(name):
-            bank_of[name] = free_banks.pop(0)
-            return ps.tile([P, 512], F32, name=name, tag=f"bank{bank_of[name]}")
+        def give_bank(key):
+            free_banks.append(place[key])
 
-        def release_bank(name):
-            free_banks.append(bank_of[name])
+        def take_stage(key, newest=False):
+            place[key] = free_stages.pop(-1 if newest else 0)
+            held[key] = sb.tile([P, STAGE], BF16, name="".join(map(str, key)), tag=f"stage{place[key]}", align_bytes=64)
+            return held[key]
 
-        def new_operand(name, words, tag, bufs):
+        def give_stage(key):
+            free_stages.append(place[key])
+
+        def new_operand(key, words, tag, bufs):
+            name = "".join(map(str, key))
             codes = sb.tile([P, words], U32, name=f"{name}_codes", tag=f"{tag}_codes", bufs=bufs, align_bytes=64)
             scales = sb.tile([P, words], U8, name=f"{name}_scales", tag=f"{tag}_scales", bufs=bufs, align_bytes=64)
-            return codes, scales
+            operands[key] = codes, scales
 
-        def quantize(operand, grouped):
-            codes, scales = operand
-            nc.vector.quantize_mx(out=codes[:].bitcast(FP8X4), scales=scales[:], in_=grouped)
-
-        def columns(operand, first, width):
-            codes, scales = operand
+        def columns(key, first, width):
+            codes, scales = operands[key]
             return codes[:, first : first + width].bitcast(FP8X4), scales[:, first : first + width]
+
+        def quantize(key, grouped, first, width):
+            codes, scales = columns(key, first, width)
+            nc.vector.quantize_mx(out=codes, scales=scales, in_=grouped[:, first * PACK : (first + width) * PACK])
 
         def multiply(out, stationary, moving, start, stop):
             nc.tensor.matmul_mx(
@@ -83,26 +87,25 @@ def tile_linear_state_step_s7_kernel(
             else:
                 nc.scalar.copy(out=out, in_=in_)
 
-        def load_x(kind, c, h):
-            view = xdram[kind][c * CHUNK : (c + 1) * CHUNK, :].rearrange("(m s) d -> m s d", s=PACK)
-            if kind == "q":
-                t = sb.tile([P, 2, D], U8, name=f"xqb{c}{h}", tag="xq_bytes", bufs=4, align_bytes=64)
-            else:
-                t = sb.tile([P, 2, D], BF16, name=f"x{kind}{c}{h}", tag="rows", bufs=10, align_bytes=64)
-            rows[kind, c, h] = t
-            nc.sync.dma_start(out=t[:], in_=view[:, 2 * h : 2 * h + 2, :])
+        x_dram = {"k": xk, "v": xv, "q": xq_bytes}
+        w_dram = {"wk": wk, "wq": wq, "wv": wv, "st": state}
 
-        def load_w(name, g):
-            w = wdram[name]
-            width = w.shape[1]
-            if width == HALF:
-                t = sb.tile([P, PACK, width], BF16, name=f"{name}raw{g}", tag="w_small", bufs=2, align_bytes=64)
-            elif name == "wv":
-                t = sb.tile([P, PACK, width], BF16, name=f"{name}raw{g}", tag="wide", bufs=2, align_bytes=64)
+        def load_x(kind, c, h):
+            view = x_dram[kind][c * CHUNK : (c + 1) * CHUNK, :].rearrange("(m s) d -> m s d", s=PACK)
+            if kind == "q":
+                t = held["bytes", c, h] = sb.tile([P, 2 * D], U8, name=f"xq_bytes{c}{h}", tag="xq_bytes", bufs=4, align_bytes=64)
             else:
-                t = sb.tile([P, PACK, width], BF16, name=f"{name}raw{g}", align_bytes=64)
-            nc.sync.dma_start(out=t[:], in_=w[512 * g : 512 * (g + 1), :].rearrange("(p j) n -> p j n", j=PACK))
-            wraw[name, g] = t
+                t = take_stage(("rows", kind, c, h))
+            nc.sync.dma_start(out=t[:].rearrange("p (s d) -> p s d", s=2), in_=view[:, 2 * h : 2 * h + 2, :])
+
+        def load_chunk(kind, c):
+            load_x(kind, c, 0)
+            load_x(kind, c, 1)
+
+        def load_w(name, g, h=0):
+            t = take_stage(("raw", name, g, h))
+            rows = w_dram[name][512 * g : 512 * (g + 1), h * HALF : (h + 1) * HALF]
+            nc.sync.dma_start(out=t[:].rearrange("p (j n) -> p j n", j=PACK), in_=rows.rearrange("(p j) n -> p j n", j=PACK))
 
         def load_scales():
             nc.sync.dma_start(out=scale_pt[:], in_=xq_scale.rearrange("o (g p t) -> p (o g) t", p=P, t=PACK))
@@ -110,89 +113,113 @@ def tile_linear_state_step_s7_kernel(
         def load_decay():
             nc.sync.dma_start(out=decay_sb[:], in_=decay.rearrange("(p i) -> p i", i=PACK))
 
-        def w_interleave(name, g, h, engine="vector", first=0, width=HALF, tag="w_grouped", bufs=3, staged=False):
-            raw = wraw[name, g][:, :, h * HALF + first : h * HALF + first + width]
-            if first == 0 and not staged:
-                w_grouped[name, g, h] = sb.tile(
-                    [P, HALF * PACK], BF16, name=f"{name}g{g}{h}", tag=tag, bufs=bufs, align_bytes=64
-                )
-            grouped = w_grouped[name, g, h][:, first * PACK : (first + width) * PACK]
+        def w_interleave(name, g, h, engine="vector", first=0, width=HALF):
+            key = ("grouped", name, g, h)
+            if key not in held:
+                take_stage(key, newest=engine == "gpsimd")
+            raw = held["raw", name, g, h][:].rearrange("p (j n) -> p j n", j=PACK)[:, :, first : first + width]
             if name == "wq":
+                planes = held[key][:].rearrange("p (t m j) -> p t m j", t=PACK, j=PACK)[:, :, first // PACK : (first + width) // PACK, :]
                 copy_on(
                     engine,
-                    grouped.rearrange("p (t c i j) -> p c t (i j)", t=PACK, i=2, j=PACK).rearrange("p c t (i j) -> p c t i j", i=2),
+                    planes.rearrange("p t (c i) j -> p c t i j", i=2),
                     raw.rearrange("p j (c i t) -> p c t i j", i=2, t=PACK),
+                )
+            elif engine == "gpsimd":
+                nc.gpsimd.tensor_scalar(
+                    out=held[key][:, first * PACK : (first + width) * PACK].rearrange("p (c j) -> p c j", j=PACK),
+                    in0=raw.rearrange("p j c -> p c j"), scalar1=1.0, scalar2=0.0, op0=ALU.mult, op1=ALU.add,
                 )
             else:
                 copy_on(
                     engine,
-                    grouped.rearrange("p (c i j) -> p c j i", i=4, j=PACK),
+                    held[key][:, first * PACK : (first + width) * PACK].rearrange("p (c i j) -> p c j i", i=4, j=PACK),
                     raw.rearrange("p j (c i) -> p c j i", i=4),
                 )
-
-        def w_interleave_gpsimd(name, g, width):
-            both = sb.tile([P, 2 * HALF * PACK], BF16, name=f"{name}g{g}", tag="handover", align_bytes=64)
-            w_grouped[name, g, 0], w_grouped[name, g, 1] = both[:, : HALF * PACK], both[:, HALF * PACK :]
-            nc.gpsimd.tensor_scalar(
-                out=both[:, : width * PACK].rearrange("p (c j) -> p c j", j=PACK),
-                in0=wraw[name, g][:, :, :width].rearrange("p j c -> p c j"),
-                scalar1=1.0, scalar2=0.0, op0=ALU.mult, op1=ALU.add,
-            )
+            if first + width == HALF and name != "st":
+                give_stage(("raw", name, g, h))
 
         def w_quantize(name, g, h, first=0, width=HALF):
             if first == 0:
-                wcodes[name, g, h] = new_operand(f"{name}c{g}{h}", HALF, f"{name}{g}{h}", 1)
-            codes, scales = wcodes[name, g, h]
-            quantize((codes[:, first : first + width], scales[:, first : first + width]),
-                     w_grouped[name, g, h][:, first * PACK : (first + width) * PACK])
+                new_operand((name, g, h), HALF, f"{name}{g}{h}", 1)
+            quantize((name, g, h), held["grouped", name, g, h], first, width)
+            if first + width == HALF:
+                give_stage(("grouped", name, g, h))
 
-        def widen(c, h):
-            t = sb.tile([P, 2, D], BF16, name=f"xq{c}{h}", tag="sorted", bufs=4, align_bytes=64)
-            sorted_x["q", c, h] = t
+        def quarter_interleave(q, g, engine):
+            key = ("quarter", q, g if engine == "gpsimd" else 0)
+            if key not in held:
+                take_stage(key, newest=engine == "gpsimd")
+            raw = held["raw", "wv", g, 1][:].rearrange("p (j n) -> p j n", j=PACK)[:, :, 256 * q : 256 * q + 256]
+            out = held[key][:, g * D : (g + 1) * D]
+            if engine == "gpsimd":
+                nc.gpsimd.tensor_scalar(
+                    out=out.rearrange("p (c j) -> p c j", j=PACK), in0=raw.rearrange("p j c -> p c j"),
+                    scalar1=1.0, scalar2=0.0, op0=ALU.mult, op1=ALU.add,
+                )
+            else:
+                copy_on(engine, out.rearrange("p (c i j) -> p c j i", i=4, j=PACK), raw.rearrange("p j (c i) -> p c j i", i=4))
+            if q == 1:
+                give_stage(("raw", "wv", g, 1))
+
+        def quarter_quantize(q, g, engine):
+            key = ("quarter", q, g if engine == "gpsimd" else 0)
+            if q == 0:
+                new_operand(("wv", g, 1), HALF, f"wv{g}1", 1)
+            codes, scales = columns(("wv", g, 1), 256 * q, 256)
+            nc.vector.quantize_mx(out=codes, scales=scales, in_=held[key][:, g * D : (g + 1) * D])
+            if g == 1 or engine == "gpsimd":
+                give_stage(key)
+
+        def widen_sorted(c, h):
+            t = take_stage(("sorted", "q", c, h))
             nc.vector.tensor_scalar(
-                out=t[:].rearrange("p u (m e) -> p m u e", e=2),
-                in0=rows["q", c, h][:].bitcast(FP8).rearrange("p s (m u e) -> p (s m) u e", u=2, e=2),
+                out=t[:].rearrange("p (u m e) -> p m u e", u=2, e=2),
+                in0=held["bytes", c, h][:].bitcast(FP8).rearrange("p (m u e) -> p m u e", u=2, e=2),
                 scalar1=ones[:, 0:1], scalar2=None, op0=ALU.mult,
             )
 
-        def widen_plain(h, engine):
-            t = sb.tile([P, 2, D], BF16, name=f"xq0{h}", tag="sorted", bufs=4, align_bytes=64)
-            copy_on(engine, t[:].rearrange("p s d -> p (s d)"), rows["q", 0, h][:].rearrange("p s d -> p (s d)").bitcast(FP8))
-            rows["q", 0, h] = t
+        def widen_plain(c, h, engine="vector"):
+            t = take_stage(("rows", "q", c, h))
+            copy_on(engine, t[:], held["bytes", c, h][:].bitcast(FP8))
 
         def sort_words(kind, c, h):
-            t = sb.tile([P, 2, D], BF16, name=f"x{kind}s{c}{h}", tag="sorted", bufs=4, align_bytes=64)
-            sorted_x[kind, c, h] = t
-            words = rows[kind, c, h][:].rearrange("p s d -> p (s d)").bitcast(F32)
+            t = take_stage(("sorted", kind, c, h))
             nc.vector.tensor_copy(
-                out=t[:].bitcast(F32).rearrange("p u m -> p m u"), in_=words.rearrange("p (m u) -> p m u", u=2)
+                out=t[:].bitcast(F32).rearrange("p (u m) -> p m u", u=2),
+                in_=held["rows", kind, c, h][:].bitcast(F32).rearrange("p (m u) -> p m u", u=2),
             )
+            give_stage(("rows", kind, c, h))
 
-        def turn(kind, c, s):
-            h, i = s // 2, s % 2
-            bank = new_bank(f"t{kind}{c}{s}")
-            x_banks[kind, c, s] = bank
-            for g in range(PASSES):
-                for u in range(2):
-                    if (kind, c, h) in sorted_x:
-                        first = (i * PASSES + g) * P
-                        chosen = sorted_x[kind, c, h][:, u, :].bitcast(F32)[:, first : first + P]
-                    else:
-                        chosen = rows[kind, c, h][:, i, :].bitcast(F32)[:, 256 * g + u : 256 * (g + 1) : 2]
-                    place = (u * PASSES + g) * P
-                    nc.tensor.transpose(bank[:, place : place + P], chosen, ident[:])
-            if kind != "q":
-                empty_turned(kind, c, s)
+        def turn(kind, c, h):
+            source = ("sorted", kind, c, h) if ("sorted", kind, c, h) in held else ("rows", kind, c, h)
+            words = held[source][:].bitcast(F32)
+            for i in range(2):
+                bank = take_bank(("turned", kind, c, 2 * h + i))
+                for g in range(PASSES):
+                    for u in range(2):
+                        if source[0] == "sorted":
+                            first = u * HALF + (i * PASSES + g) * P
+                            chosen = words[:, first : first + P]
+                        else:
+                            first = i * HALF + 2 * P * g
+                            chosen = words[:, first + u : first + 2 * P : 2]
+                        at = (u * PASSES + g) * P
+                        nc.tensor.transpose(bank[:, at : at + P], chosen, ident[:])
+                if kind != "q":
+                    empty_turned(kind, c, 2 * h + i)
+            give_stage(source)
+
+        def turn_chunk(kind, c):
+            turn(kind, c, 0)
+            turn(kind, c, 1)
 
         def empty_turned(kind, c, s):
             h, i = s // 2, s % 2
-            width = PASSES * P * PACK
             if i == 0:
-                x_grouped[kind, c, h] = sb.tile(
-                    [P, 2 * width], BF16, name=f"g{kind}{c}{h}", tag="x_grouped", bufs=4, align_bytes=64
-                )
-            part = x_grouped[kind, c, h][:, i * width : (i + 1) * width]
-            bank = x_banks[kind, c, s]
+                take_stage(("grouped", kind, c, h))
+            part = held["grouped", kind, c, h][:, i * D : (i + 1) * D]
+            bank = held["turned", kind, c, s]
             if kind == "q":
                 nc.vector.tensor_tensor(
                     out=part.rearrange("p (g m u e) -> p g m u e", g=PASSES, u=2, e=2),
@@ -205,158 +232,100 @@ def tile_linear_state_step_s7_kernel(
                     out=part.bitcast(F32).rearrange("p (g m u) -> p g m u", g=PASSES, u=2),
                     in_=bank[:].rearrange("p (u g m) -> p g m u", g=PASSES, u=2),
                 )
-            release_bank(f"t{kind}{c}{s}")
-
-        def x_quantize(kind, c, h):
-            xcodes[kind, c, h] = new_operand(f"x{kind}{c}{h}", 2 * PASSES * P, "x", 8)
-            quantize(xcodes[kind, c, h], x_grouped[kind, c, h][:])
-
-        def x_operand(kind, c, s, g):
-            return columns(xcodes[kind, c, s // 2], ((s % 2) * PASSES + g) * P, P)
-
-        def grouped_y(key, first):
-            kind, c, h = key
-            if kind == "v" and c < 2:
-                if first and h == 0:
-                    both = sb.tile([P, 4096], BF16, name=f"yv{c}", tag="wide", bufs=2, align_bytes=64)
-                    y_grouped["v", c, 0], y_grouped["v", c, 1] = both[:, :2048], both[:, 2048:]
-            elif first:
-                y_grouped[key] = sb.tile(
-                    [P, 2048], BF16, name="y" + "".join(str(x) for x in key), tag="y_grouped", bufs=8, align_bytes=64
-                )
-            return y_grouped[key]
-
-        def project_k(c, q):
-            grouped = grouped_y(("k", c, 0), q == 0)
-            bank = new_bank(f"kb{c}{q}")
-            for s in range(PACK):
-                for g in range(PASSES):
-                    multiply(bank[:, s * P : (s + 1) * P], x_operand("k", c, s, g),
-                             columns(wcodes["wk", g, 0], q * P, P), g == 0, g == PASSES - 1)
-            nc.scalar.activation(
-                out=grouped[:].rearrange("p (i m s) -> p i m s", i=PACK, s=PACK)[:, :, 32 * q : 32 * q + 32, :],
-                in_=bank[:].rearrange("p (s m i) -> p i m s", s=PACK, i=PACK),
-                func=ACT.Relu,
-            )
-            release_bank(f"kb{c}{q}")
-
-        def multiply_v(c, h, q):
-            bank = v_banks[c, h, q] = new_bank(f"vb{c}{h}{q}")
-            for s in range(PACK):
-                for g in range(PASSES):
-                    multiply(bank[:, s * P : (s + 1) * P], x_operand("v", c, s, g),
-                             columns(wcodes["wv", g, h], q * P, P), g == 0, g == PASSES - 1)
-
-        def project_v(c, h, q):
-            multiply_v(c, h, q)
-            empty_v(c, h, q)
-
-        def empty_v(c, h, q):
-            grouped = grouped_y(("v", c, h), q == 0)
-            bank = v_banks[c, h, q]
-            copy_on(
-                "scalar",
-                grouped[:].rearrange("p (n s) -> p n s", s=PACK)[:, q * P : (q + 1) * P, :],
-                bank[:].rearrange("p (s n) -> p n s", s=PACK),
-            )
-            release_bank(f"vb{c}{h}{q}")
-
-        def y_quantize(kind, c, h):
-            ycodes[kind, c, h] = new_operand(f"{kind}{c}{h}", HALF, kind, 3 if kind == "k" else 6)
-            quantize(ycodes[kind, c, h], y_grouped[kind, c, h][:])
-
-        def project_q(c, s, engine="scalar"):
-            grouped = grouped_y(("q", c, 0), s == 0)
-            bank = new_bank(f"qb{c}{s}")
-            for j in range(PACK):
-                for g in range(PASSES):
-                    multiply(bank[:, j * P : (j + 1) * P], columns(wcodes["wq", g, 0], j * P, P),
-                             x_operand("q", c, s, g), g == 0, g == PASSES - 1)
-            copy_on(
-                engine,
-                grouped[:, s * 512 : (s + 1) * 512].rearrange("p (m j) -> p m j", j=PACK),
-                bank[:].rearrange("p (j m) -> p m j", j=PACK),
-            )
-            release_bank(f"qb{c}{s}")
-
-        def q_quantize(c, h):
-            ycodes["q", c, h] = new_operand(f"q{c}{h}", 2 * P, "q", 4)
-            quantize(ycodes["q", c, h], y_grouped["q", c, 0][:, h * 1024 : (h + 1) * 1024])
-
-        out_view = out_0.rearrange("(c m s) e -> c m s e", m=P, s=PACK)
-
-        def read_state(c, s, h, engine="scalar"):
-            if h == 0:
-                out_rows[c, s] = sb.tile([P, E], F32, name=f"o{c}{s}", tag="rows", bufs=10, align_bytes=64)
-            o_sb = out_rows[c, s]
-            bank = new_bank(f"ob{c}{s}{h}")
-            multiply(bank[:], columns(ycodes["q", c, s // 2], (s % 2) * P, P), columns(wcodes["st", 0, h], 0, HALF),
-                     True, True)
-            copy_on(engine, o_sb[:, h * HALF : (h + 1) * HALF], bank[:])
-            release_bank(f"ob{c}{s}{h}")
-            if h == 1:
-                nc.sync.dma_start(out=out_view[c, :, s, :], in_=o_sb[:])
-
-        new_view = out_1.rearrange("(p i) e -> p i e", i=PACK)
-
-        def update_state(h, i, first=0, width=HALF):
-            bank = new_bank(f"ub{h}{i}{first}")
-            for c in range(CHUNKS):
-                multiply(bank[:, :width], columns(ycodes["k", c, 0], i * P, P), columns(ycodes["v", c, h], first, width),
-                         c == 0, c == CHUNKS - 1)
-            update_banks[h, i, first] = bank
-
-        def finish_update(h, i, first=0, width=HALF):
-            bank = update_banks[h, i, first]
-            new_sb = sb.tile([P, width], F32, name=f"n{h}{i}{first}", tag="rows", bufs=10, align_bytes=64)
-            cut = slice(h * HALF + first, h * HALF + first + width)
-            nc.vector.scalar_tensor_tensor(
-                out=new_sb[:], in0=wraw["st", 0][:, i, cut], scalar=decay_sb[:, i : i + 1], in1=bank[:, :width],
-                op0=ALU.mult, op1=ALU.add,
-            )
-            release_bank(f"ub{h}{i}{first}")
-            nc.sync.dma_start(out=new_view[:, i, cut], in_=new_sb[:])
-
-        def turn_pair(kind, c, h):
-            turn(kind, c, 2 * h)
-            turn(kind, c, 2 * h + 1)
-
-        def keys(c, h):
-            project_k(c, 2 * h)
-            project_k(c, 2 * h + 1)
-
-        def queries(c, h):
-            project_q(c, 2 * h)
-            project_q(c, 2 * h + 1)
+            give_bank(("turned", kind, c, s))
 
         def scale_pair(c, h):
             empty_turned("q", c, 2 * h)
             empty_turned("q", c, 2 * h + 1)
 
-        def values(c, h):
-            for q in range(4):
-                project_v(c, h, q)
+        def x_quantize(kind, c, h):
+            new_operand(("x", kind, c, h), HALF, "x", XBUFS)
+            quantize(("x", kind, c, h), held["grouped", kind, c, h], 0, HALF)
+            give_stage(("grouped", kind, c, h))
 
-        def sort_chunk(kind, c):
-            sort_words(kind, c, 0)
-            sort_words(kind, c, 1)
+        def x_operand(kind, c, s, g):
+            return columns(("x", kind, c, s // 2), ((s % 2) * PASSES + g) * P, P)
+
+        def project(kind, c, h, q):
+            if q == 0:
+                take_stage(("y", kind, c, h))
+            grouped = held["y", kind, c, h][:]
+            bank = take_bank(("proj", kind, c, h, q))
+            for s in range(PACK):
+                for g in range(PASSES):
+                    if kind == "q":
+                        pair = columns(("wq", g, 0), s * P, P), x_operand("q", c, q, g)
+                    else:
+                        pair = x_operand(kind, c, s, g), columns(("w" + kind, g, h), q * P, P)
+                    multiply(bank[:, s * P : (s + 1) * P], pair[0], pair[1], g == 0, g == PASSES - 1)
+            if kind == "k":
+                nc.scalar.activation(
+                    out=grouped.rearrange("p (i m s) -> p i m s", i=PACK, s=PACK)[:, :, 32 * q : 32 * q + 32, :],
+                    in_=bank[:].rearrange("p (s m i) -> p i m s", s=PACK, i=PACK),
+                    func=ACT.Relu,
+                )
+            else:
+                nc.scalar.copy(
+                    out=grouped[:, q * HALF : (q + 1) * HALF].rearrange("p (n s) -> p n s", s=PACK),
+                    in_=bank[:].rearrange("p (s n) -> p n s", s=PACK),
+                )
+            give_bank(("proj", kind, c, h, q))
+
+        def project_banks(kind, c, h, first=0, count=4):
+            for q in range(first, first + count):
+                project(kind, c, h, q)
+
+        def y_quantize(kind, c, h):
+            new_operand(("y", kind, c, h), HALF, kind, 3 if kind == "k" else 6)
+            quantize(("y", kind, c, h), held["y", kind, c, h], 0, HALF)
+            give_stage(("y", kind, c, h))
+
+        def q_quantize(c, h):
+            new_operand(("y", "q", c, h), 2 * P, "q", 4)
+            quantize(("y", "q", c, h), held["y", "q", c, 0][:, h * D : (h + 1) * D], 0, 2 * P)
+            if h == 1:
+                give_stage(("y", "q", c, 0))
+
+        out_view = out_0.rearrange("(c m s) e -> c m s e", m=P, s=PACK)
+        new_view = out_1.rearrange("(p i) e -> p i e", i=PACK)
+
+        def read_state(c, s, h, engine="scalar"):
+            if h == 0:
+                take_stage(("o", c, s))
+            rows = held["o", c, s][:].bitcast(F32)
+            bank = take_bank(("read", c, s, h))
+            multiply(bank[:], columns(("y", "q", c, s // 2), (s % 2) * P, P), columns(("st", 0, h), 0, HALF), True, True)
+            copy_on(engine, rows[:, h * HALF : (h + 1) * HALF], bank[:])
+            give_bank(("read", c, s, h))
+            if h == 1:
+                nc.sync.dma_start(out=out_view[c, :, s, :], in_=rows)
+                give_stage(("o", c, s))
+
+        def read_slot(c, s, second="scalar"):
+            read_state(c, s, 0)
+            read_state(c, s, 1, second)
+
+        def update_sums(h, i, first=0, width=HALF):
+            bank = take_bank(("update", h, i, first))
+            for c in range(CHUNKS):
+                multiply(bank[:, :width], columns(("y", "k", c, 0), i * P, P), columns(("y", "v", c, h), first, width),
+                         c == 0, c == CHUNKS - 1)
+
+        def update_rows(h, i, first=0, width=HALF):
+            key = ("new", h, i, first)
+            bank = held["update", h, i, first]
+            rows = take_stage(key)[:].bitcast(F32)[:, :width]
+            old = held["raw", "st", 0, h][:, i * HALF + first : i * HALF + first + width]
+            nc.vector.scalar_tensor_tensor(
+                out=rows, in0=old, scalar=decay_sb[:, i : i + 1], in1=bank[:, :width], op0=ALU.mult, op1=ALU.add,
+            )
+            give_bank(("update", h, i, first))
+            nc.sync.dma_start(out=new_view[:, i, h * HALF + first : h * HALF + first + width], in_=rows)
+            give_stage(key)
 
         def update(h, i, first=0, width=HALF):
-            update_state(h, i, first, width)
-            finish_update(h, i, first, width)
-
-        def read_pair(c, h, second="vector"):
-            for s in (2 * h, 2 * h + 1):
-                read_state(c, s, 0)
-                read_state(c, s, 1, second)
-
-        def turn_chunk(kind, c):
-            turn_pair(kind, c, 0)
-            turn_pair(kind, c, 1)
-
-        def load_chunk(kind, c):
-            load_x(kind, c, 0)
-            load_x(kind, c, 1)
+            update_sums(h, i, first, width)
+            update_rows(h, i, first, width)
 
         with tc.manual_schedule():
             load_chunk("q", 0)
@@ -366,146 +335,160 @@ def tile_linear_state_step_s7_kernel(
             load_x("k", 0, 1)
             load_w("wk", 1)
             load_x("k", 1, 0)
-            load_w("wv", 0)
+            load_w("wv", 0, 0)
             load_x("k", 1, 1)
             load_chunk("k", 2)
-            load_w("wv", 1)
+            load_w("wv", 1, 0)
             load_chunk("v", 0)
             load_chunk("v", 1)
-            widen_plain(0, "vector")
-            widen_plain(1, "vector")
-            turn_pair("q", 0, 0)
+            load_w("wq", 0)
+            load_w("wq", 1)
+            load_chunk("v", 2)
+            load_chunk("q", 1)
+            load_w("st", 0, 0)
+            load_w("st", 0, 1)
+            load_w("wv", 0, 1)
+            load_w("wv", 1, 1)
+            load_decay()
+
+            widen_plain(0, 0)
+            widen_plain(0, 1)
+            load_chunk("q", 2)
+            w_interleave("wk", 0, 0, "gpsimd", 0, 256)
+            turn("q", 0, 0)
             scale_pair(0, 0)
-            turn_pair("k", 0, 0)
-            turn_pair("q", 0, 1)
-            w_interleave("wk", 0, 0, "vector", 0, 256)
+            turn("k", 0, 0)
+            turn("q", 0, 1)
             w_interleave("wk", 0, 0, "scalar", 256, 256)
-            turn_pair("k", 0, 1)
+            turn("k", 0, 1)
             x_quantize("k", 0, 0)
-            w_interleave("wk", 1, 0, "vector", 0, 256, tag="handover", bufs=1)
+            w_interleave("wk", 1, 0, "vector", 0, 256)
             w_quantize("wk", 0, 0)
             w_quantize("wk", 1, 0, 0, 256)
             x_quantize("k", 0, 1)
-            w_interleave("wk", 1, 0, "vector", 256, 256)
-            w_quantize("wk", 1, 0, 256, 256)
-            load_chunk("q", 1)
-            load_w("wq", 0)
-            load_w("wq", 1)
-            load_w("st", 0)
-            load_decay()
-            w_interleave_gpsimd("wv", 0, 384)
-            turn_pair("k", 1, 0)
-            keys(0, 0)
-            w_interleave("wv", 0, 1, "scalar", 256, 256)
-            turn_pair("k", 1, 1)
+            w_interleave("wv", 0, 0, "gpsimd", 0, 384)
+            turn("k", 1, 0)
+            w_interleave("wk", 1, 0, "scalar", 256, 256)
+            project_banks("k", 0, 0, 0, 2)
+            turn("k", 1, 1)
             scale_pair(0, 1)
+            w_quantize("wk", 1, 0, 256, 256)
+            sort_words("k", 2, 0)
             x_quantize("k", 1, 0)
-            x_quantize("q", 0, 0)
+            sort_words("k", 2, 1)
+            project_banks("k", 0, 0, 2, 2)
             w_interleave("wv", 0, 0, "vector", 384, 128)
-            w_interleave("wv", 0, 1, "vector", 0, 256, staged=True)
             x_quantize("k", 1, 1)
-            load_chunk("v", 2)
-            load_chunk("q", 2)
-            keys(0, 1)
-            x_quantize("q", 0, 1)
-            w_quantize("wv", 0, 0)
-            w_quantize("wv", 0, 1)
             turn_chunk("k", 2)
+            w_quantize("wv", 0, 0)
             w_interleave("wv", 1, 0)
+            sort_words("v", 0, 0)
+            sort_words("v", 0, 1)
+            w_quantize("wv", 1, 0)
+            project_banks("k", 1, 0)
             x_quantize("k", 2, 0)
             x_quantize("k", 2, 1)
-            w_quantize("wv", 1, 0)
-            keys(1, 0)
-            keys(1, 1)
             turn_chunk("v", 0)
-            sort_chunk("v", 1)
+            sort_words("v", 1, 0)
+            sort_words("v", 1, 1)
+            x_quantize("q", 0, 0)
+            x_quantize("q", 0, 1)
+
+            project_banks("k", 2, 0)
             x_quantize("v", 0, 0)
             x_quantize("v", 0, 1)
-            w_interleave("wv", 1, 1)
-            keys(2, 0)
-            keys(2, 1)
             turn_chunk("v", 1)
-            widen(1, 0)
-            w_quantize("wv", 1, 1)
-            widen(1, 1)
+            w_interleave("wq", 0, 0)
+            sort_words("v", 2, 0)
+            sort_words("v", 2, 1)
+            w_interleave("wq", 1, 0)
+            project_banks("v", 0, 0)
             x_quantize("v", 1, 0)
             x_quantize("v", 1, 1)
-            w_interleave("wq", 0, 0)
-            w_interleave("wq", 1, 0, tag="handover", bufs=1)
-            sort_chunk("v", 2)
+            turn_chunk("v", 2)
+            widen_sorted(1, 0)
+            widen_sorted(1, 1)
+            project_banks("v", 1, 0)
             w_quantize("wq", 0, 0)
+            x_quantize("v", 2, 0)
             w_quantize("wq", 1, 0)
-            values(0, 0)
-            values(0, 1)
-            values(1, 0)
+            x_quantize("v", 2, 1)
+
+            w_interleave("st", 0, 0, "gpsimd")
+            w_interleave("st", 0, 1, "gpsimd", 0, 128)
+            w_interleave("st", 0, 1, "scalar", 128, 384)
             turn_chunk("q", 1)
-            w_interleave_gpsimd("st", 0, 704)
-            values(1, 1)
+            project_banks("q", 0, 0)
             scale_pair(1, 0)
             scale_pair(1, 1)
-            queries(0, 0)
-            queries(0, 1)
+            project_banks("v", 2, 0)
             x_quantize("q", 1, 0)
-            w_interleave("st", 0, 1, "vector", 192, 320)
             q_quantize(0, 0)
             w_quantize("st", 0, 0)
-            w_quantize("st", 0, 1)
             x_quantize("q", 1, 1)
+            w_quantize("st", 0, 1)
             q_quantize(0, 1)
-            turn_chunk("v", 2)
-            widen(2, 0)
-            widen(2, 1)
-            x_quantize("v", 2, 0)
-            x_quantize("v", 2, 1)
-            for s in range(PACK):
-                project_q(1, s)
-                read_state(0, s, 0)
-                if s == 2:
-                    q_quantize(1, 0)
-                read_state(0, s, 1, "scalar")
-
-            last = 2
-            turn_chunk("q", last)
-            scale_pair(last, 0)
+            quarter_interleave(0, 0, "vector")
+            quarter_interleave(0, 1, "vector")
+            quarter_quantize(0, 0, "vector")
+            quarter_quantize(0, 1, "vector")
+            project_banks("q", 1, 0, 0, 2)
+            read_state(0, 0, 0)
+            project("q", 1, 0, 2)
+            read_state(0, 0, 1)
+            project("q", 1, 0, 3)
+            for s in range(1, PACK):
+                read_slot(0, s)
+            widen_sorted(2, 0)
+            q_quantize(1, 0)
+            widen_sorted(2, 1)
             q_quantize(1, 1)
-            x_quantize("q", last, 0)
-            for q in range(4):
-                project_v(last, 0, q)
-                read_state(1, q // 2, q % 2)
-            scale_pair(last, 1)
-            queries(last, 0)
-            x_quantize("q", last, 1)
-            y_quantize("k", 0, 0)
-            read_state(1, 2, 0)
-            y_quantize("k", 1, 0)
-            read_state(1, 2, 1, "vector")
-            q_quantize(last, 0)
-            read_state(1, 3, 0)
-            read_state(1, 3, 1, "vector")
-            queries(last, 1)
-            y_quantize("k", 2, 0)
-            read_state(last, 0, 0)
-            read_state(last, 0, 1, "vector")
-            q_quantize(last, 1)
-            read_state(last, 1, 0)
-            read_state(last, 1, 1, "vector")
-            project_v(last, 1, 0)
-            project_v(last, 1, 1)
+            quarter_interleave(1, 0, "gpsimd")
+            project_banks("v", 0, 1, 0, 2)
+            turn_chunk("q", 2)
+
+            empty_turned("q", 2, 0)
+            project("v", 1, 1, 0)
+            empty_turned("q", 2, 1)
+            x_quantize("q", 2, 0)
+            quarter_interleave(1, 1, "gpsimd")
+            project("v", 1, 1, 1)
+            read_slot(1, 0)
+            project("v", 2, 1, 0)
+            empty_turned("q", 2, 2)
+            read_slot(1, 1)
+            empty_turned("q", 2, 3)
+            project("v", 2, 1, 1)
+            quarter_quantize(1, 0, "gpsimd")
+            x_quantize("q", 2, 1)
+            quarter_quantize(1, 1, "gpsimd")
+
+            project_banks("q", 2, 0, 0, 2)
+            read_slot(1, 2)
+            project_banks("q", 2, 0, 2, 2)
+            for c in range(CHUNKS):
+                y_quantize("k", c, 0)
+            q_quantize(2, 0)
+            read_slot(1, 3, "vector")
             y_quantize("v", 0, 0)
+            q_quantize(2, 1)
             y_quantize("v", 1, 0)
             y_quantize("v", 2, 0)
-            read_state(last, 2, 0)
-            read_state(last, 2, 1)
-            read_state(last, 3, 0)
-            read_state(last, 3, 1)
-            project_v(last, 1, 2)
-            project_v(last, 1, 3)
-            y_quantize("v", 0, 1)
-            y_quantize("v", 1, 1)
+            project_banks("v", 0, 1, 2, 2)
+            read_slot(2, 0, "vector")
+            project_banks("v", 1, 1, 2, 2)
             update(0, 0)
+            read_slot(2, 1, "vector")
+            y_quantize("v", 0, 1)
+            project_banks("v", 2, 1, 2, 2)
             update(0, 1)
+            y_quantize("v", 1, 1)
+            read_slot(2, 2)
+            update(0, 2)
+            read_slot(2, 3)
             y_quantize("v", 2, 1)
-            for n in range(2, 7):
-                update(n // 4, n % 4)
+            update(0, 3)
+            for i in range(3):
+                update(1, i)
             update(1, 3, 0, 256)
             update(1, 3, 256, 256)

@@ -382,8 +382,6 @@ def tile_linear_state_step_s7_kernel(
             turn_chunk("k", 2)
             w_quantize("wv", 0, 0)
             w_interleave("wv", 1, 0)
-            sort_words("v", 0, 0)
-            sort_words("v", 0, 1)
             w_quantize("wv", 1, 0)
             project_banks("k", 1, 0)
             x_quantize("k", 2, 0)
@@ -399,8 +397,6 @@ def tile_linear_state_step_s7_kernel(
             x_quantize("v", 0, 1)
             turn_chunk("v", 1)
             w_interleave("wq", 0, 0)
-            sort_words("v", 2, 0)
-            sort_words("v", 2, 1)
             w_interleave("wq", 1, 0)
             project_banks("v", 0, 0)
             x_quantize("v", 1, 0)
@@ -414,9 +410,9 @@ def tile_linear_state_step_s7_kernel(
             w_quantize("wq", 1, 0)
             x_quantize("v", 2, 1)
 
+            w_interleave("st", 0, 1, "scalar", 128, 384)
             w_interleave("st", 0, 0, "gpsimd")
             w_interleave("st", 0, 1, "gpsimd", 0, 128)
-            w_interleave("st", 0, 1, "scalar", 128, 384)
             turn_chunk("q", 1)
             project_banks("q", 0, 0)
             scale_pair(1, 0)
@@ -477,16 +473,18 @@ def tile_linear_state_step_s7_kernel(
             project_banks("v", 0, 1, 2, 2)
             read_slot(2, 0, "vector")
             project_banks("v", 1, 1, 2, 2)
-            update(0, 0)
             read_slot(2, 1, "vector")
+            update(0, 0)
             y_quantize("v", 0, 1)
-            project_banks("v", 2, 1, 2, 2)
-            update(0, 1)
-            y_quantize("v", 1, 1)
             read_slot(2, 2)
-            update(0, 2)
+            project_banks("v", 2, 1, 2, 2)
+            update_sums(0, 1)
+            y_quantize("v", 1, 1)
+            update_rows(0, 1)
             read_slot(2, 3)
+            update_sums(0, 2)
             y_quantize("v", 2, 1)
+            update_rows(0, 2)
             update(0, 3)
             for i in range(3):
                 update(1, i)

@@ -22,6 +22,7 @@ CHUNKS = T // CHUNK
 PASSES = D // 512
 HALF = 512
 STAGE = 2048
+EARLY = 256
 STAGES = 37
 XBUFS = 11
 
@@ -146,28 +147,30 @@ def tile_linear_state_step_s7_kernel(
             if first + width == HALF:
                 give_stage(("grouped", name, g, h))
 
-        def quarter_interleave(q, g, engine):
-            key = ("quarter", q, g if engine == "gpsimd" else 0)
+        def late_interleave(g, engine):
+            first, width = (0, EARLY) if engine == "vector" else (EARLY, HALF - EARLY)
+            key = ("late", engine, g if engine == "gpsimd" else 0)
             if key not in held:
                 take_stage(key, newest=engine == "gpsimd")
-            raw = held["raw", "wv", g, 1][:].rearrange("p (j n) -> p j n", j=PACK)[:, :, 256 * q : 256 * q + 256]
-            out = held[key][:, g * D : (g + 1) * D]
+            raw = held["raw", "wv", g, 1][:].rearrange("p (j n) -> p j n", j=PACK)[:, :, first : first + width]
             if engine == "gpsimd":
                 nc.gpsimd.tensor_scalar(
-                    out=out.rearrange("p (c j) -> p c j", j=PACK), in0=raw.rearrange("p j c -> p c j"),
+                    out=held[key][:, : width * PACK].rearrange("p (c j) -> p c j", j=PACK), in0=raw.rearrange("p j c -> p c j"),
                     scalar1=1.0, scalar2=0.0, op0=ALU.mult, op1=ALU.add,
                 )
-            else:
-                copy_on(engine, out.rearrange("p (c i j) -> p c j i", i=4, j=PACK), raw.rearrange("p j (c i) -> p c j i", i=4))
-            if q == 1:
                 give_stage(("raw", "wv", g, 1))
+            else:
+                out = held[key][:, g * width * PACK : (g + 1) * width * PACK]
+                copy_on(engine, out.rearrange("p (c i j) -> p c j i", i=4, j=PACK), raw.rearrange("p j (c i) -> p c j i", i=4))
 
-        def quarter_quantize(q, g, engine):
-            key = ("quarter", q, g if engine == "gpsimd" else 0)
-            if q == 0:
+        def late_quantize(g, engine):
+            first, width = (0, EARLY) if engine == "vector" else (EARLY, HALF - EARLY)
+            key = ("late", engine, g if engine == "gpsimd" else 0)
+            if engine == "vector":
                 new_operand(("wv", g, 1), HALF, f"wv{g}1", 1)
-            codes, scales = columns(("wv", g, 1), 256 * q, 256)
-            nc.vector.quantize_mx(out=codes, scales=scales, in_=held[key][:, g * D : (g + 1) * D])
+            at = g * width * PACK if engine == "vector" else 0
+            codes, scales = columns(("wv", g, 1), first, width)
+            nc.vector.quantize_mx(out=codes, scales=scales, in_=held[key][:, at : at + width * PACK])
             if g == 1 or engine == "gpsimd":
                 give_stage(key)
 
@@ -330,104 +333,106 @@ def tile_linear_state_step_s7_kernel(
         with tc.manual_schedule():
             load_chunk("q", 0)
             load_scales()
-            load_x("k", 0, 0)
+            load_chunk("q", 1)
             load_w("wk", 0)
-            load_x("k", 0, 1)
+            load_chunk("k", 0)
             load_w("wk", 1)
             load_x("k", 1, 0)
             load_w("wv", 0, 0)
             load_x("k", 1, 1)
-            load_chunk("k", 2)
             load_w("wv", 1, 0)
+            load_chunk("k", 2)
             load_chunk("v", 0)
-            load_chunk("v", 1)
             load_w("wq", 0)
             load_w("wq", 1)
+            load_chunk("v", 1)
             load_chunk("v", 2)
-            load_chunk("q", 1)
             load_w("st", 0, 0)
             load_w("st", 0, 1)
             load_w("wv", 0, 1)
             load_w("wv", 1, 1)
             load_decay()
-
             widen_plain(0, 0)
             widen_plain(0, 1)
+            widen_plain(1, 0, "scalar")
+            widen_plain(1, 1, "scalar")
             load_chunk("q", 2)
-            w_interleave("wk", 0, 0, "gpsimd", 0, 256)
-            turn("q", 0, 0)
+            w_interleave("wk", 0, 0, "gpsimd", 0, 384)
+            turn_chunk("q", 0)
             scale_pair(0, 0)
+            turn("q", 1, 0)
             turn("k", 0, 0)
-            turn("q", 0, 1)
-            w_interleave("wk", 0, 0, "scalar", 256, 256)
+            empty_turned("q", 0, 2)
             turn("k", 0, 1)
-            x_quantize("k", 0, 0)
+            turn("q", 1, 1)
+            w_interleave("wk", 0, 0, "vector", 384, 128)
+            x_quantize("q", 0, 0)
             w_interleave("wk", 1, 0, "vector", 0, 256)
             w_quantize("wk", 0, 0)
+            x_quantize("k", 0, 0)
             w_quantize("wk", 1, 0, 0, 256)
             x_quantize("k", 0, 1)
-            w_interleave("wv", 0, 0, "gpsimd", 0, 384)
-            turn("k", 1, 0)
             w_interleave("wk", 1, 0, "scalar", 256, 256)
-            project_banks("k", 0, 0, 0, 2)
-            turn("k", 1, 1)
-            scale_pair(0, 1)
             w_quantize("wk", 1, 0, 256, 256)
-            sort_words("k", 2, 0)
+            w_interleave("wv", 0, 0, "gpsimd")
+            turn("k", 1, 0)
+            project("k", 0, 0, 0)
+            empty_turned("q", 0, 3)
+            project_banks("k", 0, 0, 1, 2)
+            empty_turned("q", 1, 0)
+            project("k", 0, 0, 3)
+            turn("k", 1, 1)
+            empty_turned("q", 1, 1)
             x_quantize("k", 1, 0)
-            sort_words("k", 2, 1)
-            project_banks("k", 0, 0, 2, 2)
-            w_interleave("wv", 0, 0, "vector", 384, 128)
+            x_quantize("q", 0, 1)
             x_quantize("k", 1, 1)
+            w_interleave("wv", 1, 0, "gpsimd", 0, 320)
             turn_chunk("k", 2)
-            w_quantize("wv", 0, 0)
-            w_interleave("wv", 1, 0)
-            w_quantize("wv", 1, 0)
-            project_banks("k", 1, 0)
+            project("k", 1, 0, 0)
+            empty_turned("q", 1, 2)
+            project_banks("k", 1, 0, 1, 2)
+            empty_turned("q", 1, 3)
+            project("k", 1, 0, 3)
+            sort_words("v", 0, 1)
             x_quantize("k", 2, 0)
             x_quantize("k", 2, 1)
             turn_chunk("v", 0)
+            w_interleave("wv", 1, 0, "vector", 320, 192)
+            w_quantize("wv", 0, 0)
             sort_words("v", 1, 0)
+            w_quantize("wv", 1, 0)
             sort_words("v", 1, 1)
-            x_quantize("q", 0, 0)
-            x_quantize("q", 0, 1)
-
             project_banks("k", 2, 0)
             x_quantize("v", 0, 0)
             x_quantize("v", 0, 1)
             turn_chunk("v", 1)
             w_interleave("wq", 0, 0)
-            w_interleave("wq", 1, 0)
+            sort_words("v", 2, 0)
+            sort_words("v", 2, 1)
             project_banks("v", 0, 0)
             x_quantize("v", 1, 0)
             x_quantize("v", 1, 1)
+            w_interleave("wq", 1, 0)
             turn_chunk("v", 2)
-            widen_sorted(1, 0)
-            widen_sorted(1, 1)
-            project_banks("v", 1, 0)
             w_quantize("wq", 0, 0)
-            x_quantize("v", 2, 0)
             w_quantize("wq", 1, 0)
+            project_banks("v", 1, 0)
+            x_quantize("v", 2, 0)
             x_quantize("v", 2, 1)
-
-            w_interleave("st", 0, 1, "scalar", 128, 384)
-            w_interleave("st", 0, 0, "gpsimd")
-            w_interleave("st", 0, 1, "gpsimd", 0, 128)
-            turn_chunk("q", 1)
-            project_banks("q", 0, 0)
-            scale_pair(1, 0)
-            scale_pair(1, 1)
-            project_banks("v", 2, 0)
+            w_interleave("st", 0, 0)
             x_quantize("q", 1, 0)
-            q_quantize(0, 0)
             w_quantize("st", 0, 0)
+            project_banks("q", 0, 0)
+            w_interleave("st", 0, 1)
+            q_quantize(0, 0)
             x_quantize("q", 1, 1)
             w_quantize("st", 0, 1)
             q_quantize(0, 1)
-            quarter_interleave(0, 0, "vector")
-            quarter_interleave(0, 1, "vector")
-            quarter_quantize(0, 0, "vector")
-            quarter_quantize(0, 1, "vector")
+            project_banks("v", 2, 0)
+            late_interleave(0, "vector")
+            late_interleave(1, "vector")
+            late_quantize(0, "vector")
+            late_quantize(1, "vector")
             project_banks("q", 1, 0, 0, 2)
             read_state(0, 0, 0)
             project("q", 1, 0, 2)
@@ -439,7 +444,7 @@ def tile_linear_state_step_s7_kernel(
             q_quantize(1, 0)
             widen_sorted(2, 1)
             q_quantize(1, 1)
-            quarter_interleave(1, 0, "gpsimd")
+            late_interleave(0, "gpsimd")
             project_banks("v", 0, 1, 0, 2)
             turn_chunk("q", 2)
 
@@ -447,7 +452,7 @@ def tile_linear_state_step_s7_kernel(
             project("v", 1, 1, 0)
             empty_turned("q", 2, 1)
             x_quantize("q", 2, 0)
-            quarter_interleave(1, 1, "gpsimd")
+            late_interleave(1, "gpsimd")
             project("v", 1, 1, 1)
             read_slot(1, 0)
             project("v", 2, 1, 0)
@@ -455,23 +460,24 @@ def tile_linear_state_step_s7_kernel(
             read_slot(1, 1)
             empty_turned("q", 2, 3)
             project("v", 2, 1, 1)
-            quarter_quantize(1, 0, "gpsimd")
+            late_quantize(0, "gpsimd")
             x_quantize("q", 2, 1)
-            quarter_quantize(1, 1, "gpsimd")
+            late_quantize(1, "gpsimd")
 
             project_banks("q", 2, 0, 0, 2)
             read_slot(1, 2)
+            read_state(1, 3, 0)
             project_banks("q", 2, 0, 2, 2)
             for c in range(CHUNKS):
                 y_quantize("k", c, 0)
             q_quantize(2, 0)
-            read_slot(1, 3, "vector")
+            read_state(1, 3, 1, "vector")
             y_quantize("v", 0, 0)
-            q_quantize(2, 1)
             y_quantize("v", 1, 0)
-            y_quantize("v", 2, 0)
             project_banks("v", 0, 1, 2, 2)
             read_slot(2, 0, "vector")
+            q_quantize(2, 1)
+            y_quantize("v", 2, 0)
             project_banks("v", 1, 1, 2, 2)
             read_slot(2, 1, "vector")
             update(0, 0)

@@ -194,7 +194,7 @@ def tile_linear_state_step_s7_kernel(
             )
             give_stage(("rows", kind, c, h))
 
-        def turn(kind, c, h):
+        def turn(kind, c, h, engine="scalar"):
             source = ("sorted", kind, c, h) if ("sorted", kind, c, h) in held else ("rows", kind, c, h)
             words = held[source][:].bitcast(F32)
             for i in range(2):
@@ -209,15 +209,15 @@ def tile_linear_state_step_s7_kernel(
                             chosen = words[:, first + u : first + 2 * P : 2]
                         at = (u * PASSES + g) * P
                         nc.tensor.transpose(bank[:, at : at + P], chosen, ident[:])
-                if kind != "q":
+                if kind != "q" and engine == "scalar":
                     empty_turned(kind, c, 2 * h + i)
             give_stage(source)
 
-        def turn_chunk(kind, c):
-            turn(kind, c, 0)
-            turn(kind, c, 1)
+        def turn_chunk(kind, c, engine="scalar"):
+            turn(kind, c, 0, engine)
+            turn(kind, c, 1, engine)
 
-        def empty_turned(kind, c, s):
+        def empty_turned(kind, c, s, engine="scalar"):
             h, i = s // 2, s % 2
             if i == 0:
                 take_stage(("grouped", kind, c, h))
@@ -231,9 +231,10 @@ def tile_linear_state_step_s7_kernel(
                     op=ALU.mult,
                 )
             else:
-                nc.scalar.copy(
-                    out=part.bitcast(F32).rearrange("p (g m u) -> p g m u", g=PASSES, u=2),
-                    in_=bank[:].rearrange("p (u g m) -> p g m u", g=PASSES, u=2),
+                copy_on(
+                    engine,
+                    part.bitcast(F32).rearrange("p (g m u) -> p g m u", g=PASSES, u=2),
+                    bank[:].rearrange("p (u g m) -> p g m u", g=PASSES, u=2),
                 )
             give_bank(("turned", kind, c, s))
 
@@ -249,10 +250,7 @@ def tile_linear_state_step_s7_kernel(
         def x_operand(kind, c, s, g):
             return columns(("x", kind, c, s // 2), ((s % 2) * PASSES + g) * P, P)
 
-        def project(kind, c, h, q):
-            if q == 0:
-                take_stage(("y", kind, c, h))
-            grouped = held["y", kind, c, h][:]
+        def project_sums(kind, c, h, q):
             bank = take_bank(("proj", kind, c, h, q))
             for s in range(PACK):
                 for g in range(PASSES):
@@ -261,6 +259,16 @@ def tile_linear_state_step_s7_kernel(
                     else:
                         pair = x_operand(kind, c, s, g), columns(("w" + kind, g, h), q * P, P)
                     multiply(bank[:, s * P : (s + 1) * P], pair[0], pair[1], g == 0, g == PASSES - 1)
+
+        def project(kind, c, h, q):
+            project_sums(kind, c, h, q)
+            project_empty(kind, c, h, q)
+
+        def project_empty(kind, c, h, q, engine="scalar"):
+            if q == 0:
+                take_stage(("y", kind, c, h))
+            grouped = held["y", kind, c, h][:]
+            bank = held["proj", kind, c, h, q]
             if kind == "k":
                 nc.scalar.activation(
                     out=grouped.rearrange("p (i m s) -> p i m s", i=PACK, s=PACK)[:, :, 32 * q : 32 * q + 32, :],
@@ -268,9 +276,10 @@ def tile_linear_state_step_s7_kernel(
                     func=ACT.Relu,
                 )
             else:
-                nc.scalar.copy(
-                    out=grouped[:, q * HALF : (q + 1) * HALF].rearrange("p (n s) -> p n s", s=PACK),
-                    in_=bank[:].rearrange("p (s n) -> p n s", s=PACK),
+                copy_on(
+                    engine,
+                    grouped[:, q * HALF : (q + 1) * HALF].rearrange("p (n s) -> p n s", s=PACK),
+                    bank[:].rearrange("p (s n) -> p n s", s=PACK),
                 )
             give_bank(("proj", kind, c, h, q))
 
@@ -292,17 +301,24 @@ def tile_linear_state_step_s7_kernel(
         out_view = out_0.rearrange("(c m s) e -> c m s e", m=P, s=PACK)
         new_view = out_1.rearrange("(p i) e -> p i e", i=PACK)
 
-        def read_state(c, s, h, engine="scalar"):
-            if h == 0:
-                take_stage(("o", c, s))
-            rows = held["o", c, s][:].bitcast(F32)
+        def read_sums(c, s, h):
             bank = take_bank(("read", c, s, h))
             multiply(bank[:], columns(("y", "q", c, s // 2), (s % 2) * P, P), columns(("st", 0, h), 0, HALF), True, True)
-            copy_on(engine, rows[:, h * HALF : (h + 1) * HALF], bank[:])
+
+        def read_empty(c, s, h, engine="scalar"):
+            last = ("o", c, s) in held
+            if not last:
+                take_stage(("o", c, s))
+            rows = held["o", c, s][:].bitcast(F32)
+            copy_on(engine, rows[:, h * HALF : (h + 1) * HALF], held["read", c, s, h][:])
             give_bank(("read", c, s, h))
-            if h == 1:
+            if last:
                 nc.sync.dma_start(out=out_view[c, :, s, :], in_=rows)
                 give_stage(("o", c, s))
+
+        def read_state(c, s, h, engine="scalar"):
+            read_sums(c, s, h)
+            read_empty(c, s, h, engine)
 
         def read_slot(c, s, second="scalar"):
             read_state(c, s, 0)
@@ -331,21 +347,23 @@ def tile_linear_state_step_s7_kernel(
             update_rows(h, i, first, width)
 
         with tc.manual_schedule():
-            load_chunk("q", 0)
+            load_x("q", 0, 0)
+            load_x("q", 1, 0)
+            load_x("q", 0, 1)
             load_scales()
-            load_chunk("q", 1)
+            load_x("q", 1, 1)
             load_w("wk", 0)
             load_chunk("k", 0)
             load_w("wk", 1)
             load_x("k", 1, 0)
             load_w("wv", 0, 0)
             load_x("k", 1, 1)
-            load_w("wv", 1, 0)
             load_chunk("k", 2)
+            load_w("wv", 1, 0)
             load_chunk("v", 0)
+            load_chunk("v", 1)
             load_w("wq", 0)
             load_w("wq", 1)
-            load_chunk("v", 1)
             load_chunk("v", 2)
             load_w("st", 0, 0)
             load_w("st", 0, 1)
@@ -357,51 +375,46 @@ def tile_linear_state_step_s7_kernel(
             widen_plain(1, 0, "scalar")
             widen_plain(1, 1, "scalar")
             load_chunk("q", 2)
-            w_interleave("wk", 0, 0, "gpsimd", 0, 384)
+            w_interleave("wk", 0, 0, "gpsimd")
             turn_chunk("q", 0)
             scale_pair(0, 0)
             turn("q", 1, 0)
-            turn("k", 0, 0)
             empty_turned("q", 0, 2)
+            turn("k", 0, 0)
+            empty_turned("q", 0, 3)
             turn("k", 0, 1)
             turn("q", 1, 1)
-            w_interleave("wk", 0, 0, "vector", 384, 128)
-            x_quantize("q", 0, 0)
             w_interleave("wk", 1, 0, "vector", 0, 256)
-            w_quantize("wk", 0, 0)
+            w_quantize("wk", 0, 0, 0, 256)
             x_quantize("k", 0, 0)
             w_quantize("wk", 1, 0, 0, 256)
             x_quantize("k", 0, 1)
             w_interleave("wk", 1, 0, "scalar", 256, 256)
-            w_quantize("wk", 1, 0, 256, 256)
-            w_interleave("wv", 0, 0, "gpsimd")
             turn("k", 1, 0)
-            project("k", 0, 0, 0)
-            empty_turned("q", 0, 3)
-            project_banks("k", 0, 0, 1, 2)
-            empty_turned("q", 1, 0)
-            project("k", 0, 0, 3)
+            x_quantize("q", 0, 0)
+            w_quantize("wk", 0, 0, 256, 256)
+            w_quantize("wk", 1, 0, 256, 256)
+            w_interleave("wv", 0, 0, "gpsimd", 0, 320)
+            project_banks("k", 0, 0, 0, 2)
+            scale_pair(1, 0)
             turn("k", 1, 1)
-            empty_turned("q", 1, 1)
+            project_banks("k", 0, 0, 2, 2)
             x_quantize("k", 1, 0)
-            x_quantize("q", 0, 1)
             x_quantize("k", 1, 1)
             w_interleave("wv", 1, 0, "gpsimd", 0, 320)
             turn_chunk("k", 2)
-            project("k", 1, 0, 0)
-            empty_turned("q", 1, 2)
-            project_banks("k", 1, 0, 1, 2)
-            empty_turned("q", 1, 3)
-            project("k", 1, 0, 3)
+            scale_pair(1, 1)
+            project_banks("k", 1, 0)
             sort_words("v", 0, 1)
             x_quantize("k", 2, 0)
             x_quantize("k", 2, 1)
             turn_chunk("v", 0)
+            w_interleave("wv", 0, 0, "vector", 320, 192)
             w_interleave("wv", 1, 0, "vector", 320, 192)
-            w_quantize("wv", 0, 0)
             sort_words("v", 1, 0)
-            w_quantize("wv", 1, 0)
+            w_quantize("wv", 0, 0)
             sort_words("v", 1, 1)
+            w_quantize("wv", 1, 0)
             project_banks("k", 2, 0)
             x_quantize("v", 0, 0)
             x_quantize("v", 0, 1)
@@ -416,6 +429,7 @@ def tile_linear_state_step_s7_kernel(
             turn_chunk("v", 2)
             w_quantize("wq", 0, 0)
             w_quantize("wq", 1, 0)
+            x_quantize("q", 0, 1)
             project_banks("v", 1, 0)
             x_quantize("v", 2, 0)
             x_quantize("v", 2, 1)
@@ -441,8 +455,8 @@ def tile_linear_state_step_s7_kernel(
             for s in range(1, PACK):
                 read_slot(0, s)
             widen_sorted(2, 0)
-            q_quantize(1, 0)
             widen_sorted(2, 1)
+            q_quantize(1, 0)
             q_quantize(1, 1)
             late_interleave(0, "gpsimd")
             project_banks("v", 0, 1, 0, 2)
@@ -467,17 +481,19 @@ def tile_linear_state_step_s7_kernel(
             project_banks("q", 2, 0, 0, 2)
             read_slot(1, 2)
             read_state(1, 3, 0)
+            read_sums(1, 3, 1)
             project_banks("q", 2, 0, 2, 2)
-            for c in range(CHUNKS):
-                y_quantize("k", c, 0)
+            y_quantize("k", 0, 0)
+            read_empty(1, 3, 1, "vector")
+            y_quantize("k", 1, 0)
             q_quantize(2, 0)
-            read_state(1, 3, 1, "vector")
+            y_quantize("k", 2, 0)
             y_quantize("v", 0, 0)
             y_quantize("v", 1, 0)
-            project_banks("v", 0, 1, 2, 2)
-            read_slot(2, 0, "vector")
             q_quantize(2, 1)
             y_quantize("v", 2, 0)
+            project_banks("v", 0, 1, 2, 2)
+            read_slot(2, 0, "vector")
             project_banks("v", 1, 1, 2, 2)
             read_slot(2, 1, "vector")
             update(0, 0)

@@ -182,9 +182,10 @@ def tile_linear_state_step_s7_kernel(
                 scalar1=ones[:, 0:1], scalar2=None, op0=ALU.mult,
             )
 
-        def widen_plain(c, h, engine="vector"):
-            t = take_stage(("rows", "q", c, h))
-            copy_on(engine, t[:], held["bytes", c, h][:].bitcast(FP8))
+        def widen_plain(c, h, engine="vector", first=0, width=STAGE):
+            if first == 0:
+                take_stage(("rows", "q", c, h))
+            copy_on(engine, held["rows", "q", c, h][:, first : first + width], held["bytes", c, h][:, first : first + width].bitcast(FP8))
 
         def sort_words(kind, c, h):
             t = take_stage(("sorted", kind, c, h))
@@ -373,43 +374,45 @@ def tile_linear_state_step_s7_kernel(
             widen_plain(0, 0)
             widen_plain(0, 1)
             widen_plain(1, 0, "scalar")
-            widen_plain(1, 1, "scalar")
+            widen_plain(1, 1)
             load_chunk("q", 2)
-            w_interleave("wk", 0, 0, "gpsimd")
+            w_interleave("wk", 0, 0, "scalar", 256, 256)
+            w_interleave("wk", 0, 0, "gpsimd", 0, 256)
             turn_chunk("q", 0)
-            scale_pair(0, 0)
-            turn("q", 1, 0)
-            empty_turned("q", 0, 2)
-            turn("k", 0, 0)
-            empty_turned("q", 0, 3)
-            turn("k", 0, 1)
             turn("q", 1, 1)
+            scale_pair(0, 0)
+            turn("k", 0, 0)
+            turn("k", 0, 1)
+            empty_turned("q", 0, 2)
+            turn("q", 1, 0)
+            w_interleave("wk", 1, 0, "scalar", 256, 256)
             w_interleave("wk", 1, 0, "vector", 0, 256)
             w_quantize("wk", 0, 0, 0, 256)
             x_quantize("k", 0, 0)
             w_quantize("wk", 1, 0, 0, 256)
             x_quantize("k", 0, 1)
-            w_interleave("wk", 1, 0, "scalar", 256, 256)
             turn("k", 1, 0)
-            x_quantize("q", 0, 0)
             w_quantize("wk", 0, 0, 256, 256)
             w_quantize("wk", 1, 0, 256, 256)
-            w_interleave("wv", 0, 0, "gpsimd", 0, 320)
-            project_banks("k", 0, 0, 0, 2)
-            scale_pair(1, 0)
+            w_interleave("wv", 0, 0, "gpsimd")
+            project("k", 0, 0, 0)
+            empty_turned("q", 0, 3)
+            project("k", 0, 0, 1)
+            empty_turned("q", 1, 2)
             turn("k", 1, 1)
+            empty_turned("q", 1, 3)
             project_banks("k", 0, 0, 2, 2)
             x_quantize("k", 1, 0)
+            x_quantize("q", 0, 0)
             x_quantize("k", 1, 1)
             w_interleave("wv", 1, 0, "gpsimd", 0, 320)
             turn_chunk("k", 2)
-            scale_pair(1, 1)
+            scale_pair(1, 0)
             project_banks("k", 1, 0)
             sort_words("v", 0, 1)
             x_quantize("k", 2, 0)
             x_quantize("k", 2, 1)
             turn_chunk("v", 0)
-            w_interleave("wv", 0, 0, "vector", 320, 192)
             w_interleave("wv", 1, 0, "vector", 320, 192)
             sort_words("v", 1, 0)
             w_quantize("wv", 0, 0)

@@ -21,10 +21,10 @@ CHUNK = P * PACK
 CHUNKS = T // CHUNK
 PASSES = D // 512
 HALF = 512
-STAGE = 2048
 EARLY = 256
+STAGE = 2048
 STAGES = 37
-XBUFS = 11
+X_OPERANDS = 11
 
 
 def tile_linear_state_step_s7_kernel(
@@ -98,6 +98,12 @@ def tile_linear_state_step_s7_kernel(
             else:
                 t = take_stage(("rows", kind, c, h))
             nc.sync.dma_start(out=t[:].rearrange("p (s d) -> p s d", s=2), in_=view[:, 2 * h : 2 * h + 2, :])
+
+        def load_first_slots():
+            view = xq_bytes[:CHUNK, :].rearrange("(m s) d -> m s d", s=PACK)
+            t = held["bytes", 0, 0] = sb.tile([P, 2 * D], U8, name="xq_bytes00", tag="xq_bytes", bufs=4, align_bytes=64)
+            for s in range(2):
+                nc.sync.dma_start(out=t[:, s * D : (s + 1) * D], in_=view[:, s, :])
 
         def load_chunk(kind, c):
             load_x(kind, c, 0)
@@ -182,10 +188,11 @@ def tile_linear_state_step_s7_kernel(
                 scalar1=ones[:, 0:1], scalar2=None, op0=ALU.mult,
             )
 
-        def widen_plain(c, h, engine="vector", first=0, width=STAGE):
-            if first == 0:
-                take_stage(("rows", "q", c, h))
-            copy_on(engine, held["rows", "q", c, h][:, first : first + width], held["bytes", c, h][:, first : first + width].bitcast(FP8))
+        def widen_plain(c, h, engine="vector"):
+            t = take_stage(("rows", "q", c, h))
+            width = D if engine == "vector" else STAGE
+            for first in range(0, STAGE, width):
+                copy_on(engine, t[:, first : first + width], held["bytes", c, h][:, first : first + width].bitcast(FP8))
 
         def sort_words(kind, c, h):
             t = take_stage(("sorted", kind, c, h))
@@ -195,7 +202,7 @@ def tile_linear_state_step_s7_kernel(
             )
             give_stage(("rows", kind, c, h))
 
-        def turn(kind, c, h, engine="scalar"):
+        def turn(kind, c, h):
             source = ("sorted", kind, c, h) if ("sorted", kind, c, h) in held else ("rows", kind, c, h)
             words = held[source][:].bitcast(F32)
             for i in range(2):
@@ -210,15 +217,15 @@ def tile_linear_state_step_s7_kernel(
                             chosen = words[:, first + u : first + 2 * P : 2]
                         at = (u * PASSES + g) * P
                         nc.tensor.transpose(bank[:, at : at + P], chosen, ident[:])
-                if kind != "q" and engine == "scalar":
+                if kind != "q":
                     empty_turned(kind, c, 2 * h + i)
             give_stage(source)
 
-        def turn_chunk(kind, c, engine="scalar"):
-            turn(kind, c, 0, engine)
-            turn(kind, c, 1, engine)
+        def turn_chunk(kind, c):
+            turn(kind, c, 0)
+            turn(kind, c, 1)
 
-        def empty_turned(kind, c, s, engine="scalar"):
+        def empty_turned(kind, c, s):
             h, i = s // 2, s % 2
             if i == 0:
                 take_stage(("grouped", kind, c, h))
@@ -232,10 +239,9 @@ def tile_linear_state_step_s7_kernel(
                     op=ALU.mult,
                 )
             else:
-                copy_on(
-                    engine,
-                    part.bitcast(F32).rearrange("p (g m u) -> p g m u", g=PASSES, u=2),
-                    bank[:].rearrange("p (u g m) -> p g m u", g=PASSES, u=2),
+                nc.scalar.copy(
+                    out=part.bitcast(F32).rearrange("p (g m u) -> p g m u", g=PASSES, u=2),
+                    in_=bank[:].rearrange("p (u g m) -> p g m u", g=PASSES, u=2),
                 )
             give_bank(("turned", kind, c, s))
 
@@ -244,14 +250,14 @@ def tile_linear_state_step_s7_kernel(
             empty_turned("q", c, 2 * h + 1)
 
         def x_quantize(kind, c, h):
-            new_operand(("x", kind, c, h), HALF, "x", XBUFS)
+            new_operand(("x", kind, c, h), HALF, "x", X_OPERANDS)
             quantize(("x", kind, c, h), held["grouped", kind, c, h], 0, HALF)
             give_stage(("grouped", kind, c, h))
 
         def x_operand(kind, c, s, g):
             return columns(("x", kind, c, s // 2), ((s % 2) * PASSES + g) * P, P)
 
-        def project_sums(kind, c, h, q):
+        def project(kind, c, h, q):
             bank = take_bank(("proj", kind, c, h, q))
             for s in range(PACK):
                 for g in range(PASSES):
@@ -260,16 +266,9 @@ def tile_linear_state_step_s7_kernel(
                     else:
                         pair = x_operand(kind, c, s, g), columns(("w" + kind, g, h), q * P, P)
                     multiply(bank[:, s * P : (s + 1) * P], pair[0], pair[1], g == 0, g == PASSES - 1)
-
-        def project(kind, c, h, q):
-            project_sums(kind, c, h, q)
-            project_empty(kind, c, h, q)
-
-        def project_empty(kind, c, h, q, engine="scalar"):
             if q == 0:
                 take_stage(("y", kind, c, h))
             grouped = held["y", kind, c, h][:]
-            bank = held["proj", kind, c, h, q]
             if kind == "k":
                 nc.scalar.activation(
                     out=grouped.rearrange("p (i m s) -> p i m s", i=PACK, s=PACK)[:, :, 32 * q : 32 * q + 32, :],
@@ -277,10 +276,9 @@ def tile_linear_state_step_s7_kernel(
                     func=ACT.Relu,
                 )
             else:
-                copy_on(
-                    engine,
-                    grouped[:, q * HALF : (q + 1) * HALF].rearrange("p (n s) -> p n s", s=PACK),
-                    bank[:].rearrange("p (s n) -> p n s", s=PACK),
+                nc.scalar.copy(
+                    out=grouped[:, q * HALF : (q + 1) * HALF].rearrange("p (n s) -> p n s", s=PACK),
+                    in_=bank[:].rearrange("p (s n) -> p n s", s=PACK),
                 )
             give_bank(("proj", kind, c, h, q))
 
@@ -348,13 +346,14 @@ def tile_linear_state_step_s7_kernel(
             update_rows(h, i, first, width)
 
         with tc.manual_schedule():
-            load_x("q", 0, 0)
-            load_x("q", 1, 0)
+            load_first_slots()
             load_x("q", 0, 1)
+            load_x("q", 1, 0)
             load_scales()
             load_x("q", 1, 1)
+            load_x("k", 0, 0)
             load_w("wk", 0)
-            load_chunk("k", 0)
+            load_x("k", 0, 1)
             load_w("wk", 1)
             load_x("k", 1, 0)
             load_w("wv", 0, 0)
@@ -371,6 +370,7 @@ def tile_linear_state_step_s7_kernel(
             load_w("wv", 0, 1)
             load_w("wv", 1, 1)
             load_decay()
+
             widen_plain(0, 0)
             widen_plain(0, 1)
             widen_plain(1, 0, "scalar")
@@ -394,6 +394,7 @@ def tile_linear_state_step_s7_kernel(
             turn("k", 1, 0)
             w_quantize("wk", 0, 0, 256, 256)
             w_quantize("wk", 1, 0, 256, 256)
+
             w_interleave("wv", 0, 0, "gpsimd")
             project("k", 0, 0, 0)
             empty_turned("q", 0, 3)
@@ -418,6 +419,7 @@ def tile_linear_state_step_s7_kernel(
             w_quantize("wv", 0, 0)
             sort_words("v", 1, 1)
             w_quantize("wv", 1, 0)
+
             project_banks("k", 2, 0)
             x_quantize("v", 0, 0)
             x_quantize("v", 0, 1)
@@ -446,6 +448,7 @@ def tile_linear_state_step_s7_kernel(
             w_quantize("st", 0, 1)
             q_quantize(0, 1)
             project_banks("v", 2, 0)
+
             late_interleave(0, "vector")
             late_interleave(1, "vector")
             late_quantize(0, "vector")
@@ -461,10 +464,10 @@ def tile_linear_state_step_s7_kernel(
             widen_sorted(2, 1)
             q_quantize(1, 0)
             q_quantize(1, 1)
+
             late_interleave(0, "gpsimd")
             project_banks("v", 0, 1, 0, 2)
             turn_chunk("q", 2)
-
             empty_turned("q", 2, 0)
             project("v", 1, 1, 0)
             empty_turned("q", 2, 1)
@@ -480,7 +483,6 @@ def tile_linear_state_step_s7_kernel(
             late_quantize(0, "gpsimd")
             x_quantize("q", 2, 1)
             late_quantize(1, "gpsimd")
-
             project_banks("q", 2, 0, 0, 2)
             read_slot(1, 2)
             read_state(1, 3, 0)
@@ -495,6 +497,7 @@ def tile_linear_state_step_s7_kernel(
             y_quantize("v", 1, 0)
             q_quantize(2, 1)
             y_quantize("v", 2, 0)
+
             project_banks("v", 0, 1, 2, 2)
             read_slot(2, 0, "vector")
             project_banks("v", 1, 1, 2, 2)

from contextlib import ExitStack

import concourse.mybir as mybir
from concourse.masks import make_identity

T, D, F, E = 1536, 1024, 512, 1024
FLOPS = 2 * T * (2 * D * F + D * E + 2 * F * E)

F32 = mybir.dt.float32
BF16 = mybir.dt.bfloat16
U32 = mybir.dt.uint32
U8 = mybir.dt.uint8
FP8 = mybir.dt.float8_e4m3fn
FP8X4 = mybir.dt.float8_e4m3fn_x4
ACT = mybir.ActivationFunctionType
ALU = mybir.AluOpType

P = 128
PACK = 4
CHUNK = P * PACK
CHUNKS = T // CHUNK
PASSES = D // 512
HALF = 512
EARLY = 256
STAGE = 2048
STAGES = 37
X_OPERANDS = 11


def tile_linear_state_step_s7_kernel(
    tc, xq_bytes, xq_scale, xk, xv, wq, wk, wv, state, decay, out_0, out_1
):
    nc = tc.nc

    with ExitStack() as ctx:
        sb = ctx.enter_context(tc.tile_pool(name="sb", bufs=1))
        ps = ctx.enter_context(tc.psum_pool(name="ps", bufs=1))

        ident = sb.tile([P, P], F32, name="ident", align_bytes=64)
        make_identity(nc, ident[:])
        decay_sb = sb.tile([P, PACK], BF16, name="decay_sb")
        scale_pt = sb.tile([P, PASSES, PACK], F32, name="scale_pt", align_bytes=64)
        ones = sb.tile([P, 1], F32, name="ones")
        nc.vector.memset(ones[:], 1.0)

        free_banks, free_stages = list(range(8)), list(range(STAGES))
        held, place, operands = {}, {}, {}

        def take_bank(key):
            place[key] = free_banks.pop(0)
            held[key] = ps.tile([P, 512], F32, name="".join(map(str, key)), tag=f"bank{place[key]}")
            return held[key]

        def give_bank(key):
            free_banks.append(place[key])

        def take_stage(key, newest=False):
            place[key] = free_stages.pop(-1 if newest else 0)
            held[key] = sb.tile([P, STAGE], BF16, name="".join(map(str, key)), tag=f"stage{place[key]}", align_bytes=64)
            return held[key]

        def give_stage(key):
            free_stages.append(place[key])

        def new_operand(key, words, tag, bufs):
            name = "".join(map(str, key))
            codes = sb.tile([P, words], U32, name=f"{name}_codes", tag=f"{tag}_codes", bufs=bufs, align_bytes=64)
            scales = sb.tile([P, words], U8, name=f"{name}_scales", tag=f"{tag}_scales", bufs=bufs, align_bytes=64)
            operands[key] = codes, scales

        def columns(key, first, width):
            codes, scales = operands[key]
            return codes[:, first : first + width].bitcast(FP8X4), scales[:, first : first + width]

        def quantize(key, grouped, first, width):
            codes, scales = columns(key, first, width)
            nc.vector.quantize_mx(out=codes, scales=scales, in_=grouped[:, first * PACK : (first + width) * PACK])

        def multiply(out, stationary, moving, start, stop):
            nc.tensor.matmul_mx(
                out=out, lhsT=stationary[0], lhsT_scale=stationary[1], rhs=moving[0], rhs_scale=moving[1],
                start=start, stop=stop,
            )

        def copy_on(engine, out, in_):
            if engine == "vector":
                nc.vector.tensor_copy(out=out, in_=in_)
            else:
                nc.scalar.copy(out=out, in_=in_)

        x_dram = {"k": xk, "v": xv, "q": xq_bytes}
        w_dram = {"wk": wk, "wq": wq, "wv": wv, "st": state}

        def load_x(kind, c, h):
            view = x_dram[kind][c * CHUNK : (c + 1) * CHUNK, :].rearrange("(m s) d -> m s d", s=PACK)
            if kind == "q":
                t = held["bytes", c, h] = sb.tile([P, 2 * D], U8, name=f"xq_bytes{c}{h}", tag="xq_bytes", bufs=4, align_bytes=64)
            else:
                t = take_stage(("rows", kind, c, h))
            nc.sync.dma_start(out=t[:].rearrange("p (s d) -> p s d", s=2), in_=view[:, 2 * h : 2 * h + 2, :])

        def load_first_slots():
            view = xq_bytes[:CHUNK, :].rearrange("(m s) d -> m s d", s=PACK)
            t = held["bytes", 0, 0] = sb.tile([P, 2 * D], U8, name="xq_bytes00", tag="xq_bytes", bufs=4, align_bytes=64)
            for s in range(2):
                nc.sync.dma_start(out=t[:, s * D : (s + 1) * D], in_=view[:, s, :])

        def load_chunk(kind, c):
            load_x(kind, c, 0)
            load_x(kind, c, 1)

        def load_w(name, g, h=0):
            t = take_stage(("raw", name, g, h))
            rows = w_dram[name][512 * g : 512 * (g + 1), h * HALF : (h + 1) * HALF]
            nc.sync.dma_start(out=t[:].rearrange("p (j n) -> p j n", j=PACK), in_=rows.rearrange("(p j) n -> p j n", j=PACK))

        def load_scales():
            nc.sync.dma_start(out=scale_pt[:], in_=xq_scale.rearrange("o (g p t) -> p (o g) t", p=P, t=PACK))

        def load_decay():
            nc.sync.dma_start(out=decay_sb[:], in_=decay.rearrange("(p i) -> p i", i=PACK))

        def w_interleave(name, g, h, engine="vector", first=0, width=HALF):
            key = ("grouped", name, g, h)
            if key not in held:
                take_stage(key, newest=engine == "gpsimd")
            raw = held["raw", name, g, h][:].rearrange("p (j n) -> p j n", j=PACK)[:, :, first : first + width]
            if name == "wq":
                planes = held[key][:].rearrange("p (t m j) -> p t m j", t=PACK, j=PACK)[:, :, first // PACK : (first + width) // PACK, :]
                copy_on(
                    engine,
                    planes.rearrange("p t (c i) j -> p c t i j", i=2),
                    raw.rearrange("p j (c i t) -> p c t i j", i=2, t=PACK),
                )
            elif engine == "gpsimd":
                nc.gpsimd.tensor_scalar(
                    out=held[key][:, first * PACK : (first + width) * PACK].rearrange("p (c j) -> p c j", j=PACK),
                    in0=raw.rearrange("p j c -> p c j"), scalar1=1.0, scalar2=0.0, op0=ALU.mult, op1=ALU.add,
                )
            else:
                copy_on(
                    engine,
                    held[key][:, first * PACK : (first + width) * PACK].rearrange("p (c i j) -> p c j i", i=4, j=PACK),
                    raw.rearrange("p j (c i) -> p c j i", i=4),
                )
            if first + width == HALF and name != "st":
                give_stage(("raw", name, g, h))

        def w_quantize(name, g, h, first=0, width=HALF):
            if first == 0:
                new_operand((name, g, h), HALF, f"{name}{g}{h}", 1)
            quantize((name, g, h), held["grouped", name, g, h], first, width)
            if first + width == HALF:
                give_stage(("grouped", name, g, h))

        def late_interleave(g, engine):
            first, width = (0, EARLY) if engine == "vector" else (EARLY, HALF - EARLY)
            key = ("late", engine, g if engine == "gpsimd" else 0)
            if key not in held:
                take_stage(key, newest=engine == "gpsimd")
            raw = held["raw", "wv", g, 1][:].rearrange("p (j n) -> p j n", j=PACK)[:, :, first : first + width]
            if engine == "gpsimd":
                nc.gpsimd.tensor_scalar(
                    out=held[key][:, : width * PACK].rearrange("p (c j) -> p c j", j=PACK), in0=raw.rearrange("p j c -> p c j"),
                    scalar1=1.0, scalar2=0.0, op0=ALU.mult, op1=ALU.add,
                )
                give_stage(("raw", "wv", g, 1))
            else:
                out = held[key][:, g * width * PACK : (g + 1) * width * PACK]
                copy_on(engine, out.rearrange("p (c i j) -> p c j i", i=4, j=PACK), raw.rearrange("p j (c i) -> p c j i", i=4))

        def late_quantize(g, engine):
            first, width = (0, EARLY) if engine == "vector" else (EARLY, HALF - EARLY)
            key = ("late", engine, g if engine == "gpsimd" else 0)
            if engine == "vector":
                new_operand(("wv", g, 1), HALF, f"wv{g}1", 1)
            at = g * width * PACK if engine == "vector" else 0
            codes, scales = columns(("wv", g, 1), first, width)
            nc.vector.quantize_mx(out=codes, scales=scales, in_=held[key][:, at : at + width * PACK])
            if g == 1 or engine == "gpsimd":
                give_stage(key)

        def widen_sorted(c, h):
            t = take_stage(("sorted", "q", c, h))
            nc.vector.tensor_scalar(
                out=t[:].rearrange("p (u m e) -> p m u e", u=2, e=2),
                in0=held["bytes", c, h][:].bitcast(FP8).rearrange("p (m u e) -> p m u e", u=2, e=2),
                scalar1=ones[:, 0:1], scalar2=None, op0=ALU.mult,
            )

        def widen_plain(c, h, engine="vector"):
            t = take_stage(("rows", "q", c, h))
            width = D if engine == "vector" else STAGE
            for first in range(0, STAGE, width):
                copy_on(engine, t[:, first : first + width], held["bytes", c, h][:, first : first + width].bitcast(FP8))

        def sort_words(kind, c, h):
            t = take_stage(("sorted", kind, c, h))
            nc.vector.tensor_copy(
                out=t[:].bitcast(F32).rearrange("p (u m) -> p m u", u=2),
                in_=held["rows", kind, c, h][:].bitcast(F32).rearrange("p (m u) -> p m u", u=2),
            )
            give_stage(("rows", kind, c, h))

        def turn(kind, c, h):
            source = ("sorted", kind, c, h) if ("sorted", kind, c, h) in held else ("rows", kind, c, h)
            words = held[source][:].bitcast(F32)
            for i in range(2):
                bank = take_bank(("turned", kind, c, 2 * h + i))
                for g in range(PASSES):
                    for u in range(2):
                        if source[0] == "sorted":
                            first = u * HALF + (i * PASSES + g) * P
                            chosen = words[:, first : first + P]
                        else:
                            first = i * HALF + 2 * P * g
                            chosen = words[:, first + u : first + 2 * P : 2]
                        at = (u * PASSES + g) * P
                        nc.tensor.transpose(bank[:, at : at + P], chosen, ident[:])
                if kind != "q":
                    empty_turned(kind, c, 2 * h + i)
            give_stage(source)

        def turn_chunk(kind, c):
            turn(kind, c, 0)
            turn(kind, c, 1)

        def empty_turned(kind, c, s):
            h, i = s // 2, s % 2
            if i == 0:
                take_stage(("grouped", kind, c, h))
            part = held["grouped", kind, c, h][:, i * D : (i + 1) * D]
            bank = held["turned", kind, c, s]
            if kind == "q":
                nc.vector.tensor_tensor(
                    out=part.rearrange("p (g m u e) -> p g m u e", g=PASSES, u=2, e=2),
                    in0=bank[:].bitcast(BF16).rearrange("p (u g m e) -> p g m u e", g=PASSES, u=2, e=2),
                    in1=scale_pt[:].rearrange("p g (u e) -> p g u e", u=2).unsqueeze(2).to_broadcast([P, PASSES, P, 2, 2]),
                    op=ALU.mult,
                )
            else:
                nc.scalar.copy(
                    out=part.bitcast(F32).rearrange("p (g m u) -> p g m u", g=PASSES, u=2),
                    in_=bank[:].rearrange("p (u g m) -> p g m u", g=PASSES, u=2),
                )
            give_bank(("turned", kind, c, s))

        def scale_pair(c, h):
            empty_turned("q", c, 2 * h)
            empty_turned("q", c, 2 * h + 1)

        def x_quantize(kind, c, h):
            new_operand(("x", kind, c, h), HALF, "x", X_OPERANDS)
            quantize(("x", kind, c, h), held["grouped", kind, c, h], 0, HALF)
            give_stage(("grouped", kind, c, h))

        def x_operand(kind, c, s, g):
            return columns(("x", kind, c, s // 2), ((s % 2) * PASSES + g) * P, P)

        def project(kind, c, h, q):
            bank = take_bank(("proj", kind, c, h, q))
            for s in range(PACK):
                for g in range(PASSES):
                    if kind == "q":
                        pair = columns(("wq", g, 0), s * P, P), x_operand("q", c, q, g)
                    else:
                        pair = x_operand(kind, c, s, g), columns(("w" + kind, g, h), q * P, P)
                    multiply(bank[:, s * P : (s + 1) * P], pair[0], pair[1], g == 0, g == PASSES - 1)
            if q == 0:
                take_stage(("y", kind, c, h))
            grouped = held["y", kind, c, h][:]
            if kind == "k":
                nc.scalar.activation(
                    out=grouped.rearrange("p (i m s) -> p i m s", i=PACK, s=PACK)[:, :, 32 * q : 32 * q + 32, :],
                    in_=bank[:].rearrange("p (s m i) -> p i m s", s=PACK, i=PACK),
                    func=ACT.Relu,
                )
            else:
                nc.scalar.copy(
                    out=grouped[:, q * HALF : (q + 1) * HALF].rearrange("p (n s) -> p n s", s=PACK),
                    in_=bank[:].rearrange("p (s n) -> p n s", s=PACK),
                )
            give_bank(("proj", kind, c, h, q))

        def project_banks(kind, c, h, first=0, count=4):
            for q in range(first, first + count):
                project(kind, c, h, q)

        def y_quantize(kind, c, h):
            new_operand(("y", kind, c, h), HALF, kind, 3 if kind == "k" else 6)
            quantize(("y", kind, c, h), held["y", kind, c, h], 0, HALF)
            give_stage(("y", kind, c, h))

        def q_quantize(c, h):
            new_operand(("y", "q", c, h), 2 * P, "q", 4)
            quantize(("y", "q", c, h), held["y", "q", c, 0][:, h * D : (h + 1) * D], 0, 2 * P)
            if h == 1:
                give_stage(("y", "q", c, 0))

        out_view = out_0.rearrange("(c m s) e -> c m s e", m=P, s=PACK)
        new_view = out_1.rearrange("(p i) e -> p i e", i=PACK)

        def read_sums(c, s, h):
            bank = take_bank(("read", c, s, h))
            multiply(bank[:], columns(("y", "q", c, s // 2), (s % 2) * P, P), columns(("st", 0, h), 0, HALF), True, True)

        def read_empty(c, s, h, engine="scalar"):
            last = ("o", c, s) in held
            if not last:
                take_stage(("o", c, s))
            rows = held["o", c, s][:].bitcast(F32)
            copy_on(engine, rows[:, h * HALF : (h + 1) * HALF], held["read", c, s, h][:])
            give_bank(("read", c, s, h))
            if last:
                nc.sync.dma_start(out=out_view[c, :, s, :], in_=rows)
                give_stage(("o", c, s))

        def read_state(c, s, h, engine="scalar"):
            read_sums(c, s, h)
            read_empty(c, s, h, engine)

        def read_slot(c, s, second="scalar"):
            read_state(c, s, 0)
            read_state(c, s, 1, second)

        def update_sums(h, i, first=0, width=HALF):
            bank = take_bank(("update", h, i, first))
            for c in range(CHUNKS):
                multiply(bank[:, :width], columns(("y", "k", c, 0), i * P, P), columns(("y", "v", c, h), first, width),
                         c == 0, c == CHUNKS - 1)

        def update_rows(h, i, first=0, width=HALF):
            key = ("new", h, i, first)
            bank = held["update", h, i, first]
            rows = take_stage(key)[:].bitcast(F32)[:, :width]
            old = held["raw", "st", 0, h][:, i * HALF + first : i * HALF + first + width]
            nc.vector.scalar_tensor_tensor(
                out=rows, in0=old, scalar=decay_sb[:, i : i + 1], in1=bank[:, :width], op0=ALU.mult, op1=ALU.add,
            )
            give_bank(("update", h, i, first))
            nc.sync.dma_start(out=new_view[:, i, h * HALF + first : h * HALF + first + width], in_=rows)
            give_stage(key)

        def update(h, i, first=0, width=HALF):
            update_sums(h, i, first, width)
            update_rows(h, i, first, width)

        with tc.manual_schedule():
            load_first_slots()
            load_x("q", 0, 1)
            load_x("q", 1, 0)
            load_scales()
            load_x("q", 1, 1)
            load_x("k", 0, 0)
            load_w("wk", 0)
            load_x("k", 0, 1)
            load_w("wk", 1)
            load_x("k", 1, 0)
            load_w("wv", 0, 0)
            load_x("k", 1, 1)
            load_chunk("k", 2)
            load_w("wv", 1, 0)
            load_chunk("v", 0)
            load_chunk("v", 1)
            load_w("wq", 0)
            load_w("wq", 1)
            load_chunk("v", 2)
            load_w("st", 0, 0)
            load_w("st", 0, 1)
            load_w("wv", 0, 1)
            load_w("wv", 1, 1)
            load_decay()

            widen_plain(0, 0)
            widen_plain(0, 1)
            widen_plain(1, 0, "scalar")
            widen_plain(1, 1)
            load_chunk("q", 2)
            w_interleave("wk", 0, 0, "scalar", 256, 256)
            w_interleave("wk", 0, 0, "gpsimd", 0, 256)
            turn_chunk("q", 0)
            turn("q", 1, 1)
            scale_pair(0, 0)
            turn("k", 0, 0)
            turn("k", 0, 1)
            empty_turned("q", 0, 2)
            turn("q", 1, 0)
            w_interleave("wk", 1, 0, "scalar", 256, 256)
            w_interleave("wk", 1, 0, "vector", 0, 256)
            w_quantize("wk", 0, 0, 0, 256)
            x_quantize("k", 0, 0)
            w_quantize("wk", 1, 0, 0, 256)
            x_quantize("k", 0, 1)
            turn("k", 1, 0)
            w_quantize("wk", 0, 0, 256, 256)
            w_quantize("wk", 1, 0, 256, 256)

            w_interleave("wv", 0, 0, "gpsimd")
            project("k", 0, 0, 0)
            empty_turned("q", 0, 3)
            project("k", 0, 0, 1)
            empty_turned("q", 1, 2)
            turn("k", 1, 1)
            empty_turned("q", 1, 3)
            project_banks("k", 0, 0, 2, 2)
            x_quantize("k", 1, 0)
            x_quantize("q", 0, 0)
            x_quantize("k", 1, 1)
            w_interleave("wv", 1, 0, "gpsimd", 0, 320)
            turn_chunk("k", 2)
            scale_pair(1, 0)
            project_banks("k", 1, 0)
            sort_words("v", 0, 1)
            x_quantize("k", 2, 0)
            x_quantize("k", 2, 1)
            turn_chunk("v", 0)
            w_interleave("wv", 1, 0, "vector", 320, 192)
            sort_words("v", 1, 0)
            w_quantize("wv", 0, 0)
            sort_words("v", 1, 1)
            w_quantize("wv", 1, 0)

            project_banks("k", 2, 0)
            x_quantize("v", 0, 0)
            x_quantize("v", 0, 1)
            turn_chunk("v", 1)
            w_interleave("wq", 0, 0)
            sort_words("v", 2, 0)
            sort_words("v", 2, 1)
            project_banks("v", 0, 0)
            x_quantize("v", 1, 0)
            x_quantize("v", 1, 1)
            w_interleave("wq", 1, 0)
            turn_chunk("v", 2)
            w_quantize("wq", 0, 0)
            w_quantize("wq", 1, 0)
            x_quantize("q", 0, 1)
            project_banks("v", 1, 0)
            x_quantize("v", 2, 0)
            x_quantize("v", 2, 1)
            w_interleave("st", 0, 0)
            x_quantize("q", 1, 0)
            w_quantize("st", 0, 0)
            project_banks("q", 0, 0)
            w_interleave("st", 0, 1)
            q_quantize(0, 0)
            x_quantize("q", 1, 1)
            w_quantize("st", 0, 1)
            q_quantize(0, 1)
            project_banks("v", 2, 0)

            late_interleave(0, "vector")
            late_interleave(1, "vector")
            late_quantize(0, "vector")
            late_quantize(1, "vector")
            project_banks("q", 1, 0, 0, 2)
            read_state(0, 0, 0)
            project("q", 1, 0, 2)
            read_state(0, 0, 1)
            project("q", 1, 0, 3)
            for s in range(1, PACK):
                read_slot(0, s)
            widen_sorted(2, 0)
            widen_sorted(2, 1)
            q_quantize(1, 0)
            q_quantize(1, 1)

            late_interleave(0, "gpsimd")
            project_banks("v", 0, 1, 0, 2)
            turn_chunk("q", 2)
            empty_turned("q", 2, 0)
            project("v", 1, 1, 0)
            empty_turned("q", 2, 1)
            x_quantize("q", 2, 0)
            late_interleave(1, "gpsimd")
            project("v", 1, 1, 1)
            read_slot(1, 0)
            project("v", 2, 1, 0)
            empty_turned("q", 2, 2)
            read_slot(1, 1)
            empty_turned("q", 2, 3)
            project("v", 2, 1, 1)
            late_quantize(0, "gpsimd")
            x_quantize("q", 2, 1)
            late_quantize(1, "gpsimd")
            project_banks("q", 2, 0, 0, 2)
            read_slot(1, 2)
            read_state(1, 3, 0)
            read_sums(1, 3, 1)
            project_banks("q", 2, 0, 2, 2)
            y_quantize("k", 0, 0)
            read_empty(1, 3, 1, "vector")
            y_quantize("k", 1, 0)
            q_quantize(2, 0)
            y_quantize("k", 2, 0)
            y_quantize("v", 0, 0)
            y_quantize("v", 1, 0)
            q_quantize(2, 1)
            y_quantize("v", 2, 0)

            project_banks("v", 0, 1, 2, 2)
            read_slot(2, 0, "vector")
            project_banks("v", 1, 1, 2, 2)
            read_slot(2, 1, "vector")
            update(0, 0)
            y_quantize("v", 0, 1)
            read_slot(2, 2)
            project_banks("v", 2, 1, 2, 2)
            update_sums(0, 1)
            y_quantize("v", 1, 1)
            update_rows(0, 1)
            read_slot(2, 3)
            update_sums(0, 2)
            y_quantize("v", 2, 1)
            update_rows(0, 2)
            update(0, 3)
            for i in range(3):
                update(1, i)
            update(1, 3, 0, 256)
            update(1, 3, 256, 256)
